import numpy as np
import ml_dtypes


def mxq(x, axis, fmt="e4m3"):
    dtype, down = {"e4m3": (ml_dtypes.float8_e4m3fn, 7), "e5m2": (ml_dtypes.float8_e5m2, 14)}[fmt]
    v = np.moveaxis(np.asarray(x, np.float32).astype(ml_dtypes.bfloat16).astype(np.float64), axis, -1)
    blocks = v.reshape(v.shape[:-1] + (-1, 32))
    amax = np.abs(blocks).max(-1, keepdims=True)
    byte = np.maximum(np.where(amax > 0, np.frexp(amax)[1] - 1 + 127, 0) - down, 1)
    scale = np.exp2(byte - 127.0)
    codes = (blocks / scale).astype(np.float32).astype(dtype).astype(np.float64)
    return np.moveaxis((codes * scale).reshape(v.shape), -1, axis)


WIDE = False


def mx_kscale(k):
    if not WIDE:
        return np.ones(k)
    levels = np.array([10, -10, 5, -5, 0])
    if k % 512:
        return np.exp2(np.random.permutation(np.resize(levels, k // 32))).repeat(32)
    a = np.empty((k // 512, 16))
    for p in range(k // 512):
        a[p, :8] = np.random.permutation(np.resize(levels, 8))
        for g in range(8):
            far = levels[np.abs(levels - a[p, g]) >= 10]
            a[p, g + 8] = far[np.random.randint(len(far))]
    return np.exp2(a.ravel()).repeat(32)


def f64(x):
    return np.asarray(x).astype(np.float64)


def striped(idx):
    return np.tile(idx.reshape(-1, 16).T, (8, 1)).astype(np.uint16)


def unstriped(offs):
    return offs[:16].T.reshape(-1).astype(np.int64)


E2M1 = np.array([0.0, 0.5, 1.0, 1.5, 2.0, 3.0, 4.0, 6.0, -0.0, -0.5, -1.0, -1.5, -2.0, -3.0, -4.0, -6.0])


def pack_weight(w, fmt):
    k, n = w.shape
    w = f64(np.asarray(w, np.float32).astype(ml_dtypes.bfloat16)).reshape(k // 32, 32, n)
    amax = np.abs(w).max(1)
    if fmt == "e4m3":
        byte = np.frexp(amax)[1] - 1 + 127 - 7
    else:
        mant, ex = np.frexp(amax / 6.0)
        byte = np.where(mant > 0.5, ex, ex - 1) + 127
    byte = np.clip(np.where(amax > 0, byte, 1), 1, 254)
    scaled = (w * np.exp2(127.0 - byte)[:, None, :]).reshape(k, n).astype(np.float32)
    by_word = np.ascontiguousarray(scaled.reshape(k // 512, 128, 4, n).transpose(0, 1, 3, 2))
    if fmt == "e4m3":
        words = by_word.astype(ml_dtypes.float8_e4m3fn).view(np.uint8)
    else:
        c = by_word.astype(ml_dtypes.float4_e2m1fn).view(np.uint8) & 0xF
        words = (c[..., 0::2] | (c[..., 1::2] << 4)).reshape(k // 512, 128, 2 * n)
    return np.ascontiguousarray(words), np.ascontiguousarray(byte.astype(np.uint8).reshape(k // 512, 16, n))


def unpack_weight(words, scales, fmt):
    g, _, n = scales.shape
    words = np.ascontiguousarray(words).reshape(g, 128, n, -1)
    if fmt == "e4m3":
        vals = words.view(ml_dtypes.float8_e4m3fn).astype(np.float64)
    else:
        nib = np.empty((g, 128, n, 4), np.uint8)
        nib[..., 0::2] = words & 0xF
        nib[..., 1::2] = words >> 4
        vals = E2M1[nib]
    vals = vals * np.repeat(np.exp2(scales.astype(np.float64) - 127.0), 8, axis=1)[..., None]
    return vals.transpose(0, 1, 3, 2).reshape(g * 512, n)


def gelu(v):
    return 0.5 * v * (1.0 + np.tanh(np.sqrt(2.0 / np.pi) * (v + 0.044715 * v**3)))


K, H, N, T, S, T2 = 512, 2048, 512, 4096, 1024, 2048

def setup_inputs():
    n = np.random.standard_normal
    s = mx_kscale(K)[:, None]
    u = mx_kscale(H)[:, None]
    tab_words, tab_scales = pack_weight(n((K, T)) * s, "e4m3")
    w1 = 1.5 * n((K, H)) / np.sqrt(K) / s
    ga = np.exp(0.3 * n(H)) * u[:, 0]
    w2_words, w2_scales = pack_weight(1.2 * n((H, N)) / np.sqrt(H) / u, "e2m1")
    ws_words, ws_scales = pack_weight(n((K, N)) / np.sqrt(K) / s, "e4m3")
    return {"tab_words": tab_words, "tab_scales": tab_scales,
            "offs": striped(np.random.permutation(T)[:S]),
            "w1": w1.astype(np.float32), "ga": ga.astype(np.float32),
            "w2_words": w2_words, "w2_scales": w2_scales,
            "ws_words": ws_words, "ws_scales": ws_scales,
            "wgo": np.exp(0.3 * n((128, S))).astype(np.float32),
            "offs2": striped(np.random.permutation(T2)[:S])}

def reference(tab_words, tab_scales, offs, w1, ga, w2_words, w2_scales, ws_words, ws_scales, wgo, offs2):
    v = unpack_weight(tab_words, tab_scales, "e4m3")[:, unstriped(offs)]
    w1q = mxq(f64(w1), 0, "e4m3")
    w2 = unpack_weight(w2_words, w2_scales, "e2m1")
    ws = unpack_weight(ws_words, ws_scales, "e4m3")
    x = w1q.T @ v
    h = f64(ga)[:, None] * x / (1.0 + np.exp(-1.702 * x))
    hq = mxq(h, 0, "e4m3")
    y = w2.T @ hq + ws.T @ v
    out = np.zeros((N, T2))
    out[:, unstriped(offs2)] = np.tile(f64(wgo), (N // 128, 1)) * y
    return out

@@ -1,0 +1,245 @@
+from contextlib import ExitStack
+
+import concourse.mybir as mybir
+
+K, H, N, T, S, T2 = 512, 2048, 512, 4096, 1024, 2048
+FLOPS = 2 * S * (K * H + H * N + K * N)
+
+F32 = mybir.dt.float32
+BF16 = mybir.dt.bfloat16
+I32 = mybir.dt.int32
+U32 = mybir.dt.uint32
+U16 = mybir.dt.uint16
+U8 = mybir.dt.uint8
+FP8X4 = mybir.dt.float8_e4m3fn_x4
+FP4X4 = mybir.dt.float4_e2m1fn_x4
+ACT = mybir.ActivationFunctionType
+MULT = mybir.AluOpType.mult
+
+P = 128
+PACK = 4
+BLOCKS = H // (P * PACK)
+TILES = N // P
+GROUP = 128
+HALF = 512
+CHUNKS = [(0, 512), (512, 256), (768, 256)]
+SCALAR_BLOCKS = [0, 3, 2]
+CAST_ON_VECTOR = [0, 64, 64, 64]
+
+
+def tile_list_masked_patch_block_kernel(
+    tc, tab_words, tab_scales, offs, w1, ga, w2_words, w2_scales, ws_words, ws_scales, wgo, offs2, out
+):
+    nc = tc.nc
+    with ExitStack() as ctx:
+        keep = ctx.enter_context(tc.tile_pool(name="keep", bufs=1))
+        ring = ctx.enter_context(tc.tile_pool(name="ring", bufs=3))
+        psum = ctx.enter_context(tc.psum_pool(name="psum", bufs=4))
+
+        picks = keep.tile([P, S // 16], U16, name="picks")
+        slots = keep.tile([P, S // 16], U16, name="slots")
+        table = keep.tile([P, T], I32, name="table", align_bytes=64)
+        table_scales = keep.tile([P, T // 4], I32, name="table_scales", align_bytes=64)
+        raw = [keep.tile([P, PACK, P * PACK], F32, name=f"raw{a}", align_bytes=64) for a in range(BLOCKS)]
+        gain = keep.tile([P, BLOCKS, 8], F32, name="gain")
+        w2_codes = keep.tile([P, BLOCKS, 2 * N], U8, name="w2_codes", align_bytes=64)
+        ws_codes = keep.tile([P, N], I32, name="ws_codes", align_bytes=64)
+        out_scales = keep.tile([P, BLOCKS + 1, N // 4], I32, name="out_scales", align_bytes=64)
+        weight = keep.tile([P, S], F32, name="weight", align_bytes=64)
+        windows = [keep.tile([P, T2], F32, name=f"window{n}", align_bytes=64) for n in range(TILES)]
+        v_codes = [keep.tile([P, HALF], U32, name=f"v_codes{i}", align_bytes=64) for i in range(2)]
+        v_scales = [keep.tile([P, HALF], U8, name=f"v_scales{i}", align_bytes=64) for i in range(2)]
+        w1_codes = [keep.tile([P, P * PACK], U32, name=f"w1_codes{a}", align_bytes=64) for a in range(BLOCKS)]
+        w1_scales = [keep.tile([P, P * PACK], U8, name=f"w1_scales{a}", align_bytes=64) for a in range(BLOCKS)]
+
+        nc.vector.memset(table_scales[:], 0)
+        nc.vector.memset(out_scales[:], 0)
+
+        def load_w1(a):
+            cols = slice(a * P * PACK, (a + 1) * P * PACK)
+            nc.sync.dma_start(out=raw[a][:], in_=w1[:, cols].rearrange("(p j) c -> p j c", j=PACK))
+
+        nc.sync.dma_start(picks[:], offs)
+        for q in range(4):
+            nc.sync.dma_start(
+                out=table_scales[32 * q : 32 * q + 4, :], in_=tab_scales[0, 4 * q : 4 * q + 4, :].bitcast(I32)
+            )
+        load_w1(0)
+        nc.sync.dma_start(out=table[:], in_=tab_words[0].rearrange("p t i -> p (t i)").bitcast(I32))
+        nc.sync.dma_start(out=gain[:, :, 0:PACK], in_=ga.rearrange("(a p t) -> p a t", p=P, t=PACK))
+        for a in range(1, BLOCKS):
+            load_w1(a)
+        for q in range(4):
+            rows = slice(32 * q, 32 * q + 4)
+            nc.sync.dma_start(
+                out=out_scales[rows, 0:BLOCKS, :],
+                in_=w2_scales[:, 4 * q : 4 * q + 4, :].rearrange("a q c -> q a c").bitcast(I32),
+            )
+            nc.sync.dma_start(out=out_scales[rows, BLOCKS, :], in_=ws_scales[0, 4 * q : 4 * q + 4, :].bitcast(I32))
+        nc.sync.dma_start(out=ws_codes[:], in_=ws_words[0].rearrange("p c i -> p (c i)").bitcast(I32))
+        nc.sync.dma_start(out=w2_codes[:].bitcast(I32), in_=w2_words.rearrange("a p c -> p a c").bitcast(I32))
+        nc.sync.dma_start(slots[:], offs2)
+        nc.sync.dma_start(out=weight[:], in_=wgo)
+
+        def gather_scales(i):
+            cols = slice(i * HALF // 16, (i + 1) * HALF // 16)
+            nc.vector.tensor_copy(v_scales[i][:], table_scales[:].bitcast(U8).indirect(picks[:, cols]))
+
+        def gather_codes(i):
+            cols = slice(i * HALF // 16, (i + 1) * HALF // 16)
+            nc.vector.tensor_copy(v_codes[i][:], table[:].bitcast(U32).indirect(picks[:, cols]))
+
+        def patch(first, count):
+            i, lo = divmod(first, HALF)
+            return v_codes[i][:, lo : lo + count].bitcast(FP8X4), v_scales[i][:, lo : lo + count]
+
+        def quantize_w1(a):
+            rounded = ring.tile([P, P * PACK * PACK], BF16, name="w1_rounded", align_bytes=64)
+            dst = rounded[:].rearrange("p (t m j) -> p m t j", t=PACK, j=PACK)
+            src = raw[a][:].rearrange("p j (m t) -> p m t j", t=PACK)
+            split = CAST_ON_VECTOR[a]
+            if split > 0:
+                nc.vector.tensor_copy(out=dst[:, 0:split], in_=src[:, 0:split])
+            nc.scalar.copy(out=dst[:, split:P], in_=src[:, split:P])
+            nc.vector.quantize_mx(out=w1_codes[a][:].bitcast(FP8X4), scales=w1_scales[a][:], in_=rounded[:])
+
+        def first_product(a, t, first, count, dst):
+            codes, scales = patch(first, count)
+            cols = slice(t * P, (t + 1) * P)
+            nc.tensor.matmul_mx(
+                out=dst,
+                lhsT=w1_codes[a][:, cols].bitcast(FP8X4),
+                lhsT_scale=w1_scales[a][:, cols],
+                rhs=codes,
+                rhs_scale=scales,
+                start=True,
+                stop=True,
+            )
+
+        def hidden_group(a, first, rounded):
+            x = psum.tile([P, PACK * GROUP], F32, name="x")
+            for t in range(PACK):
+                first_product(a, t, first, GROUP, x[:, t * GROUP : (t + 1) * GROUP])
+            act = ring.tile([P, GROUP, PACK], F32, name="act", bufs=12, align_bytes=64)
+            nc.scalar.activation(act[:], x[:].rearrange("p (t j) -> p j t", t=PACK), ACT.Gelu_apprx_sigmoid)
+            gains = gain[:, a, 0:PACK].unsqueeze(1).to_broadcast([P, GROUP, PACK])
+            nc.vector.tensor_tensor(rounded.rearrange("p (j t) -> p j t", t=PACK), act[:], gains, MULT)
+
+        def hidden_on_scalar(a, first, count, rounded):
+            planes = ring.tile([P, PACK, count], BF16, name="planes", align_bytes=64)
+            for pair in range(2):
+                x = psum.tile([P, 2 * count], F32, name="x")
+                for u in range(2):
+                    first_product(a, 2 * pair + u, first, count, x[:, u * count : (u + 1) * count])
+                act = ring.tile([P, 2 * count], F32, name="act", bufs=12, align_bytes=64)
+                nc.scalar.activation(act[:], x[:], ACT.Gelu_apprx_sigmoid)
+                for u in range(2):
+                    t = 2 * pair + u
+                    nc.scalar.activation(
+                        planes[:, t, :], act[:, u * count : (u + 1) * count], ACT.Copy, scale=gain[:, a, t : t + 1]
+                    )
+            nc.scalar.copy(out=rounded.rearrange("p (j t) -> p j t", t=PACK), in_=planes[:].rearrange("p t j -> p j t"))
+
+        def quantize_hidden(c, a, rounded, count):
+            codes = keep.tile([P, count], U32, name=f"h_codes{c}_{a}", align_bytes=64)
+            scales = keep.tile([P, count], U8, name=f"h_scales{c}_{a}", align_bytes=64)
+            nc.vector.quantize_mx(out=codes[:].bitcast(FP8X4), scales=scales[:], in_=rounded)
+            return codes, scales
+
+        def shortcut_pass(n, first, count, dst):
+            codes, scales = patch(first, count)
+            nc.tensor.matmul_mx(
+                out=dst,
+                lhsT=ws_codes[:, n * P : (n + 1) * P].bitcast(FP8X4),
+                lhsT_scale=out_scales[:, BLOCKS, :].bitcast(U8)[:, n * P : (n + 1) * P],
+                rhs=codes,
+                rhs_scale=scales,
+                start=True,
+                stop=False,
+            )
+
+        def second_pass(n, a, hidden, cols, dst):
+            codes, scales = hidden
+            nc.tensor.matmul_mx(
+                out=dst,
+                lhsT=w2_codes[:, a, 2 * n * P : 2 * (n + 1) * P].bitcast(FP4X4),
+                lhsT_scale=out_scales[:, a, :].bitcast(U8)[:, n * P : (n + 1) * P],
+                rhs=codes[:, cols].bitcast(FP8X4),
+                rhs_scale=scales[:, cols],
+                start=False,
+                stop=(a == BLOCKS - 1),
+            )
+
+        def leave_bank(c, n, y, count):
+            sums = keep.tile([P, count], F32, name=f"sums{c}_{n}", align_bytes=64)
+            nc.scalar.copy(out=sums[:], in_=y[:, 0:count])
+            return sums
+
+        def scatter(c, n, sums):
+            first, count = CHUNKS[c]
+            places = slots[:, first // 16 : (first + count) // 16]
+            nc.vector.tensor_tensor(windows[n][:].indirect(places), sums[:], weight[:, first : first + count], MULT)
+
+        gather_scales(0)
+        quantize_w1(0)
+        gather_codes(0)
+        gather_scales(1)
+        for n in range(TILES):
+            nc.vector.memset(windows[n][:], 0.0)
+
+        first, count = CHUNKS[0]
+        ys = [psum.tile([P, HALF], F32, name="y") for n in range(TILES)]
+        pending = None
+
+        def finish_block(a, rounded):
+            hidden = quantize_hidden(0, a, rounded[:], count)
+            for n in range(TILES):
+                if a == 0:
+                    shortcut_pass(n, first, count, ys[n][:])
+                second_pass(n, a, hidden, slice(0, count), ys[n][:])
+
+        for a in range(BLOCKS):
+            if a + 1 < BLOCKS:
+                quantize_w1(a + 1)
+            rounded = ring.tile([P, count * PACK], BF16, name="h_rounded", bufs=4, align_bytes=64)
+            for g in range(count // GROUP):
+                hidden_group(a, first + g * GROUP, rounded[:, g * GROUP * PACK : (g + 1) * GROUP * PACK])
+                if g == 0 and pending is not None:
+                    finish_block(*pending)
+            pending = (a, rounded)
+            if a == 1:
+                gather_codes(1)
+        finish_block(*pending)
+        sums = [[leave_bank(0, n, ys[n], count) for n in range(TILES)]]
+
+        for c in range(1, len(CHUNKS)):
+            first, count = CHUNKS[c]
+            hiddens = []
+            waiting = None
+            for a in range(BLOCKS):
+                rounded = ring.tile([P, count * PACK], BF16, name="h_rounded", bufs=4, align_bytes=64)
+                if a >= BLOCKS - SCALAR_BLOCKS[c]:
+                    hidden_on_scalar(a, first, count, rounded[:])
+                else:
+                    for g in range(count // GROUP):
+                        hidden_group(a, first + g * GROUP, rounded[:, g * GROUP * PACK : (g + 1) * GROUP * PACK])
+                if waiting is not None:
+                    hiddens.append(quantize_hidden(c, a - 1, waiting[:], count))
+                waiting = rounded
+            hiddens.append(quantize_hidden(c, BLOCKS - 1, waiting[:], count))
+            row = []
+            for n in range(TILES):
+                y = psum.tile([P, HALF], F32, name="y")
+                for g in range(count // GROUP):
+                    cols = slice(g * GROUP, (g + 1) * GROUP)
+                    shortcut_pass(n, first + g * GROUP, GROUP, y[:, cols])
+                    for a in range(BLOCKS):
+                        second_pass(n, a, hiddens[a], cols, y[:, cols])
+                row.append(leave_bank(c, n, y, count))
+            sums.append(row)
+            for n in range(TILES):
+                scatter(c - 1, n, sums[c - 1][n])
+        last = len(CHUNKS) - 1
+        for n in range(TILES):
+            scatter(last, n, sums[last][n])
+            nc.sync.dma_start(out=out[n * P : (n + 1) * P, :], in_=windows[n][:])

@@ -22,9 +22,12 @@ BLOCKS = H // (P * PACK)
 TILES = N // P
 GROUP = 128
 HALF = 512
+STEP = 256
+PLANE_BYTES = 2 * PACK * STEP
 CHUNKS = [(0, 512), (512, 256), (768, 256)]
-SCALAR_BLOCKS = [0, 3, 2]
-CAST_ON_VECTOR = [0, 64, 64, 64]
+ON_VECTOR = [None, [0], [0]]
+AFTER = [None, [None, 1, 2, 3], [1, 2, 3]]
+CAST_ON_VECTOR = [0, 96, 64, 32]
 
 
 def tile_list_masked_patch_block_kernel(
@@ -34,13 +37,15 @@ def tile_list_masked_patch_block_kernel(
     with ExitStack() as ctx:
         keep = ctx.enter_context(tc.tile_pool(name="keep", bufs=1))
         ring = ctx.enter_context(tc.tile_pool(name="ring", bufs=3))
+        shared = ctx.enter_context(tc.tile_pool(name="shared", bufs=1))
         psum = ctx.enter_context(tc.psum_pool(name="psum", bufs=4))
 
         picks = keep.tile([P, S // 16], U16, name="picks")
         slots = keep.tile([P, S // 16], U16, name="slots")
         table = keep.tile([P, T], I32, name="table", align_bytes=64)
         table_scales = keep.tile([P, T // 4], I32, name="table_scales", align_bytes=64)
-        raw = [keep.tile([P, PACK, P * PACK], F32, name=f"raw{a}", align_bytes=64) for a in range(BLOCKS)]
+        raw = [keep.tile([P, PACK, P * PACK], F32, name=f"raw{a}", align_bytes=64) for a in range(BLOCKS - 1)]
+        raw.append(shared.tile([P, PACK, P * PACK], F32, name="raw_last", offset=0, align_bytes=64))
         gain = keep.tile([P, BLOCKS, 8], F32, name="gain")
         w2_codes = keep.tile([P, BLOCKS, 2 * N], U8, name="w2_codes", align_bytes=64)
         ws_codes = keep.tile([P, N], I32, name="ws_codes", align_bytes=64)
@@ -52,19 +57,25 @@ def tile_list_masked_patch_block_kernel(
         w1_codes = [keep.tile([P, P * PACK], U32, name=f"w1_codes{a}", align_bytes=64) for a in range(BLOCKS)]
         w1_scales = [keep.tile([P, P * PACK], U8, name=f"w1_scales{a}", align_bytes=64) for a in range(BLOCKS)]
 
-        nc.vector.memset(table_scales[:], 0)
+        nc.gpsimd.memset(table_scales[:], 0)
         nc.vector.memset(out_scales[:], 0)
+        for n in range(TILES):
+            if n < TILES // 2:
+                nc.vector.memset(windows[n][:], 0.0)
+            else:
+                for u in range(2):
+                    nc.gpsimd.memset(windows[n][:, u * T2 // 2 : (u + 1) * T2 // 2], 0.0)
 
         def load_w1(a):
             cols = slice(a * P * PACK, (a + 1) * P * PACK)
             nc.sync.dma_start(out=raw[a][:], in_=w1[:, cols].rearrange("(p j) c -> p j c", j=PACK))
 
         nc.sync.dma_start(picks[:], offs)
+        load_w1(0)
         for q in range(4):
             nc.sync.dma_start(
                 out=table_scales[32 * q : 32 * q + 4, :], in_=tab_scales[0, 4 * q : 4 * q + 4, :].bitcast(I32)
             )
-        load_w1(0)
         nc.sync.dma_start(out=table[:], in_=tab_words[0].rearrange("p t i -> p (t i)").bitcast(I32))
         nc.sync.dma_start(out=gain[:, :, 0:PACK], in_=ga.rearrange("(a p t) -> p a t", p=P, t=PACK))
         for a in range(1, BLOCKS):
@@ -75,9 +86,11 @@ def tile_list_masked_patch_block_kernel(
                 out=out_scales[rows, 0:BLOCKS, :],
                 in_=w2_scales[:, 4 * q : 4 * q + 4, :].rearrange("a q c -> q a c").bitcast(I32),
             )
+        nc.sync.dma_start(out=w2_codes[:].bitcast(I32), in_=w2_words.rearrange("a p c -> p a c").bitcast(I32))
+        for q in range(4):
+            rows = slice(32 * q, 32 * q + 4)
             nc.sync.dma_start(out=out_scales[rows, BLOCKS, :], in_=ws_scales[0, 4 * q : 4 * q + 4, :].bitcast(I32))
         nc.sync.dma_start(out=ws_codes[:], in_=ws_words[0].rearrange("p c i -> p (c i)").bitcast(I32))
-        nc.sync.dma_start(out=w2_codes[:].bitcast(I32), in_=w2_words.rearrange("a p c -> p a c").bitcast(I32))
         nc.sync.dma_start(slots[:], offs2)
         nc.sync.dma_start(out=weight[:], in_=wgo)
 
@@ -100,7 +113,8 @@ def tile_list_masked_patch_block_kernel(
             split = CAST_ON_VECTOR[a]
             if split > 0:
                 nc.vector.tensor_copy(out=dst[:, 0:split], in_=src[:, 0:split])
-            nc.scalar.copy(out=dst[:, split:P], in_=src[:, split:P])
+            if split < P:
+                nc.scalar.copy(out=dst[:, split:P], in_=src[:, split:P])
             nc.vector.quantize_mx(out=w1_codes[a][:].bitcast(FP8X4), scales=w1_scales[a][:], in_=rounded[:])
 
         def first_product(a, t, first, count, dst):
@@ -117,21 +131,25 @@ def tile_list_masked_patch_block_kernel(
             )
 
         def hidden_group(a, first, rounded):
-            x = psum.tile([P, PACK * GROUP], F32, name="x")
-            for t in range(PACK):
-                first_product(a, t, first, GROUP, x[:, t * GROUP : (t + 1) * GROUP])
-            act = ring.tile([P, GROUP, PACK], F32, name="act", bufs=12, align_bytes=64)
-            nc.scalar.activation(act[:], x[:].rearrange("p (t j) -> p j t", t=PACK), ACT.Gelu_apprx_sigmoid)
-            gains = gain[:, a, 0:PACK].unsqueeze(1).to_broadcast([P, GROUP, PACK])
+            act = ring.tile([P, STEP, PACK], F32, name="act", bufs=8, align_bytes=64)
+            for lo in range(0, STEP, GROUP):
+                x = psum.tile([P, PACK * GROUP], F32, name="x")
+                for t in range(PACK):
+                    first_product(a, t, first + lo, GROUP, x[:, t * GROUP : (t + 1) * GROUP])
+                nc.scalar.activation(
+                    act[:, lo : lo + GROUP, :], x[:].rearrange("p (t j) -> p j t", t=PACK), ACT.Gelu_apprx_sigmoid
+                )
+            gains = gain[:, a, 0:PACK].unsqueeze(1).to_broadcast([P, STEP, PACK])
             nc.vector.tensor_tensor(rounded.rearrange("p (j t) -> p j t", t=PACK), act[:], gains, MULT)
 
-        def hidden_on_scalar(a, first, count, rounded):
-            planes = ring.tile([P, PACK, count], BF16, name="planes", align_bytes=64)
+        def hidden_on_scalar(c, a, first, count, rounded):
+            place = (c - 1) * BLOCKS + a
+            planes = shared.tile([P, PACK, count], BF16, name=f"planes{place}", offset=place * PLANE_BYTES, align_bytes=64)
             for pair in range(2):
                 x = psum.tile([P, 2 * count], F32, name="x")
                 for u in range(2):
                     first_product(a, 2 * pair + u, first, count, x[:, u * count : (u + 1) * count])
-                act = ring.tile([P, 2 * count], F32, name="act", bufs=12, align_bytes=64)
+                act = ring.tile([P, 2 * count], F32, name="act_planes", bufs=2, align_bytes=64)
                 nc.scalar.activation(act[:], x[:], ACT.Gelu_apprx_sigmoid)
                 for u in range(2):
                     t = 2 * pair + u
@@ -154,7 +172,7 @@ def tile_list_masked_patch_block_kernel(
                 lhsT_scale=out_scales[:, BLOCKS, :].bitcast(U8)[:, n * P : (n + 1) * P],
                 rhs=codes,
                 rhs_scale=scales,
-                start=True,
+                start=False,
                 stop=False,
             )
 
@@ -166,80 +184,100 @@ def tile_list_masked_patch_block_kernel(
                 lhsT_scale=out_scales[:, a, :].bitcast(U8)[:, n * P : (n + 1) * P],
                 rhs=codes[:, cols].bitcast(FP8X4),
                 rhs_scale=scales[:, cols],
-                start=False,
+                start=(a == 0),
                 stop=(a == BLOCKS - 1),
             )
 
-        def leave_bank(c, n, y, count):
-            sums = keep.tile([P, count], F32, name=f"sums{c}_{n}", align_bytes=64)
-            nc.scalar.copy(out=sums[:], in_=y[:, 0:count])
-            return sums
+        def leave_bank(y, first, count, sums):
+            nc.vector.tensor_tensor(sums, y[:, 0:count], weight[:, first : first + count], MULT)
 
-        def scatter(c, n, sums):
-            first, count = CHUNKS[c]
+        def sums_tile(c, n, count, place):
+            if place is None:
+                return keep.tile([P, count], F32, name=f"sums{c}_{n}", align_bytes=64)
+            return shared.tile([P, count], F32, name=f"sums{c}_{n}", offset=place * PLANE_BYTES, align_bytes=64)
+
+        def scatter(n, first, count, sums):
             places = slots[:, first // 16 : (first + count) // 16]
-            nc.vector.tensor_tensor(windows[n][:].indirect(places), sums[:], weight[:, first : first + count], MULT)
+            nc.vector.tensor_copy(windows[n][:].indirect(places), sums[:])
+
+        def finish_tile(c, n, y, place):
+            first, count = CHUNKS[c]
+            sums = sums_tile(c, n, count, place)
+            leave_bank(y, first, count, sums[:])
+            scatter(n, first, count, sums)
+
+        def second_product(c, n, hiddens):
+            first, count = CHUNKS[c]
+            y = psum.tile([P, HALF], F32, name="y")
+            for lo in range(0, count, GROUP):
+                cols = slice(lo, lo + GROUP)
+                for a in range(BLOCKS):
+                    if a == BLOCKS - 1:
+                        shortcut_pass(n, first + lo, GROUP, y[:, cols])
+                    second_pass(n, a, hiddens[a], cols, y[:, cols])
+            return y
+
+        def hidden_chunk(c, earlier):
+            first, count = CHUNKS[c]
+            hiddens = []
+            for n, a in enumerate(AFTER[c]):
+                if a is None:
+                    finish_tile(c - 1, n, earlier[n], None)
+            for a in range(BLOCKS):
+                rounded = ring.tile([P, count * PACK], BF16, name="h_rounded_late", bufs=8, align_bytes=64)
+                if a in ON_VECTOR[c]:
+                    hidden_group(a, first, rounded[:])
+                else:
+                    hidden_on_scalar(c, a, first, count, rounded[:])
+                hiddens.append(quantize_hidden(c, a, rounded[:], count))
+                for n, b in enumerate(AFTER[c]):
+                    if b == a:
+                        finish_tile(c - 1, n, earlier[n], (c - 1) * BLOCKS + a)
+            return hiddens
 
         gather_scales(0)
         quantize_w1(0)
         gather_codes(0)
         gather_scales(1)
-        for n in range(TILES):
-            nc.vector.memset(windows[n][:], 0.0)
 
         first, count = CHUNKS[0]
         ys = [psum.tile([P, HALF], F32, name="y") for n in range(TILES)]
         pending = None
 
+        hiddens = []
+
         def finish_block(a, rounded):
-            hidden = quantize_hidden(0, a, rounded[:], count)
-            for n in range(TILES):
-                if a == 0:
-                    shortcut_pass(n, first, count, ys[n][:])
-                second_pass(n, a, hidden, slice(0, count), ys[n][:])
+            hiddens.append(quantize_hidden(0, a, rounded[:], count))
 
         for a in range(BLOCKS):
             if a + 1 < BLOCKS:
                 quantize_w1(a + 1)
-            rounded = ring.tile([P, count * PACK], BF16, name="h_rounded", bufs=4, align_bytes=64)
-            for g in range(count // GROUP):
-                hidden_group(a, first + g * GROUP, rounded[:, g * GROUP * PACK : (g + 1) * GROUP * PACK])
+            rounded = ring.tile([P, count * PACK], BF16, name="h_rounded", align_bytes=64)
+            for g in range(count // STEP):
+                hidden_group(a, first + g * STEP, rounded[:, g * STEP * PACK : (g + 1) * STEP * PACK])
                 if g == 0 and pending is not None:
                     finish_block(*pending)
             pending = (a, rounded)
             if a == 1:
                 gather_codes(1)
         finish_block(*pending)
-        sums = [[leave_bank(0, n, ys[n], count) for n in range(TILES)]]
+        for a in range(BLOCKS):
+            for n in range(TILES):
+                if a == BLOCKS - 1:
+                    shortcut_pass(n, first, count, ys[n][:])
+                second_pass(n, a, hiddens[a], slice(0, count), ys[n][:])
 
-        for c in range(1, len(CHUNKS)):
-            first, count = CHUNKS[c]
-            hiddens = []
-            waiting = None
-            for a in range(BLOCKS):
-                rounded = ring.tile([P, count * PACK], BF16, name="h_rounded", bufs=4, align_bytes=64)
-                if a >= BLOCKS - SCALAR_BLOCKS[c]:
-                    hidden_on_scalar(a, first, count, rounded[:])
-                else:
-                    for g in range(count // GROUP):
-                        hidden_group(a, first + g * GROUP, rounded[:, g * GROUP * PACK : (g + 1) * GROUP * PACK])
-                if waiting is not None:
-                    hiddens.append(quantize_hidden(c, a - 1, waiting[:], count))
-                waiting = rounded
-            hiddens.append(quantize_hidden(c, BLOCKS - 1, waiting[:], count))
-            row = []
-            for n in range(TILES):
-                y = psum.tile([P, HALF], F32, name="y")
-                for g in range(count // GROUP):
-                    cols = slice(g * GROUP, (g + 1) * GROUP)
-                    shortcut_pass(n, first + g * GROUP, GROUP, y[:, cols])
-                    for a in range(BLOCKS):
-                        second_pass(n, a, hiddens[a], cols, y[:, cols])
-                row.append(leave_bank(c, n, y, count))
-            sums.append(row)
-            for n in range(TILES):
-                scatter(c - 1, n, sums[c - 1][n])
-        last = len(CHUNKS) - 1
+        last = TILES - 1
+        hiddens = hidden_chunk(1, ys)
+        ys = [second_product(1, n, hiddens) for n in range(TILES)]
+        joint = keep.tile([P, HALF], F32, name="joint", align_bytes=64)
+        leave_bank(ys[last], HALF, STEP, joint[:, 0:STEP])
+        hiddens = hidden_chunk(2, ys)
         for n in range(TILES):
-            scatter(last, n, sums[last][n])
+            y = second_product(2, n, hiddens)
+            if n < last:
+                finish_tile(2, n, y, None)
+            else:
+                leave_bank(y, HALF + STEP, STEP, joint[:, STEP:HALF])
+                scatter(n, HALF, HALF, joint)
             nc.sync.dma_start(out=out[n * P : (n + 1) * P, :], in_=windows[n][:])

@@ -23,11 +23,11 @@ TILES = N // P
 GROUP = 128
 HALF = 512
 STEP = 256
-PLANE_BYTES = 2 * PACK * STEP
+PLACE_BYTES = 4 * PACK * STEP
 CHUNKS = [(0, 512), (512, 256), (768, 256)]
-ON_VECTOR = [None, [0], [0]]
-AFTER = [None, [None, 1, 2, 3], [1, 2, 3]]
-CAST_ON_VECTOR = [0, 96, 64, 32]
+ON_SCALAR = [(1, 2), (1, 3), (2, 2), (2, 3)]
+RELEASES = [[1], [2, 3], [0], [1, 2]]
+CAST_ON_VECTOR = [0, 128, 96, 64]
 
 
 def tile_list_masked_patch_block_kernel(
@@ -60,7 +60,7 @@ def tile_list_masked_patch_block_kernel(
         nc.gpsimd.memset(table_scales[:], 0)
         nc.vector.memset(out_scales[:], 0)
         for n in range(TILES):
-            if n < TILES // 2:
+            if n < TILES - 1:
                 nc.vector.memset(windows[n][:], 0.0)
             else:
                 for u in range(2):
@@ -77,8 +77,9 @@ def tile_list_masked_patch_block_kernel(
                 out=table_scales[32 * q : 32 * q + 4, :], in_=tab_scales[0, 4 * q : 4 * q + 4, :].bitcast(I32)
             )
         nc.sync.dma_start(out=table[:], in_=tab_words[0].rearrange("p t i -> p (t i)").bitcast(I32))
+        load_w1(1)
         nc.sync.dma_start(out=gain[:, :, 0:PACK], in_=ga.rearrange("(a p t) -> p a t", p=P, t=PACK))
-        for a in range(1, BLOCKS):
+        for a in range(2, BLOCKS):
             load_w1(a)
         for q in range(4):
             rows = slice(32 * q, 32 * q + 4)
@@ -142,9 +143,9 @@ def tile_list_masked_patch_block_kernel(
             gains = gain[:, a, 0:PACK].unsqueeze(1).to_broadcast([P, STEP, PACK])
             nc.vector.tensor_tensor(rounded.rearrange("p (j t) -> p j t", t=PACK), act[:], gains, MULT)
 
-        def hidden_on_scalar(c, a, first, count, rounded):
-            place = (c - 1) * BLOCKS + a
-            planes = shared.tile([P, PACK, count], BF16, name=f"planes{place}", offset=place * PLANE_BYTES, align_bytes=64)
+        def hidden_on_scalar(place, a, first, count, rounded):
+            offset = place * PLACE_BYTES + PLACE_BYTES // 4
+            planes = shared.tile([P, PACK, count], BF16, name=f"planes{place}", offset=offset, align_bytes=64)
             for pair in range(2):
                 x = psum.tile([P, 2 * count], F32, name="x")
                 for u in range(2):
@@ -188,22 +189,25 @@ def tile_list_masked_patch_block_kernel(
                 stop=(a == BLOCKS - 1),
             )
 
-        def leave_bank(y, first, count, sums):
-            nc.vector.tensor_tensor(sums, y[:, 0:count], weight[:, first : first + count], MULT)
+        def leave_bank(y, count, sums):
+            nc.scalar.copy(out=sums, in_=y[:, 0:count])
 
-        def sums_tile(c, n, count, place):
-            if place is None:
+        def sums_tile(c, n, count, gate):
+            if gate is None:
                 return keep.tile([P, count], F32, name=f"sums{c}_{n}", align_bytes=64)
-            return shared.tile([P, count], F32, name=f"sums{c}_{n}", offset=place * PLANE_BYTES, align_bytes=64)
+            place, upper = gate
+            middle = place * PLACE_BYTES + PLACE_BYTES // 2
+            offset = middle if upper else middle - 4 * count
+            return shared.tile([P, count], F32, name=f"sums{c}_{n}", offset=offset, align_bytes=64)
 
         def scatter(n, first, count, sums):
             places = slots[:, first // 16 : (first + count) // 16]
-            nc.vector.tensor_copy(windows[n][:].indirect(places), sums[:])
+            nc.vector.tensor_tensor(windows[n][:].indirect(places), sums[:], weight[:, first : first + count], MULT)
 
         def finish_tile(c, n, y, place):
             first, count = CHUNKS[c]
             sums = sums_tile(c, n, count, place)
-            leave_bank(y, first, count, sums[:])
+            leave_bank(y, count, sums[:])
             scatter(n, first, count, sums)
 
         def second_product(c, n, hiddens):
@@ -217,23 +221,23 @@ def tile_list_masked_patch_block_kernel(
                     second_pass(n, a, hiddens[a], cols, y[:, cols])
             return y
 
-        def hidden_chunk(c, earlier):
+        late = {}
+
+        def late_block(c, a):
             first, count = CHUNKS[c]
-            hiddens = []
-            for n, a in enumerate(AFTER[c]):
-                if a is None:
-                    finish_tile(c - 1, n, earlier[n], None)
-            for a in range(BLOCKS):
-                rounded = ring.tile([P, count * PACK], BF16, name="h_rounded_late", bufs=8, align_bytes=64)
-                if a in ON_VECTOR[c]:
-                    hidden_group(a, first, rounded[:])
-                else:
-                    hidden_on_scalar(c, a, first, count, rounded[:])
-                hiddens.append(quantize_hidden(c, a, rounded[:], count))
-                for n, b in enumerate(AFTER[c]):
-                    if b == a:
-                        finish_tile(c - 1, n, earlier[n], (c - 1) * BLOCKS + a)
-            return hiddens
+            rounded = ring.tile([P, count * PACK], BF16, name="h_rounded_late", bufs=8, align_bytes=64)
+            if (c, a) in ON_SCALAR:
+                hidden_on_scalar(ON_SCALAR.index((c, a)), a, first, count, rounded[:])
+            else:
+                hidden_group(a, first, rounded[:])
+            late[c, a] = quantize_hidden(c, a, rounded[:], count)
+
+        def scalar_blocks(c, earlier):
+            for place, (d, a) in enumerate(ON_SCALAR):
+                if d == c:
+                    late_block(c, a)
+                    for upper, n in enumerate(RELEASES[place]):
+                        finish_tile(c - 1, n, earlier[n], (place, upper))
 
         gather_scales(0)
         quantize_w1(0)
@@ -268,16 +272,22 @@ def tile_list_masked_patch_block_kernel(
                 second_pass(n, a, hiddens[a], slice(0, count), ys[n][:])
 
         last = TILES - 1
-        hiddens = hidden_chunk(1, ys)
-        ys = [second_product(1, n, hiddens) for n in range(TILES)]
+        for c in (1, 2):
+            for a in range(BLOCKS):
+                if (c, a) not in ON_SCALAR:
+                    late_block(c, a)
+        finish_tile(0, 0, ys[0], None)
+        scalar_blocks(1, ys)
+        ys = [second_product(1, n, [late[1, a] for a in range(BLOCKS)]) for n in range(TILES)]
         joint = keep.tile([P, HALF], F32, name="joint", align_bytes=64)
-        leave_bank(ys[last], HALF, STEP, joint[:, 0:STEP])
-        hiddens = hidden_chunk(2, ys)
+        leave_bank(ys[last], STEP, joint[:, 0:STEP])
+        scalar_blocks(2, ys)
+        hiddens = [late[2, a] for a in range(BLOCKS)]
         for n in range(TILES):
             y = second_product(2, n, hiddens)
             if n < last:
                 finish_tile(2, n, y, None)
             else:
-                leave_bank(y, HALF + STEP, STEP, joint[:, STEP:HALF])
+                leave_bank(y, STEP, joint[:, STEP:HALF])
                 scatter(n, HALF, HALF, joint)
             nc.sync.dma_start(out=out[n * P : (n + 1) * P, :], in_=windows[n][:])

@@ -23,11 +23,11 @@ TILES = N // P
 GROUP = 128
 HALF = 512
 STEP = 256
-PLACE_BYTES = 4 * PACK * STEP
-CHUNKS = [(0, 512), (512, 256), (768, 256)]
-ON_SCALAR = [(1, 2), (1, 3), (2, 2), (2, 3)]
-RELEASES = [[1], [2, 3], [0], [1, 2]]
-CAST_ON_VECTOR = [0, 128, 96, 64]
+CAST_ON_VECTOR = [0, 128, 32, 64]
+ON_SCALAR = [0, 1, 1, 2]
+CHUNKS = S // STEP
+AHEAD = 2
+KIB = 1024
 
 
 def tile_list_masked_patch_block_kernel(
@@ -38,33 +38,32 @@ def tile_list_masked_patch_block_kernel(
         keep = ctx.enter_context(tc.tile_pool(name="keep", bufs=1))
         ring = ctx.enter_context(tc.tile_pool(name="ring", bufs=3))
         shared = ctx.enter_context(tc.tile_pool(name="shared", bufs=1))
-        psum = ctx.enter_context(tc.psum_pool(name="psum", bufs=4))
+        lower = ctx.enter_context(tc.psum_pool(name="lower", bufs=1))
+        upper = ctx.enter_context(tc.psum_pool(name="upper", bufs=1))
 
         picks = keep.tile([P, S // 16], U16, name="picks")
         slots = keep.tile([P, S // 16], U16, name="slots")
         table = keep.tile([P, T], I32, name="table", align_bytes=64)
         table_scales = keep.tile([P, T // 4], I32, name="table_scales", align_bytes=64)
-        raw = [keep.tile([P, PACK, P * PACK], F32, name=f"raw{a}", align_bytes=64) for a in range(BLOCKS - 1)]
-        raw.append(shared.tile([P, PACK, P * PACK], F32, name="raw_last", offset=0, align_bytes=64))
+        raw = [keep.tile([P, PACK, P * PACK], F32, name=f"raw{a}", align_bytes=64) for a in range(BLOCKS)]
         gain = keep.tile([P, BLOCKS, 8], F32, name="gain")
         w2_codes = keep.tile([P, BLOCKS, 2 * N], U8, name="w2_codes", align_bytes=64)
         ws_codes = keep.tile([P, N], I32, name="ws_codes", align_bytes=64)
         out_scales = keep.tile([P, BLOCKS + 1, N // 4], I32, name="out_scales", align_bytes=64)
         weight = keep.tile([P, S], F32, name="weight", align_bytes=64)
         windows = [keep.tile([P, T2], F32, name=f"window{n}", align_bytes=64) for n in range(TILES)]
-        v_codes = [keep.tile([P, HALF], U32, name=f"v_codes{i}", align_bytes=64) for i in range(2)]
-        v_scales = [keep.tile([P, HALF], U8, name=f"v_scales{i}", align_bytes=64) for i in range(2)]
+        v_codes = [
+            keep.tile([P, HALF], U32, name="v_codes0", align_bytes=64),
+            keep.tile([P, HALF], U32, name="v_codes1", align_bytes=64),
+        ]
+        v_scales = keep.tile([P, S], U8, name="v_scales", align_bytes=64)
         w1_codes = [keep.tile([P, P * PACK], U32, name=f"w1_codes{a}", align_bytes=64) for a in range(BLOCKS)]
         w1_scales = [keep.tile([P, P * PACK], U8, name=f"w1_scales{a}", align_bytes=64) for a in range(BLOCKS)]
 
-        nc.gpsimd.memset(table_scales[:], 0)
+        nc.vector.memset(table_scales[:], 0)
         nc.vector.memset(out_scales[:], 0)
         for n in range(TILES):
-            if n < TILES - 1:
-                nc.vector.memset(windows[n][:], 0.0)
-            else:
-                for u in range(2):
-                    nc.gpsimd.memset(windows[n][:, u * T2 // 2 : (u + 1) * T2 // 2], 0.0)
+            nc.vector.memset(windows[n][:], 0.0)
 
         def load_w1(a):
             cols = slice(a * P * PACK, (a + 1) * P * PACK)
@@ -92,12 +91,8 @@ def tile_list_masked_patch_block_kernel(
             rows = slice(32 * q, 32 * q + 4)
             nc.sync.dma_start(out=out_scales[rows, BLOCKS, :], in_=ws_scales[0, 4 * q : 4 * q + 4, :].bitcast(I32))
         nc.sync.dma_start(out=ws_codes[:], in_=ws_words[0].rearrange("p c i -> p (c i)").bitcast(I32))
-        nc.sync.dma_start(slots[:], offs2)
         nc.sync.dma_start(out=weight[:], in_=wgo)
-
-        def gather_scales(i):
-            cols = slice(i * HALF // 16, (i + 1) * HALF // 16)
-            nc.vector.tensor_copy(v_scales[i][:], table_scales[:].bitcast(U8).indirect(picks[:, cols]))
+        nc.sync.dma_start(slots[:], offs2)
 
         def gather_codes(i):
             cols = slice(i * HALF // 16, (i + 1) * HALF // 16)
@@ -105,7 +100,7 @@ def tile_list_masked_patch_block_kernel(
 
         def patch(first, count):
             i, lo = divmod(first, HALF)
-            return v_codes[i][:, lo : lo + count].bitcast(FP8X4), v_scales[i][:, lo : lo + count]
+            return v_codes[i][:, lo : lo + count].bitcast(FP8X4), v_scales[:, first : first + count]
 
         def quantize_w1(a):
             rounded = ring.tile([P, P * PACK * PACK], BF16, name="w1_rounded", align_bytes=64)
@@ -131,23 +126,34 @@ def tile_list_masked_patch_block_kernel(
                 stop=True,
             )
 
-        def hidden_group(a, first, rounded):
-            act = ring.tile([P, STEP, PACK], F32, name="act", bufs=8, align_bytes=64)
-            for lo in range(0, STEP, GROUP):
-                x = psum.tile([P, PACK * GROUP], F32, name="x")
+        turns = []
+
+        def upper_bank():
+            turns.append(len(turns))
+            return upper.tile([P, HALF], F32, name=f"upper{turns[-1]}", offset=turns[-1] % TILES * 2 * KIB)
+
+        late_turns = []
+
+        def lower_bank():
+            late_turns.append(len(late_turns))
+            return lower.tile([P, HALF], F32, name=f"lower{late_turns[-1]}", offset=late_turns[-1] % TILES * 2 * KIB)
+
+        def activate(a, first, count, act):
+            for lo in range(0, count, GROUP):
+                x = upper_bank() if first == 0 else lower_bank()
                 for t in range(PACK):
                     first_product(a, t, first + lo, GROUP, x[:, t * GROUP : (t + 1) * GROUP])
                 nc.scalar.activation(
                     act[:, lo : lo + GROUP, :], x[:].rearrange("p (t j) -> p j t", t=PACK), ACT.Gelu_apprx_sigmoid
                 )
-            gains = gain[:, a, 0:PACK].unsqueeze(1).to_broadcast([P, STEP, PACK])
-            nc.vector.tensor_tensor(rounded.rearrange("p (j t) -> p j t", t=PACK), act[:], gains, MULT)
 
-        def hidden_on_scalar(place, a, first, count, rounded):
-            offset = place * PLACE_BYTES + PLACE_BYTES // 4
-            planes = shared.tile([P, PACK, count], BF16, name=f"planes{place}", offset=offset, align_bytes=64)
+        def apply_gain(engine, a, act, rounded):
+            gains = gain[:, a, 0:PACK].unsqueeze(1).to_broadcast(list(act.shape))
+            engine.tensor_tensor(rounded.rearrange("p (j t) -> p j t", t=PACK), act, gains, MULT)
+
+        def hidden_on_scalar(a, first, count, planes):
             for pair in range(2):
-                x = psum.tile([P, 2 * count], F32, name="x")
+                x = lower_bank()
                 for u in range(2):
                     first_product(a, 2 * pair + u, first, count, x[:, u * count : (u + 1) * count])
                 act = ring.tile([P, 2 * count], F32, name="act_planes", bufs=2, align_bytes=64)
@@ -157,11 +163,13 @@ def tile_list_masked_patch_block_kernel(
                     nc.scalar.activation(
                         planes[:, t, :], act[:, u * count : (u + 1) * count], ACT.Copy, scale=gain[:, a, t : t + 1]
                     )
+
+        def interleave(planes, rounded):
             nc.scalar.copy(out=rounded.rearrange("p (j t) -> p j t", t=PACK), in_=planes[:].rearrange("p t j -> p j t"))
 
-        def quantize_hidden(c, a, rounded, count):
-            codes = keep.tile([P, count], U32, name=f"h_codes{c}_{a}", align_bytes=64)
-            scales = keep.tile([P, count], U8, name=f"h_scales{c}_{a}", align_bytes=64)
+        def quantize_hidden(name, rounded, count):
+            codes = keep.tile([P, count], U32, name=f"h_codes{name}", align_bytes=64)
+            scales = keep.tile([P, count], U8, name=f"h_scales{name}", align_bytes=64)
             nc.vector.quantize_mx(out=codes[:].bitcast(FP8X4), scales=scales[:], in_=rounded)
             return codes, scales
 
@@ -177,7 +185,7 @@ def tile_list_masked_patch_block_kernel(
                 stop=False,
             )
 
-        def second_pass(n, a, hidden, cols, dst):
+        def second_pass(n, a, hidden, cols, dst, start, stop):
             codes, scales = hidden
             nc.tensor.matmul_mx(
                 out=dst,
@@ -185,109 +193,134 @@ def tile_list_masked_patch_block_kernel(
                 lhsT_scale=out_scales[:, a, :].bitcast(U8)[:, n * P : (n + 1) * P],
                 rhs=codes[:, cols].bitcast(FP8X4),
                 rhs_scale=scales[:, cols],
-                start=(a == 0),
-                stop=(a == BLOCKS - 1),
+                start=start,
+                stop=stop,
             )
 
-        def leave_bank(y, count, sums):
-            nc.scalar.copy(out=sums, in_=y[:, 0:count])
+        def places(first, count):
+            return slots[:, first // 16 : (first + count) // 16]
 
-        def sums_tile(c, n, count, gate):
+        def scatter_weighted(n, first, count, sums):
+            nc.vector.tensor_tensor(
+                windows[n][:].indirect(places(first, count)), sums[:], weight[:, first : first + count], MULT
+            )
+
+        def band_passes(n, a, hidden, base, dst):
+            for lo in range(0, STEP, GROUP):
+                start = a == 0 and lo == 0
+                stop = a == BLOCKS - 1 and lo + GROUP == STEP
+                cols = slice(base + lo, base + lo + GROUP)
+                second_pass(n, a, hidden, cols, dst[:, lo : lo + GROUP], start, stop)
+
+        def late_product(n, c, hidden, dst):
+            for a in range(BLOCKS):
+                if a == BLOCKS - 1:
+                    shortcut_pass(n, c * STEP, STEP, dst)
+                band_passes(n, a, hidden, a * STEP, dst)
+
+        def act_tile(c, a, place):
+            return shared.tile([P, STEP, PACK], F32, name=f"act{c}_{a}", offset=(8 + 4 * place) * KIB, align_bytes=64)
+
+        def gate_offset(c):
+            return (40 + 2 * (c - 1)) * KIB
+
+        def weigh(c, n, y, gate):
             if gate is None:
-                return keep.tile([P, count], F32, name=f"sums{c}_{n}", align_bytes=64)
-            place, upper = gate
-            middle = place * PLACE_BYTES + PLACE_BYTES // 2
-            offset = middle if upper else middle - 4 * count
-            return shared.tile([P, count], F32, name=f"sums{c}_{n}", offset=offset, align_bytes=64)
-
-        def scatter(n, first, count, sums):
-            places = slots[:, first // 16 : (first + count) // 16]
-            nc.vector.tensor_tensor(windows[n][:].indirect(places), sums[:], weight[:, first : first + count], MULT)
-
-        def finish_tile(c, n, y, place):
-            first, count = CHUNKS[c]
-            sums = sums_tile(c, n, count, place)
-            leave_bank(y, count, sums[:])
-            scatter(n, first, count, sums)
-
-        def second_product(c, n, hiddens):
-            first, count = CHUNKS[c]
-            y = psum.tile([P, HALF], F32, name="y")
-            for lo in range(0, count, GROUP):
-                cols = slice(lo, lo + GROUP)
-                for a in range(BLOCKS):
-                    if a == BLOCKS - 1:
-                        shortcut_pass(n, first + lo, GROUP, y[:, cols])
-                    second_pass(n, a, hiddens[a], cols, y[:, cols])
-            return y
-
-        late = {}
-
-        def late_block(c, a):
-            first, count = CHUNKS[c]
-            rounded = ring.tile([P, count * PACK], BF16, name="h_rounded_late", bufs=8, align_bytes=64)
-            if (c, a) in ON_SCALAR:
-                hidden_on_scalar(ON_SCALAR.index((c, a)), a, first, count, rounded[:])
+                weighted = ring.tile([P, STEP], F32, name="weighted", bufs=3, align_bytes=64)
             else:
-                hidden_group(a, first, rounded[:])
-            late[c, a] = quantize_hidden(c, a, rounded[:], count)
+                offset = gate_offset(gate)
+                weighted = shared.tile([P, STEP], F32, name=f"weighted{c}", offset=offset, align_bytes=64)
+            nc.vector.tensor_tensor(weighted[:], y, weight[:, c * STEP : (c + 1) * STEP], MULT)
+            return weighted
 
-        def scalar_blocks(c, earlier):
-            for place, (d, a) in enumerate(ON_SCALAR):
-                if d == c:
-                    late_block(c, a)
-                    for upper, n in enumerate(RELEASES[place]):
-                        finish_tile(c - 1, n, earlier[n], (place, upper))
+        def scatter_copy(c, n, weighted):
+            nc.vector.tensor_copy(windows[n][:].indirect(places(c * STEP, STEP)), weighted[:])
 
-        gather_scales(0)
+        acts = {}
+
+        def late_activate(c, a):
+            acts[c, a] = act_tile(c, a, [2, 0, 1][a] if c == 1 else 3 * c - 3 + a)
+            activate(a, c * STEP, STEP, acts[c, a])
+
+        def late_hidden(c):
+            first = c * STEP
+            rounded = shared.tile([P, BLOCKS * STEP * PACK], BF16, name=f"late_rounded{c}", offset=0, align_bytes=64)
+            count = ON_SCALAR[c]
+            waiting = []
+            for a in range(BLOCKS):
+                dst = rounded[:, a * STEP * PACK : (a + 1) * STEP * PACK]
+                if a < BLOCKS - count:
+                    if (c, a) not in acts:
+                        late_activate(c, a)
+                    apply_gain(nc.gpsimd, a, acts[c, a][:], dst)
+                else:
+                    if a == last:
+                        offset = gate_offset(c)
+                        planes = shared.tile([P, PACK, STEP], BF16, name=f"planes{c}", offset=offset, align_bytes=64)
+                    else:
+                        planes = ring.tile([P, PACK, STEP], BF16, name="planes", bufs=2, align_bytes=64)
+                    hidden_on_scalar(a, first, STEP, planes)
+                    waiting.append((planes, dst))
+            if c + 1 < CHUNKS:
+                for a in range(AHEAD):
+                    late_activate(c + 1, a)
+            for planes, dst in waiting:
+                interleave(planes, dst)
+            return rounded
+
+        nc.vector.tensor_copy(v_scales[:], table_scales[:].bitcast(U8).indirect(picks[:]))
         quantize_w1(0)
         gather_codes(0)
-        gather_scales(1)
+        gather_codes(1)
+        quantize_w1(1)
 
-        first, count = CHUNKS[0]
-        ys = [psum.tile([P, HALF], F32, name="y") for n in range(TILES)]
-        pending = None
-
+        last = BLOCKS - 1
         hiddens = []
-
-        def finish_block(a, rounded):
-            hiddens.append(quantize_hidden(0, a, rounded[:], count))
-
         for a in range(BLOCKS):
-            if a + 1 < BLOCKS:
-                quantize_w1(a + 1)
-            rounded = ring.tile([P, count * PACK], BF16, name="h_rounded", align_bytes=64)
-            for g in range(count // STEP):
-                hidden_group(a, first + g * STEP, rounded[:, g * STEP * PACK : (g + 1) * STEP * PACK])
-                if g == 0 and pending is not None:
-                    finish_block(*pending)
-            pending = (a, rounded)
-            if a == 1:
-                gather_codes(1)
-        finish_block(*pending)
-        for a in range(BLOCKS):
-            for n in range(TILES):
-                if a == BLOCKS - 1:
-                    shortcut_pass(n, first, count, ys[n][:])
-                second_pass(n, a, hiddens[a], slice(0, count), ys[n][:])
-
-        last = TILES - 1
-        for c in (1, 2):
-            for a in range(BLOCKS):
-                if (c, a) not in ON_SCALAR:
-                    late_block(c, a)
-        finish_tile(0, 0, ys[0], None)
-        scalar_blocks(1, ys)
-        ys = [second_product(1, n, [late[1, a] for a in range(BLOCKS)]) for n in range(TILES)]
-        joint = keep.tile([P, HALF], F32, name="joint", align_bytes=64)
-        leave_bank(ys[last], STEP, joint[:, 0:STEP])
-        scalar_blocks(2, ys)
-        hiddens = [late[2, a] for a in range(BLOCKS)]
-        for n in range(TILES):
-            y = second_product(2, n, hiddens)
-            if n < last:
-                finish_tile(2, n, y, None)
+            if a < last:
+                rounded = ring.tile([P, STEP * PACK], BF16, name="h_rounded", bufs=2, align_bytes=64)
             else:
-                leave_bank(y, STEP, joint[:, STEP:HALF])
-                scatter(n, HALF, HALF, joint)
+                rounded = shared.tile([P, STEP * PACK], BF16, name="h_rounded_last", offset=0, align_bytes=64)
+            act = act_tile(0, a, a % 2)
+            activate(a, 0, STEP, act)
+            apply_gain(nc.vector, a, act[:], rounded[:])
+            hiddens.append(quantize_hidden(a, rounded[:], STEP))
+            if a + 2 < BLOCKS:
+                quantize_w1(a + 2)
+        ys = [upper_bank() for n in range(TILES)]
+        for n in range(TILES):
+            for a in range(BLOCKS):
+                if a == last:
+                    shortcut_pass(n, 0, STEP, ys[n][:, 0:STEP])
+                band_passes(n, a, hiddens[a], 0, ys[n][:, 0:STEP])
+
+        for c in range(1, CHUNKS):
+            early = TILES - 1 if c < CHUNKS - 1 else TILES - 2
+            for n in range(early):
+                scatter_copy(c - 1, n, weigh(c - 1, n, ys[n][:, 0:STEP], None))
+            rounded = late_hidden(c)
+            if c < CHUNKS - 1:
+                weighted = weigh(c - 1, early, ys[early][:, 0:STEP], c)
+                hidden = quantize_hidden(f"late{c}", rounded[:], BLOCKS * STEP)
+                scatter_copy(c - 1, early, weighted)
+                ys = [upper_bank() for n in range(TILES)]
+                for n in range(TILES):
+                    late_product(n, c, hidden, ys[n][:, 0:STEP])
+        c = CHUNKS - 1
+        hidden = quantize_hidden(f"late{c}", rounded[:], BLOCKS * STEP)
+        sums = shared.tile([P, STEP], F32, name="sums_held", offset=gate_offset(c), align_bytes=64)
+        nc.scalar.copy(out=sums[:], in_=ys[early][:, 0:STEP])
+        scatter_weighted(early, (c - 1) * STEP, STEP, sums)
+        for n in range(TILES):
+            if n < last:
+                y = upper_bank()
+                late_product(n, c, hidden, y[:, 0:STEP])
+                sums = keep.tile([P, STEP], F32, name=f"sums{n}", align_bytes=64)
+                nc.scalar.copy(out=sums[:], in_=y[:, 0:STEP])
+                scatter_weighted(n, c * STEP, STEP, sums)
+            else:
+                late_product(n, c, hidden, ys[n][:, STEP:HALF])
+                sums = keep.tile([P, HALF], F32, name=f"sums{n}", align_bytes=64)
+                nc.scalar.copy(out=sums[:], in_=ys[n][:])
+                scatter_weighted(n, HALF, HALF, sums)
             nc.sync.dma_start(out=out[n * P : (n + 1) * P, :], in_=windows[n][:])

@@ -23,10 +23,13 @@ TILES = N // P
 GROUP = 128
 HALF = 512
 STEP = 256
-CAST_ON_VECTOR = [0, 128, 32, 64]
+CAST_ON_VECTOR = [0, 128, 48, 80]
 ON_SCALAR = [0, 1, 1, 2]
 CHUNKS = S // STEP
-AHEAD = 2
+AHEAD = [0, 2, 2]
+SHORTCUT_AT = 2
+EARLY_BANKS = [0, 1, 2, 3]
+LATE_BANKS = [4, 5, 6, 7, 2, 3]
 KIB = 1024
 
 
@@ -38,8 +41,7 @@ def tile_list_masked_patch_block_kernel(
         keep = ctx.enter_context(tc.tile_pool(name="keep", bufs=1))
         ring = ctx.enter_context(tc.tile_pool(name="ring", bufs=3))
         shared = ctx.enter_context(tc.tile_pool(name="shared", bufs=1))
-        lower = ctx.enter_context(tc.psum_pool(name="lower", bufs=1))
-        upper = ctx.enter_context(tc.psum_pool(name="upper", bufs=1))
+        psum = ctx.enter_context(tc.psum_pool(name="psum", bufs=1))
 
         picks = keep.tile([P, S // 16], U16, name="picks")
         slots = keep.tile([P, S // 16], U16, name="slots")
@@ -54,16 +56,16 @@ def tile_list_masked_patch_block_kernel(
         windows = [keep.tile([P, T2], F32, name=f"window{n}", align_bytes=64) for n in range(TILES)]
         v_codes = [
             keep.tile([P, HALF], U32, name="v_codes0", align_bytes=64),
-            keep.tile([P, HALF], U32, name="v_codes1", align_bytes=64),
+            shared.tile([P, HALF], U32, name="v_codes1", offset=46 * KIB, align_bytes=64),
         ]
         v_scales = keep.tile([P, S], U8, name="v_scales", align_bytes=64)
         w1_codes = [keep.tile([P, P * PACK], U32, name=f"w1_codes{a}", align_bytes=64) for a in range(BLOCKS)]
         w1_scales = [keep.tile([P, P * PACK], U8, name=f"w1_scales{a}", align_bytes=64) for a in range(BLOCKS)]
 
         nc.vector.memset(table_scales[:], 0)
-        nc.vector.memset(out_scales[:], 0)
         for n in range(TILES):
             nc.vector.memset(windows[n][:], 0.0)
+        nc.vector.memset(out_scales[:], 0)
 
         def load_w1(a):
             cols = slice(a * P * PACK, (a + 1) * P * PACK)
@@ -89,7 +91,7 @@ def tile_list_masked_patch_block_kernel(
         nc.sync.dma_start(out=w2_codes[:].bitcast(I32), in_=w2_words.rearrange("a p c -> p a c").bitcast(I32))
         for q in range(4):
             rows = slice(32 * q, 32 * q + 4)
-            nc.sync.dma_start(out=out_scales[rows, BLOCKS, :], in_=ws_scales[0, 4 * q : 4 * q + 4, :].bitcast(I32))
+            nc.scalar.dma_start(out=out_scales[rows, BLOCKS, :], in_=ws_scales[0, 4 * q : 4 * q + 4, :].bitcast(I32))
         nc.sync.dma_start(out=ws_codes[:], in_=ws_words[0].rearrange("p c i -> p (c i)").bitcast(I32))
         nc.sync.dma_start(out=weight[:], in_=wgo)
         nc.sync.dma_start(slots[:], offs2)
@@ -126,21 +128,23 @@ def tile_list_masked_patch_block_kernel(
                 stop=True,
             )
 
-        turns = []
+        tenants = []
 
-        def upper_bank():
-            turns.append(len(turns))
-            return upper.tile([P, HALF], F32, name=f"upper{turns[-1]}", offset=turns[-1] % TILES * 2 * KIB)
+        def bank(k):
+            tenants.append(k)
+            return psum.tile([P, HALF], F32, name=f"bank{len(tenants)}", offset=k * 2 * KIB)
 
+        early_turns = []
         late_turns = []
 
-        def lower_bank():
-            late_turns.append(len(late_turns))
-            return lower.tile([P, HALF], F32, name=f"lower{late_turns[-1]}", offset=late_turns[-1] % TILES * 2 * KIB)
+        def next_bank(early):
+            turns, banks = (early_turns, EARLY_BANKS) if early else (late_turns, LATE_BANKS)
+            turns.append(banks[len(turns) % len(banks)])
+            return bank(turns[-1])
 
         def activate(a, first, count, act):
             for lo in range(0, count, GROUP):
-                x = upper_bank() if first == 0 else lower_bank()
+                x = next_bank(first == 0)
                 for t in range(PACK):
                     first_product(a, t, first + lo, GROUP, x[:, t * GROUP : (t + 1) * GROUP])
                 nc.scalar.activation(
@@ -153,7 +157,7 @@ def tile_list_masked_patch_block_kernel(
 
         def hidden_on_scalar(a, first, count, planes):
             for pair in range(2):
-                x = lower_bank()
+                x = next_bank(False)
                 for u in range(2):
                     first_product(a, 2 * pair + u, first, count, x[:, u * count : (u + 1) * count])
                 act = ring.tile([P, 2 * count], F32, name="act_planes", bufs=2, align_bytes=64)
@@ -167,9 +171,12 @@ def tile_list_masked_patch_block_kernel(
         def interleave(planes, rounded):
             nc.scalar.copy(out=rounded.rearrange("p (j t) -> p j t", t=PACK), in_=planes[:].rearrange("p t j -> p j t"))
 
-        def quantize_hidden(name, rounded, count):
+        def quantize_hidden(name, rounded, count, offset=None):
             codes = keep.tile([P, count], U32, name=f"h_codes{name}", align_bytes=64)
-            scales = keep.tile([P, count], U8, name=f"h_scales{name}", align_bytes=64)
+            if offset is None:
+                scales = keep.tile([P, count], U8, name=f"h_scales{name}", align_bytes=64)
+            else:
+                scales = shared.tile([P, count], U8, name=f"h_scales{name}", offset=offset, align_bytes=64)
             nc.vector.quantize_mx(out=codes[:].bitcast(FP8X4), scales=scales[:], in_=rounded)
             return codes, scales
 
@@ -205,21 +212,36 @@ def tile_list_masked_patch_block_kernel(
                 windows[n][:].indirect(places(first, count)), sums[:], weight[:, first : first + count], MULT
             )
 
-        def band_passes(n, a, hidden, base, dst):
-            for lo in range(0, STEP, GROUP):
-                start = a == 0 and lo == 0
-                stop = a == BLOCKS - 1 and lo + GROUP == STEP
-                cols = slice(base + lo, base + lo + GROUP)
-                second_pass(n, a, hidden, cols, dst[:, lo : lo + GROUP], start, stop)
-
-        def late_product(n, c, hidden, dst):
+        def accumulate(c, hidden, stripes):
             for a in range(BLOCKS):
-                if a == BLOCKS - 1:
-                    shortcut_pass(n, c * STEP, STEP, dst)
-                band_passes(n, a, hidden, a * STEP, dst)
+                for i, (n, dst) in enumerate(stripes):
+                    if a == SHORTCUT_AT:
+                        shortcut_pass(n, c * STEP, STEP, dst)
+                    for lo in range(0, STEP, GROUP):
+                        start = a == 0 and i == 0 and lo == 0
+                        stop = a == BLOCKS - 1 and i == len(stripes) - 1 and lo + GROUP == STEP
+                        second_pass(n, a, hidden[a], slice(lo, lo + GROUP), dst[:, lo : lo + GROUP], start, stop)
+
+        def second_product(c, hidden):
+            banks = [bank(k) for k in range(2)]
+            ys = [banks[n // 2][:, n % 2 * STEP : (n % 2 + 1) * STEP] for n in range(TILES)]
+            accumulate(c, hidden, [(0, ys[0]), (1, ys[1])])
+            accumulate(c, hidden, [(2, ys[2])])
+            return ys
+
+        def quantize_late(c, rounded):
+            hidden = []
+            for u in range(2):
+                width = 2 * STEP * PACK
+                offset = gate_offset(c) + KIB if u == 0 else None
+                half = rounded[:, u * width : (u + 1) * width]
+                codes, scales = quantize_hidden(f"late{c}_{u}", half, 2 * STEP, offset)
+                for k in range(2):
+                    hidden.append((codes[:, k * STEP : (k + 1) * STEP], scales[:, k * STEP : (k + 1) * STEP]))
+            return hidden
 
         def act_tile(c, a, place):
-            return shared.tile([P, STEP, PACK], F32, name=f"act{c}_{a}", offset=(8 + 4 * place) * KIB, align_bytes=64)
+            return shared.tile([P, STEP, PACK], F32, name=f"act{c}_{a}", offset=place * KIB, align_bytes=64)
 
         def gate_offset(c):
             return (40 + 2 * (c - 1)) * KIB
@@ -239,7 +261,7 @@ def tile_list_masked_patch_block_kernel(
         acts = {}
 
         def late_activate(c, a):
-            acts[c, a] = act_tile(c, a, [2, 0, 1][a] if c == 1 else 3 * c - 3 + a)
+            acts[c, a] = act_tile(c, a, [16, 8, 48][a] if c == 1 else 8 + 4 * (3 * c - 3 + a))
             activate(a, c * STEP, STEP, acts[c, a])
 
         def late_hidden(c):
@@ -262,7 +284,7 @@ def tile_list_masked_patch_block_kernel(
                     hidden_on_scalar(a, first, STEP, planes)
                     waiting.append((planes, dst))
             if c + 1 < CHUNKS:
-                for a in range(AHEAD):
+                for a in range(AHEAD[c]):
                     late_activate(c + 1, a)
             for planes, dst in waiting:
                 interleave(planes, dst)
@@ -271,7 +293,6 @@ def tile_list_masked_patch_block_kernel(
         nc.vector.tensor_copy(v_scales[:], table_scales[:].bitcast(U8).indirect(picks[:]))
         quantize_w1(0)
         gather_codes(0)
-        gather_codes(1)
         quantize_w1(1)
 
         last = BLOCKS - 1
@@ -281,46 +302,47 @@ def tile_list_masked_patch_block_kernel(
                 rounded = ring.tile([P, STEP * PACK], BF16, name="h_rounded", bufs=2, align_bytes=64)
             else:
                 rounded = shared.tile([P, STEP * PACK], BF16, name="h_rounded_last", offset=0, align_bytes=64)
-            act = act_tile(0, a, a % 2)
+            act = act_tile(0, a, [8, 12, 8, 46][a])
             activate(a, 0, STEP, act)
-            apply_gain(nc.vector, a, act[:], rounded[:])
+            width = STEP if a < last else GROUP
+            for lo in range(0, STEP, width):
+                apply_gain(nc.vector, a, act[:, lo : lo + width, :], rounded[:, lo * PACK : (lo + width) * PACK])
             hiddens.append(quantize_hidden(a, rounded[:], STEP))
             if a + 2 < BLOCKS:
                 quantize_w1(a + 2)
-        ys = [upper_bank() for n in range(TILES)]
-        for n in range(TILES):
-            for a in range(BLOCKS):
-                if a == last:
-                    shortcut_pass(n, 0, STEP, ys[n][:, 0:STEP])
-                band_passes(n, a, hiddens[a], 0, ys[n][:, 0:STEP])
+        gather_codes(1)
+        hidden = hiddens
+        ys = second_product(0, hidden)
 
         for c in range(1, CHUNKS):
             early = TILES - 1 if c < CHUNKS - 1 else TILES - 2
+            weighed = [weigh(c - 1, n, ys[n][:, 0:STEP], None) for n in range(early)]
             for n in range(early):
-                scatter_copy(c - 1, n, weigh(c - 1, n, ys[n][:, 0:STEP], None))
+                scatter_copy(c - 1, n, weighed[n])
             rounded = late_hidden(c)
             if c < CHUNKS - 1:
-                weighted = weigh(c - 1, early, ys[early][:, 0:STEP], c)
-                hidden = quantize_hidden(f"late{c}", rounded[:], BLOCKS * STEP)
+                accumulate(c - 1, hidden, [(last, ys[last])])
+                weighted = weigh(c - 1, early, ys[early], c)
+                hidden = quantize_late(c, rounded)
                 scatter_copy(c - 1, early, weighted)
-                ys = [upper_bank() for n in range(TILES)]
-                for n in range(TILES):
-                    late_product(n, c, hidden, ys[n][:, 0:STEP])
+                ys = second_product(c, hidden)
         c = CHUNKS - 1
-        hidden = quantize_hidden(f"late{c}", rounded[:], BLOCKS * STEP)
+        joint = next_bank(False)
+        accumulate(c - 1, hidden, [(last, joint[:, 0:STEP])])
+        hidden = quantize_late(c, rounded)
         sums = shared.tile([P, STEP], F32, name="sums_held", offset=gate_offset(c), align_bytes=64)
         nc.scalar.copy(out=sums[:], in_=ys[early][:, 0:STEP])
         scatter_weighted(early, (c - 1) * STEP, STEP, sums)
         for n in range(TILES):
             if n < last:
-                y = upper_bank()
-                late_product(n, c, hidden, y[:, 0:STEP])
+                y = next_bank(False)
+                accumulate(c, hidden, [(n, y[:, 0:STEP])])
                 sums = keep.tile([P, STEP], F32, name=f"sums{n}", align_bytes=64)
                 nc.scalar.copy(out=sums[:], in_=y[:, 0:STEP])
                 scatter_weighted(n, c * STEP, STEP, sums)
             else:
-                late_product(n, c, hidden, ys[n][:, STEP:HALF])
+                accumulate(c, hidden, [(n, joint[:, STEP:HALF])])
                 sums = keep.tile([P, HALF], F32, name=f"sums{n}", align_bytes=64)
-                nc.scalar.copy(out=sums[:], in_=ys[n][:])
+                nc.scalar.copy(out=sums[:], in_=joint[:])
                 scatter_weighted(n, HALF, HALF, sums)
             nc.sync.dma_start(out=out[n * P : (n + 1) * P, :], in_=windows[n][:])

@@ -106,8 +106,8 @@ def tile_list_masked_patch_block_kernel(
 
         def quantize_w1(a):
             rounded = ring.tile([P, P * PACK * PACK], BF16, name="w1_rounded", align_bytes=64)
-            dst = rounded[:].rearrange("p (t m j) -> p m t j", t=PACK, j=PACK)
-            src = raw[a][:].rearrange("p j (m t) -> p m t j", t=PACK)
+            dst = rounded[:].rearrange("p (t m j) -> p m j t", t=PACK, j=PACK)
+            src = raw[a][:].rearrange("p j (m t) -> p m j t", t=PACK)
             split = CAST_ON_VECTOR[a]
             if split > 0:
                 nc.vector.tensor_copy(out=dst[:, 0:split], in_=src[:, 0:split])

@@ -18,19 +18,31 @@ MULT = mybir.AluOpType.mult
 
 P = 128
 PACK = 4
-BLOCKS = H // (P * PACK)
-TILES = N // P
+BANDS = H // (P * PACK)
+STRIPES = N // P
+LAST = BANDS - 1
 GROUP = 128
 HALF = 512
 STEP = 256
-CAST_ON_VECTOR = [0, 128, 48, 80]
-ON_SCALAR = [0, 1, 1, 2]
 CHUNKS = S // STEP
-AHEAD = [0, 2, 2]
+LANES = 16
+KIB = 1024
+
+ROUNDED_BY_VECTOR = [0, 128, 48, 80]
+UNITS_ON_SCALAR = [0, 1, 1, 2]
+AHEAD = 2
 SHORTCUT_AT = 2
 EARLY_BANKS = [0, 1, 2, 3]
 LATE_BANKS = [4, 5, 6, 7, 2, 3]
-KIB = 1024
+
+ROUNDED_AT = 0
+FIRST_ACTS_AT = [8, 12, 8, 46]
+SECOND_GATHER_AT = 46
+SECOND_ACTS_AT = [16, 8, 48]
+LATER_ACTS_AT = 20
+LAST_WINDOW_AT = 52
+TABLE_SCALES_AT = 60
+GATES_AT = 40
 
 
 def tile_list_masked_patch_block_kernel(
@@ -43,28 +55,34 @@ def tile_list_masked_patch_block_kernel(
         shared = ctx.enter_context(tc.tile_pool(name="shared", bufs=1))
         psum = ctx.enter_context(tc.psum_pool(name="psum", bufs=1))
 
-        picks = keep.tile([P, S // 16], U16, name="picks")
-        slots = keep.tile([P, S // 16], U16, name="slots")
+        picks = keep.tile([P, S // LANES], U16, name="picks")
+        slots = keep.tile([P, S // LANES], U16, name="slots")
         table = keep.tile([P, T], I32, name="table", align_bytes=64)
-        table_scales = keep.tile([P, T // 4], I32, name="table_scales", align_bytes=64)
-        raw = [keep.tile([P, PACK, P * PACK], F32, name=f"raw{a}", align_bytes=64) for a in range(BLOCKS)]
-        gain = keep.tile([P, BLOCKS, 8], F32, name="gain")
-        w2_codes = keep.tile([P, BLOCKS, 2 * N], U8, name="w2_codes", align_bytes=64)
+        table_scales = shared.tile(
+            [P, T // 4], I32, name="table_scales", offset=TABLE_SCALES_AT * KIB, align_bytes=64
+        )
+        raw = [keep.tile([P, PACK, P * PACK], F32, name=f"raw{a}", align_bytes=64) for a in range(BANDS)]
+        gain = keep.tile([P, BANDS, 8], F32, name="gain")
+        w2_codes = keep.tile([P, BANDS, 2 * N], U8, name="w2_codes", align_bytes=64)
         ws_codes = keep.tile([P, N], I32, name="ws_codes", align_bytes=64)
-        out_scales = keep.tile([P, BLOCKS + 1, N // 4], I32, name="out_scales", align_bytes=64)
+        out_scales = keep.tile([P, BANDS + 1, N // 4], I32, name="out_scales", align_bytes=64)
         weight = keep.tile([P, S], F32, name="weight", align_bytes=64)
-        windows = [keep.tile([P, T2], F32, name=f"window{n}", align_bytes=64) for n in range(TILES)]
+        windows = [keep.tile([P, T2], F32, name=f"window{n}", align_bytes=64) for n in range(LAST)]
         v_codes = [
             keep.tile([P, HALF], U32, name="v_codes0", align_bytes=64),
-            shared.tile([P, HALF], U32, name="v_codes1", offset=46 * KIB, align_bytes=64),
+            shared.tile([P, HALF], U32, name="v_codes1", offset=SECOND_GATHER_AT * KIB, align_bytes=64),
         ]
         v_scales = keep.tile([P, S], U8, name="v_scales", align_bytes=64)
-        w1_codes = [keep.tile([P, P * PACK], U32, name=f"w1_codes{a}", align_bytes=64) for a in range(BLOCKS)]
-        w1_scales = [keep.tile([P, P * PACK], U8, name=f"w1_scales{a}", align_bytes=64) for a in range(BLOCKS)]
+        w1_codes = [keep.tile([P, P * PACK], U32, name=f"w1_codes{a}", align_bytes=64) for a in range(BANDS)]
+        w1_scales = [
+            shared.tile([P, P * PACK], U8, name="w1_scales0", offset=TABLE_SCALES_AT * KIB, align_bytes=64)
+        ]
+        for a in range(1, BANDS):
+            w1_scales.append(keep.tile([P, P * PACK], U8, name=f"w1_scales{a}", align_bytes=64))
 
         nc.vector.memset(table_scales[:], 0)
-        for n in range(TILES):
-            nc.vector.memset(windows[n][:], 0.0)
+        for n in range(LAST):
+            nc.vector.memset(windows[n][:].bitcast(I32), 0)
         nc.vector.memset(out_scales[:], 0)
 
         def load_w1(a):
@@ -80,24 +98,24 @@ def tile_list_masked_patch_block_kernel(
         nc.sync.dma_start(out=table[:], in_=tab_words[0].rearrange("p t i -> p (t i)").bitcast(I32))
         load_w1(1)
         nc.sync.dma_start(out=gain[:, :, 0:PACK], in_=ga.rearrange("(a p t) -> p a t", p=P, t=PACK))
-        for a in range(2, BLOCKS):
+        for a in range(2, BANDS):
             load_w1(a)
         for q in range(4):
             rows = slice(32 * q, 32 * q + 4)
             nc.sync.dma_start(
-                out=out_scales[rows, 0:BLOCKS, :],
+                out=out_scales[rows, 0:BANDS, :],
                 in_=w2_scales[:, 4 * q : 4 * q + 4, :].rearrange("a q c -> q a c").bitcast(I32),
             )
         nc.sync.dma_start(out=w2_codes[:].bitcast(I32), in_=w2_words.rearrange("a p c -> p a c").bitcast(I32))
         for q in range(4):
             rows = slice(32 * q, 32 * q + 4)
-            nc.scalar.dma_start(out=out_scales[rows, BLOCKS, :], in_=ws_scales[0, 4 * q : 4 * q + 4, :].bitcast(I32))
+            nc.scalar.dma_start(out=out_scales[rows, BANDS, :], in_=ws_scales[0, 4 * q : 4 * q + 4, :].bitcast(I32))
         nc.sync.dma_start(out=ws_codes[:], in_=ws_words[0].rearrange("p c i -> p (c i)").bitcast(I32))
         nc.sync.dma_start(out=weight[:], in_=wgo)
         nc.sync.dma_start(slots[:], offs2)
 
         def gather_codes(i):
-            cols = slice(i * HALF // 16, (i + 1) * HALF // 16)
+            cols = slice(i * HALF // LANES, (i + 1) * HALF // LANES)
             nc.vector.tensor_copy(v_codes[i][:], table[:].bitcast(U32).indirect(picks[:, cols]))
 
         def patch(first, count):
@@ -108,7 +126,7 @@ def tile_list_masked_patch_block_kernel(
             rounded = ring.tile([P, P * PACK * PACK], BF16, name="w1_rounded", align_bytes=64)
             dst = rounded[:].rearrange("p (t m j) -> p m j t", t=PACK, j=PACK)
             src = raw[a][:].rearrange("p j (m t) -> p m j t", t=PACK)
-            split = CAST_ON_VECTOR[a]
+            split = ROUNDED_BY_VECTOR[a]
             if split > 0:
                 nc.vector.tensor_copy(out=dst[:, 0:split], in_=src[:, 0:split])
             if split < P:
@@ -142,11 +160,11 @@ def tile_list_masked_patch_block_kernel(
             turns.append(banks[len(turns) % len(banks)])
             return bank(turns[-1])
 
-        def activate(a, first, count, act):
-            for lo in range(0, count, GROUP):
-                x = next_bank(first == 0)
+        def activate(a, c, act):
+            for lo in range(0, STEP, GROUP):
+                x = next_bank(c == 0)
                 for t in range(PACK):
-                    first_product(a, t, first + lo, GROUP, x[:, t * GROUP : (t + 1) * GROUP])
+                    first_product(a, t, c * STEP + lo, GROUP, x[:, t * GROUP : (t + 1) * GROUP])
                 nc.scalar.activation(
                     act[:, lo : lo + GROUP, :], x[:].rearrange("p (t j) -> p j t", t=PACK), ACT.Gelu_apprx_sigmoid
                 )
@@ -155,17 +173,21 @@ def tile_list_masked_patch_block_kernel(
             gains = gain[:, a, 0:PACK].unsqueeze(1).to_broadcast(list(act.shape))
             engine.tensor_tensor(rounded.rearrange("p (j t) -> p j t", t=PACK), act, gains, MULT)
 
-        def hidden_on_scalar(a, first, count, planes):
+        def apply_gain_to_pair(pair, rounded):
+            gains = gain[:, 0:2, 0:PACK].unsqueeze(2).to_broadcast([P, 2, STEP, PACK])
+            nc.gpsimd.tensor_tensor(rounded.rearrange("p (a j t) -> p a j t", a=2, t=PACK), pair, gains, MULT)
+
+        def hidden_on_scalar(a, c, planes):
             for pair in range(2):
                 x = next_bank(False)
                 for u in range(2):
-                    first_product(a, 2 * pair + u, first, count, x[:, u * count : (u + 1) * count])
-                act = ring.tile([P, 2 * count], F32, name="act_planes", bufs=2, align_bytes=64)
+                    first_product(a, 2 * pair + u, c * STEP, STEP, x[:, u * STEP : (u + 1) * STEP])
+                act = ring.tile([P, 2 * STEP], F32, name="act_planes", bufs=2, align_bytes=64)
                 nc.scalar.activation(act[:], x[:], ACT.Gelu_apprx_sigmoid)
                 for u in range(2):
                     t = 2 * pair + u
                     nc.scalar.activation(
-                        planes[:, t, :], act[:, u * count : (u + 1) * count], ACT.Copy, scale=gain[:, a, t : t + 1]
+                        planes[:, t, :], act[:, u * STEP : (u + 1) * STEP], ACT.Copy, scale=gain[:, a, t : t + 1]
                     )
 
         def interleave(planes, rounded):
@@ -180,60 +202,62 @@ def tile_list_masked_patch_block_kernel(
             nc.vector.quantize_mx(out=codes[:].bitcast(FP8X4), scales=scales[:], in_=rounded)
             return codes, scales
 
-        def shortcut_pass(n, first, count, dst):
-            codes, scales = patch(first, count)
+        def shortcut_pass(n, c, dst, start):
+            codes, scales = patch(c * STEP, STEP)
             nc.tensor.matmul_mx(
                 out=dst,
                 lhsT=ws_codes[:, n * P : (n + 1) * P].bitcast(FP8X4),
-                lhsT_scale=out_scales[:, BLOCKS, :].bitcast(U8)[:, n * P : (n + 1) * P],
+                lhsT_scale=out_scales[:, BANDS, :].bitcast(U8)[:, n * P : (n + 1) * P],
                 rhs=codes,
                 rhs_scale=scales,
-                start=False,
+                start=start,
                 stop=False,
             )
 
-        def second_pass(n, a, hidden, cols, dst, start, stop):
-            codes, scales = hidden
-            nc.tensor.matmul_mx(
-                out=dst,
-                lhsT=w2_codes[:, a, 2 * n * P : 2 * (n + 1) * P].bitcast(FP4X4),
-                lhsT_scale=out_scales[:, a, :].bitcast(U8)[:, n * P : (n + 1) * P],
-                rhs=codes[:, cols].bitcast(FP8X4),
-                rhs_scale=scales[:, cols],
-                start=start,
-                stop=stop,
-            )
-
-        def places(first, count):
-            return slots[:, first // 16 : (first + count) // 16]
-
-        def scatter_weighted(n, first, count, sums):
-            nc.vector.tensor_tensor(
-                windows[n][:].indirect(places(first, count)), sums[:], weight[:, first : first + count], MULT
-            )
+        def band_passes(n, a, hidden, dst, opens, closes):
+            codes, scales = hidden[a]
+            for lo in range(0, STEP, GROUP):
+                nc.tensor.matmul_mx(
+                    out=dst[:, lo : lo + GROUP],
+                    lhsT=w2_codes[:, a, 2 * n * P : 2 * (n + 1) * P].bitcast(FP4X4),
+                    lhsT_scale=out_scales[:, a, :].bitcast(U8)[:, n * P : (n + 1) * P],
+                    rhs=codes[:, lo : lo + GROUP].bitcast(FP8X4),
+                    rhs_scale=scales[:, lo : lo + GROUP],
+                    start=opens and lo == 0,
+                    stop=closes and lo + GROUP == STEP,
+                )
 
         def accumulate(c, hidden, stripes):
-            for a in range(BLOCKS):
+            for a in range(BANDS):
                 for i, (n, dst) in enumerate(stripes):
                     if a == SHORTCUT_AT:
-                        shortcut_pass(n, c * STEP, STEP, dst)
-                    for lo in range(0, STEP, GROUP):
-                        start = a == 0 and i == 0 and lo == 0
-                        stop = a == BLOCKS - 1 and i == len(stripes) - 1 and lo + GROUP == STEP
-                        second_pass(n, a, hidden[a], slice(lo, lo + GROUP), dst[:, lo : lo + GROUP], start, stop)
+                        shortcut_pass(n, c, dst, False)
+                    band_passes(n, a, hidden, dst, a == 0 and i == 0, a == LAST and i == len(stripes) - 1)
+
+        def accumulate_behind_quantise(c, hidden, stripes):
+            for i, (n, dst) in enumerate(stripes):
+                shortcut_pass(n, c, dst, i == 0)
+            bands = [0, 1, 2, 3] if stripes[0][0] == 0 else [2, 3, 0, 1]
+            for a in bands:
+                for i, (n, dst) in enumerate(stripes):
+                    band_passes(n, a, hidden, dst, False, a == bands[-1] and i == len(stripes) - 1)
 
         def second_product(c, hidden):
             banks = [bank(k) for k in range(2)]
-            ys = [banks[n // 2][:, n % 2 * STEP : (n % 2 + 1) * STEP] for n in range(TILES)]
-            accumulate(c, hidden, [(0, ys[0]), (1, ys[1])])
-            accumulate(c, hidden, [(2, ys[2])])
+            ys = [banks[n // 2][:, n % 2 * STEP : (n % 2 + 1) * STEP] for n in range(STRIPES)]
+            add_up = accumulate if c == 0 else accumulate_behind_quantise
+            add_up(c, hidden, [(0, ys[0]), (1, ys[1])])
+            add_up(c, hidden, [(2, ys[2])])
             return ys
+
+        def gate(c):
+            return (GATES_AT + 2 * (c - 1)) * KIB
 
         def quantize_late(c, rounded):
             hidden = []
             for u in range(2):
                 width = 2 * STEP * PACK
-                offset = gate_offset(c) + KIB if u == 0 else None
+                offset = gate(c) + KIB if u == 0 else None
                 half = rounded[:, u * width : (u + 1) * width]
                 codes, scales = quantize_hidden(f"late{c}_{u}", half, 2 * STEP, offset)
                 for k in range(2):
@@ -243,14 +267,13 @@ def tile_list_masked_patch_block_kernel(
         def act_tile(c, a, place):
             return shared.tile([P, STEP, PACK], F32, name=f"act{c}_{a}", offset=place * KIB, align_bytes=64)
 
-        def gate_offset(c):
-            return (40 + 2 * (c - 1)) * KIB
+        def places(first, count):
+            return slots[:, first // LANES : (first + count) // LANES]
 
-        def weigh(c, n, y, gate):
-            if gate is None:
+        def weigh(c, y, offset=None):
+            if offset is None:
                 weighted = ring.tile([P, STEP], F32, name="weighted", bufs=3, align_bytes=64)
             else:
-                offset = gate_offset(gate)
                 weighted = shared.tile([P, STEP], F32, name=f"weighted{c}", offset=offset, align_bytes=64)
             nc.vector.tensor_tensor(weighted[:], y, weight[:, c * STEP : (c + 1) * STEP], MULT)
             return weighted
@@ -258,33 +281,50 @@ def tile_list_masked_patch_block_kernel(
         def scatter_copy(c, n, weighted):
             nc.vector.tensor_copy(windows[n][:].indirect(places(c * STEP, STEP)), weighted[:])
 
+        def scatter_weighted(n, first, count, sums):
+            nc.vector.tensor_tensor(
+                windows[n][:].indirect(places(first, count)), sums[:], weight[:, first : first + count], MULT
+            )
+
         acts = {}
+        pairs = {}
 
         def late_activate(c, a):
-            acts[c, a] = act_tile(c, a, [16, 8, 48][a] if c == 1 else 8 + 4 * (3 * c - 3 + a))
-            activate(a, c * STEP, STEP, acts[c, a])
+            place = SECOND_ACTS_AT[a] if c == 1 else LATER_ACTS_AT + 4 * (3 * (c - 2) + a)
+            if c > 1 and a < 2:
+                if a == 0:
+                    pairs[c] = shared.tile(
+                        [P, 2, STEP, PACK], F32, name=f"act_pair{c}", offset=place * KIB, align_bytes=64
+                    )
+                acts[c, a] = pairs[c][:, a]
+            else:
+                acts[c, a] = act_tile(c, a, place)
+            activate(a, c, acts[c, a])
 
         def late_hidden(c):
-            first = c * STEP
-            rounded = shared.tile([P, BLOCKS * STEP * PACK], BF16, name=f"late_rounded{c}", offset=0, align_bytes=64)
-            count = ON_SCALAR[c]
+            unit = STEP * PACK
+            rounded = shared.tile(
+                [P, BANDS * unit], BF16, name=f"late_rounded{c}", offset=ROUNDED_AT * KIB, align_bytes=64
+            )
             waiting = []
-            for a in range(BLOCKS):
-                dst = rounded[:, a * STEP * PACK : (a + 1) * STEP * PACK]
-                if a < BLOCKS - count:
+            for a in range(BANDS):
+                dst = rounded[:, a * unit : (a + 1) * unit]
+                if a < BANDS - UNITS_ON_SCALAR[c]:
                     if (c, a) not in acts:
                         late_activate(c, a)
-                    apply_gain(nc.gpsimd, a, acts[c, a][:], dst)
+                    if c == 1 or a > 1:
+                        apply_gain(nc.gpsimd, a, acts[c, a][:], dst)
+                    elif a == 1:
+                        apply_gain_to_pair(pairs[c][:], rounded[:, 0 : 2 * unit])
                 else:
-                    if a == last:
-                        offset = gate_offset(c)
-                        planes = shared.tile([P, PACK, STEP], BF16, name=f"planes{c}", offset=offset, align_bytes=64)
+                    if a == LAST:
+                        planes = shared.tile([P, PACK, STEP], BF16, name=f"planes{c}", offset=gate(c), align_bytes=64)
                     else:
                         planes = ring.tile([P, PACK, STEP], BF16, name="planes", bufs=2, align_bytes=64)
-                    hidden_on_scalar(a, first, STEP, planes)
+                    hidden_on_scalar(a, c, planes)
                     waiting.append((planes, dst))
             if c + 1 < CHUNKS:
-                for a in range(AHEAD[c]):
+                for a in range(AHEAD):
                     late_activate(c + 1, a)
             for planes, dst in waiting:
                 interleave(planes, dst)
@@ -292,57 +332,63 @@ def tile_list_masked_patch_block_kernel(
 
         nc.vector.tensor_copy(v_scales[:], table_scales[:].bitcast(U8).indirect(picks[:]))
         quantize_w1(0)
+        warm = shared.tile([P, 1], F32, name="warm", offset=LAST_WINDOW_AT * KIB)
+        nc.scalar.activation(warm[:], windows[LAST - 1][:, 0:1], ACT.Gelu_apprx_sigmoid)
+        windows.append(shared.tile([P, T2], F32, name="window_last", offset=LAST_WINDOW_AT * KIB, align_bytes=64))
+        nc.gpsimd.memset(windows[LAST][:].bitcast(I32), 0)
         gather_codes(0)
         quantize_w1(1)
 
-        last = BLOCKS - 1
-        hiddens = []
-        for a in range(BLOCKS):
-            if a < last:
+        hidden = []
+        for a in range(BANDS):
+            if a < LAST:
                 rounded = ring.tile([P, STEP * PACK], BF16, name="h_rounded", bufs=2, align_bytes=64)
             else:
-                rounded = shared.tile([P, STEP * PACK], BF16, name="h_rounded_last", offset=0, align_bytes=64)
-            act = act_tile(0, a, [8, 12, 8, 46][a])
-            activate(a, 0, STEP, act)
-            width = STEP if a < last else GROUP
+                rounded = shared.tile(
+                    [P, STEP * PACK], BF16, name="h_rounded_last", offset=ROUNDED_AT * KIB, align_bytes=64
+                )
+            act = act_tile(0, a, FIRST_ACTS_AT[a])
+            activate(a, 0, act)
+            width = STEP if a < LAST else GROUP
             for lo in range(0, STEP, width):
                 apply_gain(nc.vector, a, act[:, lo : lo + width, :], rounded[:, lo * PACK : (lo + width) * PACK])
-            hiddens.append(quantize_hidden(a, rounded[:], STEP))
-            if a + 2 < BLOCKS:
+            hidden.append(quantize_hidden(a, rounded[:], STEP))
+            if a + 2 < BANDS:
                 quantize_w1(a + 2)
         gather_codes(1)
-        hidden = hiddens
         ys = second_product(0, hidden)
 
         for c in range(1, CHUNKS):
-            early = TILES - 1 if c < CHUNKS - 1 else TILES - 2
-            weighed = [weigh(c - 1, n, ys[n][:, 0:STEP], None) for n in range(early)]
+            early = STRIPES - 1 if c < CHUNKS - 1 else STRIPES - 2
+            weighed = [weigh(c - 1, ys[n]) for n in range(early)]
             for n in range(early):
                 scatter_copy(c - 1, n, weighed[n])
             rounded = late_hidden(c)
             if c < CHUNKS - 1:
-                accumulate(c - 1, hidden, [(last, ys[last])])
-                weighted = weigh(c - 1, early, ys[early], c)
+                accumulate(c - 1, hidden, [(LAST, ys[LAST])])
+                weighted = weigh(c - 1, ys[LAST], gate(c))
                 hidden = quantize_late(c, rounded)
-                scatter_copy(c - 1, early, weighted)
+                scatter_copy(c - 1, LAST, weighted)
                 ys = second_product(c, hidden)
+
         c = CHUNKS - 1
+        held = STRIPES - 2
         joint = next_bank(False)
-        accumulate(c - 1, hidden, [(last, joint[:, 0:STEP])])
+        accumulate(c - 1, hidden, [(LAST, joint[:, 0:STEP])])
         hidden = quantize_late(c, rounded)
-        sums = shared.tile([P, STEP], F32, name="sums_held", offset=gate_offset(c), align_bytes=64)
-        nc.scalar.copy(out=sums[:], in_=ys[early][:, 0:STEP])
-        scatter_weighted(early, (c - 1) * STEP, STEP, sums)
-        for n in range(TILES):
-            if n < last:
+        sums = shared.tile([P, STEP], F32, name="sums_held", offset=gate(c), align_bytes=64)
+        nc.scalar.copy(out=sums[:], in_=ys[held])
+        scatter_weighted(held, (c - 1) * STEP, STEP, sums)
+        for n in range(STRIPES):
+            if n < LAST:
                 y = next_bank(False)
-                accumulate(c, hidden, [(n, y[:, 0:STEP])])
+                accumulate_behind_quantise(c, hidden, [(n, y[:, 0:STEP])])
                 sums = keep.tile([P, STEP], F32, name=f"sums{n}", align_bytes=64)
                 nc.scalar.copy(out=sums[:], in_=y[:, 0:STEP])
                 scatter_weighted(n, c * STEP, STEP, sums)
             else:
-                accumulate(c, hidden, [(n, joint[:, STEP:HALF])])
+                accumulate_behind_quantise(c, hidden, [(n, joint[:, STEP:HALF])])
                 sums = keep.tile([P, HALF], F32, name=f"sums{n}", align_bytes=64)
                 nc.scalar.copy(out=sums[:], in_=joint[:])
-                scatter_weighted(n, HALF, HALF, sums)
+                scatter_weighted(n, (c - 1) * STEP, HALF, sums)
             nc.sync.dma_start(out=out[n * P : (n + 1) * P, :], in_=windows[n][:])

@@ -1,6 +1,7 @@
 from contextlib import ExitStack
 
 import concourse.mybir as mybir
+from concourse.masks import make_identity
 
 K, H, N, T, S, T2 = 512, 2048, 512, 4096, 1024, 2048
 FLOPS = 2 * S * (K * H + H * N + K * N)
@@ -28,21 +29,23 @@ CHUNKS = S // STEP
 LANES = 16
 KIB = 1024
 
-ROUNDED_BY_VECTOR = [0, 128, 48, 80]
+ROUNDED_BY_VECTOR = [0, 128, 72]
+LAST_ROUNDED_BY_VECTOR = [0, 128]
 UNITS_ON_SCALAR = [0, 1, 1, 2]
 AHEAD = 2
 SHORTCUT_AT = 2
-EARLY_BANKS = [0, 1, 2, 3]
-LATE_BANKS = [4, 5, 6, 7, 2, 3]
+TURN_BANKS = [0, 1, 3, 4, 5, 6, 7]
+LAST_BANK = 2
 
 ROUNDED_AT = 0
 FIRST_ACTS_AT = [8, 12, 8, 46]
-SECOND_GATHER_AT = 46
-SECOND_ACTS_AT = [16, 8, 48]
+SECOND_ACTS_AT = [32, 12]
+LAST_W1_AT = 66
 LATER_ACTS_AT = 20
 LAST_WINDOW_AT = 52
 TABLE_SCALES_AT = 60
-GATES_AT = 40
+SECOND_RAW_AT = 79
+GATES_AT = 70
 
 
 def tile_list_masked_patch_block_kernel(
@@ -61,16 +64,24 @@ def tile_list_masked_patch_block_kernel(
         table_scales = shared.tile(
             [P, T // 4], I32, name="table_scales", offset=TABLE_SCALES_AT * KIB, align_bytes=64
         )
-        raw = [keep.tile([P, PACK, P * PACK], F32, name=f"raw{a}", align_bytes=64) for a in range(BANDS)]
-        gain = keep.tile([P, BANDS, 8], F32, name="gain")
+        raw = [keep.tile([P, PACK, P * PACK], F32, name=f"raw{a}", align_bytes=64) for a in range(LAST) if a != 1]
+        raw.insert(1, shared.tile([P, PACK, P * PACK], F32, name="raw1", offset=SECOND_RAW_AT * KIB, align_bytes=64))
+        raw_last = [
+            shared.tile([P, 2, P * PACK], F32, name="raw_last0", offset=FIRST_ACTS_AT[1] * KIB, align_bytes=64),
+            keep.tile([P, 2, P * PACK], F32, name="raw_last1", align_bytes=64),
+        ]
+        gain_rows = keep.tile([P, P * PACK], F32, name="gain_rows", align_bytes=64)
+        identity = keep.tile([P, P], F32, name="identity", align_bytes=64)
+        gain = shared.tile([P, BANDS, PACK], F32, name="gain", offset=(TABLE_SCALES_AT + 1) * KIB)
         w2_codes = keep.tile([P, BANDS, 2 * N], U8, name="w2_codes", align_bytes=64)
         ws_codes = keep.tile([P, N], I32, name="ws_codes", align_bytes=64)
-        out_scales = keep.tile([P, BANDS + 1, N // 4], I32, name="out_scales", align_bytes=64)
+        w2_planes = keep.tile([P, BANDS, N // 4], I32, name="w2_planes", align_bytes=64)
+        ws_plane = shared.tile([P, N // 4], I32, name="ws_plane", offset=(TABLE_SCALES_AT + 2) * KIB, align_bytes=64)
         weight = keep.tile([P, S], F32, name="weight", align_bytes=64)
         windows = [keep.tile([P, T2], F32, name=f"window{n}", align_bytes=64) for n in range(LAST)]
         v_codes = [
             keep.tile([P, HALF], U32, name="v_codes0", align_bytes=64),
-            shared.tile([P, HALF], U32, name="v_codes1", offset=SECOND_GATHER_AT * KIB, align_bytes=64),
+            keep.tile([P, HALF], U32, name="v_codes1", align_bytes=64),
         ]
         v_scales = keep.tile([P, S], U8, name="v_scales", align_bytes=64)
         w1_codes = [keep.tile([P, P * PACK], U32, name=f"w1_codes{a}", align_bytes=64) for a in range(BANDS)]
@@ -81,9 +92,11 @@ def tile_list_masked_patch_block_kernel(
             w1_scales.append(keep.tile([P, P * PACK], U8, name=f"w1_scales{a}", align_bytes=64))
 
         nc.vector.memset(table_scales[:], 0)
+        nc.vector.memset(gain_rows[:], 0.0)
         for n in range(LAST):
             nc.vector.memset(windows[n][:].bitcast(I32), 0)
-        nc.vector.memset(out_scales[:], 0)
+        nc.vector.memset(w2_planes[:], 0)
+        make_identity(nc, identity[:])
 
         def load_w1(a):
             cols = slice(a * P * PACK, (a + 1) * P * PACK)
@@ -91,25 +104,24 @@ def tile_list_masked_patch_block_kernel(
 
         nc.sync.dma_start(picks[:], offs)
         load_w1(0)
+        nc.sync.dma_start(out=gain_rows[0:BANDS, :], in_=ga.rearrange("(a c) -> a c", a=BANDS))
         for q in range(4):
             nc.sync.dma_start(
                 out=table_scales[32 * q : 32 * q + 4, :], in_=tab_scales[0, 4 * q : 4 * q + 4, :].bitcast(I32)
             )
         nc.sync.dma_start(out=table[:], in_=tab_words[0].rearrange("p t i -> p (t i)").bitcast(I32))
         load_w1(1)
-        nc.sync.dma_start(out=gain[:, :, 0:PACK], in_=ga.rearrange("(a p t) -> p a t", p=P, t=PACK))
-        for a in range(2, BANDS):
-            load_w1(a)
+        load_w1(2)
+        last_rows = w1[:, LAST * P * PACK :].rearrange("(p j) c -> p j c", j=PACK)
+        for u in range(2):
+            nc.sync.dma_start(out=raw_last[u][:], in_=last_rows[:, 2 * u : 2 * u + 2, :])
         for q in range(4):
             rows = slice(32 * q, 32 * q + 4)
             nc.sync.dma_start(
-                out=out_scales[rows, 0:BANDS, :],
+                out=w2_planes[rows],
                 in_=w2_scales[:, 4 * q : 4 * q + 4, :].rearrange("a q c -> q a c").bitcast(I32),
             )
         nc.sync.dma_start(out=w2_codes[:].bitcast(I32), in_=w2_words.rearrange("a p c -> p a c").bitcast(I32))
-        for q in range(4):
-            rows = slice(32 * q, 32 * q + 4)
-            nc.scalar.dma_start(out=out_scales[rows, BANDS, :], in_=ws_scales[0, 4 * q : 4 * q + 4, :].bitcast(I32))
         nc.sync.dma_start(out=ws_codes[:], in_=ws_words[0].rearrange("p c i -> p (c i)").bitcast(I32))
         nc.sync.dma_start(out=weight[:], in_=wgo)
         nc.sync.dma_start(slots[:], offs2)
@@ -123,7 +135,12 @@ def tile_list_masked_patch_block_kernel(
             return v_codes[i][:, lo : lo + count].bitcast(FP8X4), v_scales[:, first : first + count]
 
         def quantize_w1(a):
-            rounded = ring.tile([P, P * PACK * PACK], BF16, name="w1_rounded", align_bytes=64)
+            if a == 0:
+                rounded = shared.tile(
+                    [P, P * PACK * PACK], BF16, name="w1_first", offset=LAST_WINDOW_AT * KIB, align_bytes=64
+                )
+            else:
+                rounded = ring.tile([P, P * PACK * PACK], BF16, name="w1_rounded", bufs=2, align_bytes=64)
             dst = rounded[:].rearrange("p (t m j) -> p m j t", t=PACK, j=PACK)
             src = raw[a][:].rearrange("p j (m t) -> p m j t", t=PACK)
             split = ROUNDED_BY_VECTOR[a]
@@ -132,6 +149,18 @@ def tile_list_masked_patch_block_kernel(
             if split < P:
                 nc.scalar.copy(out=dst[:, split:P], in_=src[:, split:P])
             nc.vector.quantize_mx(out=w1_codes[a][:].bitcast(FP8X4), scales=w1_scales[a][:], in_=rounded[:])
+
+        def quantize_last_w1():
+            rounded = shared.tile([P, P * PACK * PACK], BF16, name="w1_last", offset=LAST_W1_AT * KIB, align_bytes=64)
+            dst = rounded[:].rearrange("p (t m j) -> p m j t", t=PACK, j=PACK)
+            for u in range(2):
+                src = raw_last[u][:].rearrange("p j (m t) -> p m j t", t=PACK)
+                split = LAST_ROUNDED_BY_VECTOR[u]
+                if split > 0:
+                    nc.vector.tensor_copy(out=dst[:, 0:split, 2 * u : 2 * u + 2], in_=src[:, 0:split])
+                if split < P:
+                    nc.scalar.copy(out=dst[:, split:P, 2 * u : 2 * u + 2], in_=src[:, split:P])
+            nc.vector.quantize_mx(out=w1_codes[LAST][:].bitcast(FP8X4), scales=w1_scales[LAST][:], in_=rounded[:])
 
         def first_product(a, t, first, count, dst):
             codes, scales = patch(first, count)
@@ -152,34 +181,32 @@ def tile_list_masked_patch_block_kernel(
             tenants.append(k)
             return psum.tile([P, HALF], F32, name=f"bank{len(tenants)}", offset=k * 2 * KIB)
 
-        early_turns = []
-        late_turns = []
+        turns = []
 
-        def next_bank(early):
-            turns, banks = (early_turns, EARLY_BANKS) if early else (late_turns, LATE_BANKS)
-            turns.append(banks[len(turns) % len(banks)])
+        def next_bank():
+            turns.append(TURN_BANKS[len(turns) % len(TURN_BANKS)])
             return bank(turns[-1])
 
         def activate(a, c, act):
             for lo in range(0, STEP, GROUP):
-                x = next_bank(c == 0)
+                x = next_bank()
                 for t in range(PACK):
                     first_product(a, t, c * STEP + lo, GROUP, x[:, t * GROUP : (t + 1) * GROUP])
                 nc.scalar.activation(
                     act[:, lo : lo + GROUP, :], x[:].rearrange("p (t j) -> p j t", t=PACK), ACT.Gelu_apprx_sigmoid
                 )
 
-        def apply_gain(engine, a, act, rounded):
-            gains = gain[:, a, 0:PACK].unsqueeze(1).to_broadcast(list(act.shape))
+        def apply_gain(engine, gains, act, rounded):
+            gains = gains.unsqueeze(1).to_broadcast(list(act.shape))
             engine.tensor_tensor(rounded.rearrange("p (j t) -> p j t", t=PACK), act, gains, MULT)
 
-        def apply_gain_to_pair(pair, rounded):
-            gains = gain[:, 0:2, 0:PACK].unsqueeze(2).to_broadcast([P, 2, STEP, PACK])
+        def apply_gain_to_pair(a, pair, rounded):
+            gains = gain[:, a : a + 2, :].unsqueeze(2).to_broadcast([P, 2, STEP, PACK])
             nc.gpsimd.tensor_tensor(rounded.rearrange("p (a j t) -> p a j t", a=2, t=PACK), pair, gains, MULT)
 
         def hidden_on_scalar(a, c, planes):
             for pair in range(2):
-                x = next_bank(False)
+                x = next_bank()
                 for u in range(2):
                     first_product(a, 2 * pair + u, c * STEP, STEP, x[:, u * STEP : (u + 1) * STEP])
                 act = ring.tile([P, 2 * STEP], F32, name="act_planes", bufs=2, align_bytes=64)
@@ -200,14 +227,14 @@ def tile_list_masked_patch_block_kernel(
             else:
                 scales = shared.tile([P, count], U8, name=f"h_scales{name}", offset=offset, align_bytes=64)
             nc.vector.quantize_mx(out=codes[:].bitcast(FP8X4), scales=scales[:], in_=rounded)
-            return codes, scales
+            return [(codes[:, lo : lo + GROUP], scales[:, lo : lo + GROUP]) for lo in range(0, count, GROUP)]
 
         def shortcut_pass(n, c, dst, start):
             codes, scales = patch(c * STEP, STEP)
             nc.tensor.matmul_mx(
                 out=dst,
                 lhsT=ws_codes[:, n * P : (n + 1) * P].bitcast(FP8X4),
-                lhsT_scale=out_scales[:, BANDS, :].bitcast(U8)[:, n * P : (n + 1) * P],
+                lhsT_scale=ws_plane[:].bitcast(U8)[:, n * P : (n + 1) * P],
                 rhs=codes,
                 rhs_scale=scales,
                 start=start,
@@ -215,53 +242,48 @@ def tile_list_masked_patch_block_kernel(
             )
 
         def band_passes(n, a, hidden, dst, opens, closes):
-            codes, scales = hidden[a]
             for lo in range(0, STEP, GROUP):
+                codes, scales = hidden[a][lo // GROUP]
                 nc.tensor.matmul_mx(
                     out=dst[:, lo : lo + GROUP],
                     lhsT=w2_codes[:, a, 2 * n * P : 2 * (n + 1) * P].bitcast(FP4X4),
-                    lhsT_scale=out_scales[:, a, :].bitcast(U8)[:, n * P : (n + 1) * P],
-                    rhs=codes[:, lo : lo + GROUP].bitcast(FP8X4),
-                    rhs_scale=scales[:, lo : lo + GROUP],
+                    lhsT_scale=w2_planes[:, a, :].bitcast(U8)[:, n * P : (n + 1) * P],
+                    rhs=codes.bitcast(FP8X4),
+                    rhs_scale=scales,
                     start=opens and lo == 0,
                     stop=closes and lo + GROUP == STEP,
                 )
 
-        def accumulate(c, hidden, stripes):
-            for a in range(BANDS):
-                for i, (n, dst) in enumerate(stripes):
-                    if a == SHORTCUT_AT:
-                        shortcut_pass(n, c, dst, False)
-                    band_passes(n, a, hidden, dst, a == 0 and i == 0, a == LAST and i == len(stripes) - 1)
+        def accumulate(c, hidden, groups, turn=0):
+            bands = [(turn + i) % BANDS for i in range(BANDS)]
+            steps = [bands[0], None] + bands[1:] if c == 0 else [None] + bands
+            for a in steps:
+                for stripes in groups:
+                    for i, (n, dst) in enumerate(stripes):
+                        opens = a == steps[0] and i == 0
+                        if a is None:
+                            shortcut_pass(n, c, dst, opens)
+                        else:
+                            band_passes(n, a, hidden, dst, opens, a == steps[-1] and i == len(stripes) - 1)
 
-        def accumulate_behind_quantise(c, hidden, stripes):
-            for i, (n, dst) in enumerate(stripes):
-                shortcut_pass(n, c, dst, i == 0)
-            bands = [0, 1, 2, 3] if stripes[0][0] == 0 else [2, 3, 0, 1]
-            for a in bands:
-                for i, (n, dst) in enumerate(stripes):
-                    band_passes(n, a, hidden, dst, False, a == bands[-1] and i == len(stripes) - 1)
-
-        def second_product(c, hidden):
-            banks = [bank(k) for k in range(2)]
-            ys = [banks[n // 2][:, n % 2 * STEP : (n % 2 + 1) * STEP] for n in range(STRIPES)]
-            add_up = accumulate if c == 0 else accumulate_behind_quantise
-            add_up(c, hidden, [(0, ys[0]), (1, ys[1])])
-            add_up(c, hidden, [(2, ys[2])])
+        def second_product(c, hidden, turn):
+            banks = [next_bank() for k in range(2)]
+            ys = [banks[n // 2][:, n % 2 * STEP : (n % 2 + 1) * STEP] for n in range(LAST)]
+            accumulate(c, hidden, [[(0, ys[0]), (1, ys[1])]])
+            accumulate(c, hidden, [[(2, ys[2])]], turn)
             return ys
 
         def gate(c):
-            return (GATES_AT + 2 * (c - 1)) * KIB
+            return (GATES_AT + 3 * (c - 1)) * KIB
 
         def quantize_late(c, rounded):
             hidden = []
             for u in range(2):
                 width = 2 * STEP * PACK
-                offset = gate(c) + KIB if u == 0 else None
+                offset = gate(c) + 2 * KIB + (2 * u - 1) * KIB // 4
                 half = rounded[:, u * width : (u + 1) * width]
-                codes, scales = quantize_hidden(f"late{c}_{u}", half, 2 * STEP, offset)
-                for k in range(2):
-                    hidden.append((codes[:, k * STEP : (k + 1) * STEP], scales[:, k * STEP : (k + 1) * STEP]))
+                groups = quantize_hidden(f"late{c}_{u}", half, 2 * STEP, offset)
+                hidden.extend([groups[0:2], groups[2:4]])
             return hidden
 
         def act_tile(c, a, place):
@@ -270,11 +292,11 @@ def tile_list_masked_patch_block_kernel(
         def places(first, count):
             return slots[:, first // LANES : (first + count) // LANES]
 
-        def weigh(c, y, offset=None):
+        def weigh(c, n, y, offset=None):
             if offset is None:
-                weighted = ring.tile([P, STEP], F32, name="weighted", bufs=3, align_bytes=64)
+                weighted = ring.tile([P, STEP], F32, name="weighted", bufs=2, align_bytes=64)
             else:
-                weighted = shared.tile([P, STEP], F32, name=f"weighted{c}", offset=offset, align_bytes=64)
+                weighted = shared.tile([P, STEP], F32, name=f"weighted{c}_{n}", offset=offset, align_bytes=64)
             nc.vector.tensor_tensor(weighted[:], y, weight[:, c * STEP : (c + 1) * STEP], MULT)
             return weighted
 
@@ -286,108 +308,137 @@ def tile_list_masked_patch_block_kernel(
                 windows[n][:].indirect(places(first, count)), sums[:], weight[:, first : first + count], MULT
             )
 
-        acts = {}
-        pairs = {}
+        unit = STEP * PACK
 
-        def late_activate(c, a):
-            place = SECOND_ACTS_AT[a] if c == 1 else LATER_ACTS_AT + 4 * (3 * (c - 2) + a)
-            if c > 1 and a < 2:
-                if a == 0:
-                    pairs[c] = shared.tile(
-                        [P, 2, STEP, PACK], F32, name=f"act_pair{c}", offset=place * KIB, align_bytes=64
-                    )
-                acts[c, a] = pairs[c][:, a]
-            else:
-                acts[c, a] = act_tile(c, a, place)
-            activate(a, c, acts[c, a])
+        def act_pair(c, a, place):
+            pair = shared.tile([P, 2, STEP, PACK], F32, name=f"act_pair{c}", offset=place * KIB, align_bytes=64)
+            for u in range(2):
+                activate(a + u, c, pair[:, u])
+            return pair
 
-        def late_hidden(c):
-            unit = STEP * PACK
-            rounded = shared.tile(
-                [P, BANDS * unit], BF16, name=f"late_rounded{c}", offset=ROUNDED_AT * KIB, align_bytes=64
-            )
-            waiting = []
-            for a in range(BANDS):
-                dst = rounded[:, a * unit : (a + 1) * unit]
-                if a < BANDS - UNITS_ON_SCALAR[c]:
-                    if (c, a) not in acts:
-                        late_activate(c, a)
-                    if c == 1 or a > 1:
-                        apply_gain(nc.gpsimd, a, acts[c, a][:], dst)
-                    elif a == 1:
-                        apply_gain_to_pair(pairs[c][:], rounded[:, 0 : 2 * unit])
-                else:
-                    if a == LAST:
-                        planes = shared.tile([P, PACK, STEP], BF16, name=f"planes{c}", offset=gate(c), align_bytes=64)
-                    else:
-                        planes = ring.tile([P, PACK, STEP], BF16, name="planes", bufs=2, align_bytes=64)
-                    hidden_on_scalar(a, c, planes)
-                    waiting.append((planes, dst))
-            if c + 1 < CHUNKS:
-                for a in range(AHEAD):
-                    late_activate(c + 1, a)
-            for planes, dst in waiting:
-                interleave(planes, dst)
-            return rounded
+        def last_planes(c):
+            planes = shared.tile([P, PACK, STEP], BF16, name=f"planes{c}", offset=gate(c), align_bytes=64)
+            hidden_on_scalar(LAST, c, planes)
+            return planes
+
+        def scatter_early(c, ys, count):
+            weighed = [weigh(c, n, ys[n], gate(c + 1) + 2 * KIB if n == count - 2 else None) for n in range(count)]
+            for n in range(count):
+                scatter_copy(c, n, weighed[n])
+
+        def last_stripe(c, hidden):
+            y = bank(LAST_BANK)[:, 0:STEP]
+            accumulate(c, hidden, [[(LAST, y)]])
+            return y
 
         nc.vector.tensor_copy(v_scales[:], table_scales[:].bitcast(U8).indirect(picks[:]))
         quantize_w1(0)
-        warm = shared.tile([P, 1], F32, name="warm", offset=LAST_WINDOW_AT * KIB)
-        nc.scalar.activation(warm[:], windows[LAST - 1][:, 0:1], ACT.Gelu_apprx_sigmoid)
+        nc.vector.memset(ws_plane[:], 0)
+        for q in range(4):
+            rows = slice(32 * q, 32 * q + 4)
+            nc.scalar.dma_start(out=ws_plane[rows], in_=ws_scales[0, 4 * q : 4 * q + 4, :].bitcast(I32))
         windows.append(shared.tile([P, T2], F32, name="window_last", offset=LAST_WINDOW_AT * KIB, align_bytes=64))
         nc.gpsimd.memset(windows[LAST][:].bitcast(I32), 0)
+        turned = bank(LAST_BANK)
+        for t in range(PACK):
+            nc.tensor.transpose(turned[:, t * P : (t + 1) * P], gain_rows[:, t : P * PACK : PACK], identity[:])
+        bank_gain = turned[:].rearrange("p (t a) -> p a t", t=PACK)
+        nc.scalar.copy(out=gain[:], in_=bank_gain[:, 0:BANDS, :])
         gather_codes(0)
-        quantize_w1(1)
-
-        hidden = []
-        for a in range(BANDS):
-            if a < LAST:
-                rounded = ring.tile([P, STEP * PACK], BF16, name="h_rounded", bufs=2, align_bytes=64)
-            else:
-                rounded = shared.tile(
-                    [P, STEP * PACK], BF16, name="h_rounded_last", offset=ROUNDED_AT * KIB, align_bytes=64
-                )
-            act = act_tile(0, a, FIRST_ACTS_AT[a])
-            activate(a, 0, act)
-            width = STEP if a < LAST else GROUP
-            for lo in range(0, STEP, width):
-                apply_gain(nc.vector, a, act[:, lo : lo + width, :], rounded[:, lo * PACK : (lo + width) * PACK])
-            hidden.append(quantize_hidden(a, rounded[:], STEP))
-            if a + 2 < BANDS:
-                quantize_w1(a + 2)
         gather_codes(1)
-        ys = second_product(0, hidden)
+        for a in range(1, LAST):
+            quantize_w1(a)
+        quantize_last_w1()
 
-        for c in range(1, CHUNKS):
-            early = STRIPES - 1 if c < CHUNKS - 1 else STRIPES - 2
-            weighed = [weigh(c - 1, ys[n]) for n in range(early)]
-            for n in range(early):
-                scatter_copy(c - 1, n, weighed[n])
-            rounded = late_hidden(c)
-            if c < CHUNKS - 1:
-                accumulate(c - 1, hidden, [(LAST, ys[LAST])])
-                weighted = weigh(c - 1, ys[LAST], gate(c))
-                hidden = quantize_late(c, rounded)
-                scatter_copy(c - 1, LAST, weighted)
-                ys = second_product(c, hidden)
+        rounded_first = shared.tile(
+            [P, unit], BF16, name="h_rounded_first", offset=SECOND_RAW_AT * KIB, align_bytes=64
+        )
+        rounded_middle = keep.tile([P, 2 * unit], BF16, name="h_rounded_middle", align_bytes=64)
+        rounded_last = shared.tile([P, unit], BF16, name="h_rounded_last", offset=ROUNDED_AT * KIB, align_bytes=64)
+        first_acts = []
+        for a in range(BANDS):
+            first_acts.append(act_tile(0, a, FIRST_ACTS_AT[a]))
+            activate(a, 0, first_acts[a])
+            if a == 0:
+                apply_gain(nc.vector, bank_gain[:, a, :], first_acts[a][:], rounded_first[:])
+                hidden = [quantize_hidden(0, rounded_first[:], STEP)]
+                act_ahead = act_tile(1, 0, SECOND_ACTS_AT[0])
+                activate(0, 1, act_ahead)
+            elif a < LAST:
+                dst = rounded_middle[:, (a - 1) * unit : a * unit]
+                apply_gain(nc.vector, bank_gain[:, a, :], first_acts[a][:], dst)
+        halves = [rounded_last[:, lo * PACK : (lo + GROUP) * PACK] for lo in range(0, STEP, GROUP)]
+        apply_gain(nc.vector, bank_gain[:, LAST, :], first_acts[LAST][:, 0:GROUP, :], halves[0])
+        groups = quantize_hidden("middle", rounded_middle[:], 2 * STEP)
+        hidden.extend([groups[0:2], groups[2:4]])
+        apply_gain(nc.vector, bank_gain[:, LAST, :], first_acts[LAST][:, GROUP:STEP, :], halves[1])
+        hidden.append([quantize_hidden(f"last{u}", halves[u], GROUP)[0] for u in range(2)])
+        rounded_ahead = shared.tile(
+            [P, unit], BF16, name="h_rounded_ahead", offset=(LAST_W1_AT + 2) * KIB, align_bytes=64
+        )
+        apply_gain(nc.gpsimd, gain[:, 0, :], act_ahead[:], rounded_ahead[:])
+        ahead = quantize_hidden("ahead", rounded_ahead[:], STEP, FIRST_ACTS_AT[LAST] * KIB)
+
+        pair = act_pair(1, 1, SECOND_ACTS_AT[1])
+        ys = second_product(0, hidden, 3)
+        scatter_early(0, ys, 2)
+        sums = keep.tile([P, STEP], F32, name="sums_early0", align_bytes=64)
+        nc.scalar.copy(out=sums[:], in_=ys[2])
+        scatter_weighted(2, 0 * STEP, STEP, sums)
+        rounded = shared.tile([P, 3 * unit], BF16, name="rounded1", offset=ROUNDED_AT * KIB, align_bytes=64)
+        apply_gain_to_pair(1, pair[:], rounded[:, 0 : 2 * unit])
+        planes = last_planes(1)
+        pair = act_pair(2, 0, LATER_ACTS_AT)
+        interleave(planes, rounded[:, 2 * unit : 3 * unit])
+        y_last = last_stripe(0, hidden)
+        weighted = weigh(0, LAST, y_last, gate(1))
+        groups = quantize_hidden("second_pair", rounded[:, 0 : 2 * unit], 2 * STEP, gate(1) + 7 * KIB // 4)
+        last = quantize_hidden("second_last", rounded[:, 2 * unit : 3 * unit], STEP, gate(1) + 9 * KIB // 4)
+        hidden = [ahead, groups[0:2], groups[2:4], last]
+        scatter_copy(0, LAST, weighted)
+
+        ys = second_product(1, hidden, 3)
+        scatter_early(1, ys, LAST)
+        rounded = shared.tile([P, BANDS * unit], BF16, name="rounded2", offset=ROUNDED_AT * KIB, align_bytes=64)
+        apply_gain_to_pair(0, pair[:], rounded[:, 0 : 2 * unit])
+        act = act_tile(2, 2, LATER_ACTS_AT + 8)
+        activate(2, 2, act)
+        apply_gain(nc.gpsimd, gain[:, 2, :], act[:], rounded[:, 2 * unit : 3 * unit])
+        planes = last_planes(2)
+        last_pair = act_pair(3, 0, LATER_ACTS_AT + 12)
+        interleave(planes, rounded[:, 3 * unit : 4 * unit])
+        y_last = last_stripe(1, hidden)
+        weighted = weigh(1, LAST, y_last, gate(2))
+        hidden = quantize_late(2, rounded)
+        scatter_copy(1, LAST, weighted)
+
+        ys = second_product(2, hidden, 2)
+        scatter_early(2, ys, 2)
+        rounded = shared.tile([P, BANDS * unit], BF16, name="rounded3", offset=ROUNDED_AT * KIB, align_bytes=64)
+        apply_gain_to_pair(0, last_pair[:], rounded[:, 0 : 2 * unit])
+        third_planes = keep.tile([P, PACK, STEP], BF16, name="third_planes", align_bytes=64)
+        hidden_on_scalar(2, 3, third_planes)
+        planes = last_planes(3)
+        interleave(third_planes, rounded[:, 2 * unit : 3 * unit])
+        interleave(planes, rounded[:, 3 * unit : 4 * unit])
 
         c = CHUNKS - 1
         held = STRIPES - 2
-        joint = next_bank(False)
-        accumulate(c - 1, hidden, [(LAST, joint[:, 0:STEP])])
+        joint = bank(LAST_BANK)
+        accumulate(c - 1, hidden, [[(LAST, joint[:, 0:STEP])]])
         hidden = quantize_late(c, rounded)
         sums = shared.tile([P, STEP], F32, name="sums_held", offset=gate(c), align_bytes=64)
         nc.scalar.copy(out=sums[:], in_=ys[held])
         scatter_weighted(held, (c - 1) * STEP, STEP, sums)
         for n in range(STRIPES):
             if n < LAST:
-                y = next_bank(False)
-                accumulate_behind_quantise(c, hidden, [(n, y[:, 0:STEP])])
+                y = next_bank()
+                accumulate(c, hidden, [[(n, y[:, 0:STEP])]], 2 if n > 0 else 0)
                 sums = keep.tile([P, STEP], F32, name=f"sums{n}", align_bytes=64)
                 nc.scalar.copy(out=sums[:], in_=y[:, 0:STEP])
                 scatter_weighted(n, c * STEP, STEP, sums)
             else:
-                accumulate_behind_quantise(c, hidden, [(n, joint[:, STEP:HALF])])
+                accumulate(c, hidden, [[(n, joint[:, STEP:HALF])]], 2)
                 sums = keep.tile([P, HALF], F32, name=f"sums{n}", align_bytes=64)
                 nc.scalar.copy(out=sums[:], in_=joint[:])
                 scatter_weighted(n, (c - 1) * STEP, HALF, sums)

@@ -29,8 +29,7 @@ CHUNKS = S // STEP
 LANES = 16
 KIB = 1024
 
-ROUNDED_BY_VECTOR = [0, 128, 72]
-LAST_ROUNDED_BY_VECTOR = [0, 128]
+ROUNDED_BY_VECTOR = [0, 128, 64, 72]
 UNITS_ON_SCALAR = [0, 1, 1, 2]
 AHEAD = 2
 SHORTCUT_AT = 2
@@ -66,10 +65,7 @@ def tile_list_masked_patch_block_kernel(
         )
         raw = [keep.tile([P, PACK, P * PACK], F32, name=f"raw{a}", align_bytes=64) for a in range(LAST) if a != 1]
         raw.insert(1, shared.tile([P, PACK, P * PACK], F32, name="raw1", offset=SECOND_RAW_AT * KIB, align_bytes=64))
-        raw_last = [
-            shared.tile([P, 2, P * PACK], F32, name="raw_last0", offset=FIRST_ACTS_AT[1] * KIB, align_bytes=64),
-            keep.tile([P, 2, P * PACK], F32, name="raw_last1", align_bytes=64),
-        ]
+        raw.append(keep.tile([P, PACK, P * PACK], F32, name="raw3", align_bytes=64))
         gain_rows = keep.tile([P, P * PACK], F32, name="gain_rows", align_bytes=64)
         identity = keep.tile([P, P], F32, name="identity", align_bytes=64)
         gain = shared.tile([P, BANDS, PACK], F32, name="gain", offset=(TABLE_SCALES_AT + 1) * KIB)
@@ -112,9 +108,7 @@ def tile_list_masked_patch_block_kernel(
         nc.sync.dma_start(out=table[:], in_=tab_words[0].rearrange("p t i -> p (t i)").bitcast(I32))
         load_w1(1)
         load_w1(2)
-        last_rows = w1[:, LAST * P * PACK :].rearrange("(p j) c -> p j c", j=PACK)
-        for u in range(2):
-            nc.sync.dma_start(out=raw_last[u][:], in_=last_rows[:, 2 * u : 2 * u + 2, :])
+        load_w1(LAST)
         for q in range(4):
             rows = slice(32 * q, 32 * q + 4)
             nc.sync.dma_start(
@@ -135,9 +129,10 @@ def tile_list_masked_patch_block_kernel(
             return v_codes[i][:, lo : lo + count].bitcast(FP8X4), v_scales[:, first : first + count]
 
         def quantize_w1(a):
-            if a == 0:
+            if a == 0 or a == LAST:
+                place = LAST_WINDOW_AT if a == 0 else LAST_W1_AT
                 rounded = shared.tile(
-                    [P, P * PACK * PACK], BF16, name="w1_first", offset=LAST_WINDOW_AT * KIB, align_bytes=64
+                    [P, P * PACK * PACK], BF16, name=f"w1_rounded{a}", offset=place * KIB, align_bytes=64
                 )
             else:
                 rounded = ring.tile([P, P * PACK * PACK], BF16, name="w1_rounded", bufs=2, align_bytes=64)
@@ -149,18 +144,6 @@ def tile_list_masked_patch_block_kernel(
             if split < P:
                 nc.scalar.copy(out=dst[:, split:P], in_=src[:, split:P])
             nc.vector.quantize_mx(out=w1_codes[a][:].bitcast(FP8X4), scales=w1_scales[a][:], in_=rounded[:])
-
-        def quantize_last_w1():
-            rounded = shared.tile([P, P * PACK * PACK], BF16, name="w1_last", offset=LAST_W1_AT * KIB, align_bytes=64)
-            dst = rounded[:].rearrange("p (t m j) -> p m j t", t=PACK, j=PACK)
-            for u in range(2):
-                src = raw_last[u][:].rearrange("p j (m t) -> p m j t", t=PACK)
-                split = LAST_ROUNDED_BY_VECTOR[u]
-                if split > 0:
-                    nc.vector.tensor_copy(out=dst[:, 0:split, 2 * u : 2 * u + 2], in_=src[:, 0:split])
-                if split < P:
-                    nc.scalar.copy(out=dst[:, split:P, 2 * u : 2 * u + 2], in_=src[:, split:P])
-            nc.vector.quantize_mx(out=w1_codes[LAST][:].bitcast(FP8X4), scales=w1_scales[LAST][:], in_=rounded[:])
 
         def first_product(a, t, first, count, dst):
             codes, scales = patch(first, count)
@@ -341,19 +324,20 @@ def tile_list_masked_patch_block_kernel(
         nc.gpsimd.memset(windows[LAST][:].bitcast(I32), 0)
         turned = bank(LAST_BANK)
         for t in range(PACK):
-            nc.tensor.transpose(turned[:, t * P : (t + 1) * P], gain_rows[:, t : P * PACK : PACK], identity[:])
-        bank_gain = turned[:].rearrange("p (t a) -> p a t", t=PACK)
+            nc.tensor.transpose(turned[:, t : HALF : PACK], gain_rows[:, t : P * PACK : PACK], identity[:])
+        bank_gain = turned[:].rearrange("p (a t) -> p a t", t=PACK)
         nc.scalar.copy(out=gain[:], in_=bank_gain[:, 0:BANDS, :])
         gather_codes(0)
         gather_codes(1)
-        for a in range(1, LAST):
+        for a in range(1, BANDS):
             quantize_w1(a)
-        quantize_last_w1()
 
         rounded_first = shared.tile(
             [P, unit], BF16, name="h_rounded_first", offset=SECOND_RAW_AT * KIB, align_bytes=64
         )
-        rounded_middle = keep.tile([P, 2 * unit], BF16, name="h_rounded_middle", align_bytes=64)
+        rounded_middle = shared.tile(
+            [P, 2 * unit], BF16, name="h_rounded_middle", offset=(LAST_W1_AT - 2) * KIB, align_bytes=64
+        )
         rounded_last = shared.tile([P, unit], BF16, name="h_rounded_last", offset=ROUNDED_AT * KIB, align_bytes=64)
         first_acts = []
         for a in range(BANDS):

@@ -43,6 +43,7 @@ LAST_W1_AT = 66
 LATER_ACTS_AT = 20
 LAST_WINDOW_AT = 52
 TABLE_SCALES_AT = 60
+FIRST_RAW_AT = 87
 SECOND_RAW_AT = 79
 GATES_AT = 70
 
@@ -63,8 +64,10 @@ def tile_list_masked_patch_block_kernel(
         table_scales = shared.tile(
             [P, T // 4], I32, name="table_scales", offset=TABLE_SCALES_AT * KIB, align_bytes=64
         )
-        raw = [keep.tile([P, PACK, P * PACK], F32, name=f"raw{a}", align_bytes=64) for a in range(LAST) if a != 1]
-        raw.insert(1, shared.tile([P, PACK, P * PACK], F32, name="raw1", offset=SECOND_RAW_AT * KIB, align_bytes=64))
+        raw = [keep.tile([P, PACK, P * PACK], F32, name=f"raw{a}", align_bytes=64) for a in range(2, LAST)]
+        for a in range(2):
+            place = [FIRST_RAW_AT, SECOND_RAW_AT][a]
+            raw.insert(a, shared.tile([P, PACK, P * PACK], F32, name=f"raw{a}", offset=place * KIB, align_bytes=64))
         raw.append(keep.tile([P, PACK, P * PACK], F32, name="raw3", align_bytes=64))
         gain_rows = keep.tile([P, P * PACK], F32, name="gain_rows", align_bytes=64)
         identity = keep.tile([P, P], F32, name="identity", align_bytes=64)
@@ -74,7 +77,7 @@ def tile_list_masked_patch_block_kernel(
         w2_planes = keep.tile([P, BANDS, N // 4], I32, name="w2_planes", align_bytes=64)
         ws_plane = shared.tile([P, N // 4], I32, name="ws_plane", offset=(TABLE_SCALES_AT + 2) * KIB, align_bytes=64)
         weight = keep.tile([P, S], F32, name="weight", align_bytes=64)
-        windows = [keep.tile([P, T2], F32, name=f"window{n}", align_bytes=64) for n in range(LAST)]
+        windows = [keep.tile([P, T2], F32, name=f"window{n}", align_bytes=64) for n in range(2)]
         v_codes = [
             keep.tile([P, HALF], U32, name="v_codes0", align_bytes=64),
             keep.tile([P, HALF], U32, name="v_codes1", align_bytes=64),
@@ -89,7 +92,7 @@ def tile_list_masked_patch_block_kernel(
 
         nc.vector.memset(table_scales[:], 0)
         nc.vector.memset(gain_rows[:], 0.0)
-        for n in range(LAST):
+        for n in range(2):
             nc.vector.memset(windows[n][:].bitcast(I32), 0)
         nc.vector.memset(w2_planes[:], 0)
         make_identity(nc, identity[:])
@@ -320,6 +323,8 @@ def tile_list_masked_patch_block_kernel(
         for q in range(4):
             rows = slice(32 * q, 32 * q + 4)
             nc.scalar.dma_start(out=ws_plane[rows], in_=ws_scales[0, 4 * q : 4 * q + 4, :].bitcast(I32))
+        windows.append(shared.tile([P, T2], F32, name="window2", offset=FIRST_RAW_AT * KIB, align_bytes=64))
+        nc.gpsimd.memset(windows[2][:].bitcast(I32), 0)
         windows.append(shared.tile([P, T2], F32, name="window_last", offset=LAST_WINDOW_AT * KIB, align_bytes=64))
         nc.gpsimd.memset(windows[LAST][:].bitcast(I32), 0)
         turned = bank(LAST_BANK)

@@ -29,7 +29,7 @@ CHUNKS = S // STEP
 LANES = 16
 KIB = 1024
 
-ROUNDED_BY_VECTOR = [0, 128, 64, 72]
+ROUNDED_BY_VECTOR = [0, 128, 64, 80]
 UNITS_ON_SCALAR = [0, 1, 1, 2]
 AHEAD = 2
 SHORTCUT_AT = 2
@@ -43,6 +43,7 @@ LAST_W1_AT = 66
 LATER_ACTS_AT = 20
 LAST_WINDOW_AT = 52
 TABLE_SCALES_AT = 60
+LAST_RAW_AT = 95
 FIRST_RAW_AT = 87
 SECOND_RAW_AT = 79
 GATES_AT = 70
@@ -68,14 +69,13 @@ def tile_list_masked_patch_block_kernel(
         for a in range(2):
             place = [FIRST_RAW_AT, SECOND_RAW_AT][a]
             raw.insert(a, shared.tile([P, PACK, P * PACK], F32, name=f"raw{a}", offset=place * KIB, align_bytes=64))
-        raw.append(keep.tile([P, PACK, P * PACK], F32, name="raw3", align_bytes=64))
+        raw.append(shared.tile([P, PACK, P * PACK], F32, name="raw3", offset=LAST_RAW_AT * KIB, align_bytes=64))
         gain_rows = keep.tile([P, P * PACK], F32, name="gain_rows", align_bytes=64)
         identity = keep.tile([P, P], F32, name="identity", align_bytes=64)
         gain = shared.tile([P, BANDS, PACK], F32, name="gain", offset=(TABLE_SCALES_AT + 1) * KIB)
         w2_codes = keep.tile([P, BANDS, 2 * N], U8, name="w2_codes", align_bytes=64)
         ws_codes = keep.tile([P, N], I32, name="ws_codes", align_bytes=64)
-        w2_planes = keep.tile([P, BANDS, N // 4], I32, name="w2_planes", align_bytes=64)
-        ws_plane = shared.tile([P, N // 4], I32, name="ws_plane", offset=(TABLE_SCALES_AT + 2) * KIB, align_bytes=64)
+        out_scales = keep.tile([P, BANDS + 1, N // 4], I32, name="out_scales", align_bytes=64)
         weight = keep.tile([P, S], F32, name="weight", align_bytes=64)
         windows = [keep.tile([P, T2], F32, name=f"window{n}", align_bytes=64) for n in range(2)]
         v_codes = [
@@ -94,7 +94,7 @@ def tile_list_masked_patch_block_kernel(
         nc.vector.memset(gain_rows[:], 0.0)
         for n in range(2):
             nc.vector.memset(windows[n][:].bitcast(I32), 0)
-        nc.vector.memset(w2_planes[:], 0)
+        nc.vector.memset(out_scales[:], 0)
         make_identity(nc, identity[:])
 
         def load_w1(a):
@@ -109,13 +109,16 @@ def tile_list_masked_patch_block_kernel(
                 out=table_scales[32 * q : 32 * q + 4, :], in_=tab_scales[0, 4 * q : 4 * q + 4, :].bitcast(I32)
             )
         nc.sync.dma_start(out=table[:], in_=tab_words[0].rearrange("p t i -> p (t i)").bitcast(I32))
+        for q in range(4):
+            rows = slice(32 * q, 32 * q + 4)
+            nc.sync.dma_start(out=out_scales[rows, BANDS, :], in_=ws_scales[0, 4 * q : 4 * q + 4, :].bitcast(I32))
         load_w1(1)
         load_w1(2)
         load_w1(LAST)
         for q in range(4):
             rows = slice(32 * q, 32 * q + 4)
             nc.sync.dma_start(
-                out=w2_planes[rows],
+                out=out_scales[rows, 0:BANDS, :],
                 in_=w2_scales[:, 4 * q : 4 * q + 4, :].rearrange("a q c -> q a c").bitcast(I32),
             )
         nc.sync.dma_start(out=w2_codes[:].bitcast(I32), in_=w2_words.rearrange("a p c -> p a c").bitcast(I32))
@@ -220,7 +223,7 @@ def tile_list_masked_patch_block_kernel(
             nc.tensor.matmul_mx(
                 out=dst,
                 lhsT=ws_codes[:, n * P : (n + 1) * P].bitcast(FP8X4),
-                lhsT_scale=ws_plane[:].bitcast(U8)[:, n * P : (n + 1) * P],
+                lhsT_scale=out_scales[:, BANDS, :].bitcast(U8)[:, n * P : (n + 1) * P],
                 rhs=codes,
                 rhs_scale=scales,
                 start=start,
@@ -233,7 +236,7 @@ def tile_list_masked_patch_block_kernel(
                 nc.tensor.matmul_mx(
                     out=dst[:, lo : lo + GROUP],
                     lhsT=w2_codes[:, a, 2 * n * P : 2 * (n + 1) * P].bitcast(FP4X4),
-                    lhsT_scale=w2_planes[:, a, :].bitcast(U8)[:, n * P : (n + 1) * P],
+                    lhsT_scale=out_scales[:, a, :].bitcast(U8)[:, n * P : (n + 1) * P],
                     rhs=codes.bitcast(FP8X4),
                     rhs_scale=scales,
                     start=opens and lo == 0,
@@ -319,10 +322,6 @@ def tile_list_masked_patch_block_kernel(
 
         nc.vector.tensor_copy(v_scales[:], table_scales[:].bitcast(U8).indirect(picks[:]))
         quantize_w1(0)
-        nc.vector.memset(ws_plane[:], 0)
-        for q in range(4):
-            rows = slice(32 * q, 32 * q + 4)
-            nc.scalar.dma_start(out=ws_plane[rows], in_=ws_scales[0, 4 * q : 4 * q + 4, :].bitcast(I32))
         windows.append(shared.tile([P, T2], F32, name="window2", offset=FIRST_RAW_AT * KIB, align_bytes=64))
         nc.gpsimd.memset(windows[2][:].bitcast(I32), 0)
         windows.append(shared.tile([P, T2], F32, name="window_last", offset=LAST_WINDOW_AT * KIB, align_bytes=64))
@@ -341,7 +340,7 @@ def tile_list_masked_patch_block_kernel(
             [P, unit], BF16, name="h_rounded_first", offset=SECOND_RAW_AT * KIB, align_bytes=64
         )
         rounded_middle = shared.tile(
-            [P, 2 * unit], BF16, name="h_rounded_middle", offset=(LAST_W1_AT - 2) * KIB, align_bytes=64
+            [P, 2 * unit], BF16, name="h_rounded_middle", offset=LAST_RAW_AT * KIB, align_bytes=64
         )
         rounded_last = shared.tile([P, unit], BF16, name="h_rounded_last", offset=ROUNDED_AT * KIB, align_bytes=64)
         first_acts = []
@@ -371,14 +370,16 @@ def tile_list_masked_patch_block_kernel(
         pair = act_pair(1, 1, SECOND_ACTS_AT[1])
         ys = second_product(0, hidden, 3)
         scatter_early(0, ys, 2)
-        sums = keep.tile([P, STEP], F32, name="sums_early0", align_bytes=64)
-        nc.scalar.copy(out=sums[:], in_=ys[2])
-        scatter_weighted(2, 0 * STEP, STEP, sums)
         rounded = shared.tile([P, 3 * unit], BF16, name="rounded1", offset=ROUNDED_AT * KIB, align_bytes=64)
         apply_gain_to_pair(1, pair[:], rounded[:, 0 : 2 * unit])
         planes = last_planes(1)
-        pair = act_pair(2, 0, LATER_ACTS_AT)
+        sums = keep.tile([P, STEP], F32, name="sums_early0", align_bytes=64)
+        nc.scalar.copy(out=sums[:], in_=ys[2])
+        scatter_weighted(2, 0 * STEP, STEP, sums)
+        pair = shared.tile([P, 2, STEP, PACK], F32, name="act_pair2", offset=LATER_ACTS_AT * KIB, align_bytes=64)
+        activate(0, 2, pair[:, 0])
         interleave(planes, rounded[:, 2 * unit : 3 * unit])
+        activate(1, 2, pair[:, 1])
         y_last = last_stripe(0, hidden)
         weighted = weigh(0, LAST, y_last, gate(1))
         groups = quantize_hidden("second_pair", rounded[:, 0 : 2 * unit], 2 * STEP, gate(1) + 7 * KIB // 4)

@@ -104,22 +104,18 @@ def tile_list_masked_patch_block_kernel(
         nc.sync.dma_start(picks[:], offs)
         load_w1(0)
         nc.sync.dma_start(out=gain_rows[0:BANDS, :], in_=ga.rearrange("(a c) -> a c", a=BANDS))
-        for q in range(4):
-            nc.sync.dma_start(
-                out=table_scales[32 * q : 32 * q + 4, :], in_=tab_scales[0, 4 * q : 4 * q + 4, :].bitcast(I32)
-            )
+        for r in range(4):
+            nc.sync.dma_start(out=table_scales[r:P:32, :], in_=tab_scales[0, r:16:4, :].bitcast(I32))
         nc.sync.dma_start(out=table[:], in_=tab_words[0].rearrange("p t i -> p (t i)").bitcast(I32))
-        for q in range(4):
-            rows = slice(32 * q, 32 * q + 4)
-            nc.sync.dma_start(out=out_scales[rows, BANDS, :], in_=ws_scales[0, 4 * q : 4 * q + 4, :].bitcast(I32))
+        for r in range(4):
+            nc.sync.dma_start(out=out_scales[r:P:32, BANDS, :], in_=ws_scales[0, r:16:4, :].bitcast(I32))
         load_w1(1)
         load_w1(2)
         load_w1(LAST)
-        for q in range(4):
-            rows = slice(32 * q, 32 * q + 4)
+        for r in range(4):
             nc.sync.dma_start(
-                out=out_scales[rows, 0:BANDS, :],
-                in_=w2_scales[:, 4 * q : 4 * q + 4, :].rearrange("a q c -> q a c").bitcast(I32),
+                out=out_scales[r:P:32, 0:BANDS, :],
+                in_=w2_scales[:, r:16:4, :].rearrange("a q c -> q a c").bitcast(I32),
             )
         nc.sync.dma_start(out=w2_codes[:].bitcast(I32), in_=w2_words.rearrange("a p c -> p a c").bitcast(I32))
         nc.sync.dma_start(out=ws_codes[:], in_=ws_words[0].rearrange("p c i -> p (c i)").bitcast(I32))

@@ -45,7 +45,8 @@ LAST_WINDOW_AT = 52
 TABLE_SCALES_AT = 60
 LAST_RAW_AT = 95
 FIRST_RAW_AT = 87
-SECOND_RAW_AT = 79
+SECOND_RAW_AT = 62
+GAIN_ROWS_AT = 79
 GATES_AT = 70
 
 
@@ -70,18 +71,20 @@ def tile_list_masked_patch_block_kernel(
             place = [FIRST_RAW_AT, SECOND_RAW_AT][a]
             raw.insert(a, shared.tile([P, PACK, P * PACK], F32, name=f"raw{a}", offset=place * KIB, align_bytes=64))
         raw.append(shared.tile([P, PACK, P * PACK], F32, name="raw3", offset=LAST_RAW_AT * KIB, align_bytes=64))
-        gain_rows = keep.tile([P, P * PACK], F32, name="gain_rows", align_bytes=64)
+        gain_rows = shared.tile([P, P * PACK], F32, name="gain_rows", offset=GAIN_ROWS_AT * KIB, align_bytes=64)
         identity = keep.tile([P, P], F32, name="identity", align_bytes=64)
         gain = shared.tile([P, BANDS, PACK], F32, name="gain", offset=(TABLE_SCALES_AT + 1) * KIB)
         w2_codes = keep.tile([P, BANDS, 2 * N], U8, name="w2_codes", align_bytes=64)
         ws_codes = keep.tile([P, N], I32, name="ws_codes", align_bytes=64)
-        out_scales = keep.tile([P, BANDS + 1, N // 4], I32, name="out_scales", align_bytes=64)
+        out_scales = keep.tile([P, BANDS, N // 4], I32, name="out_scales", align_bytes=64)
+        ws_plane = keep.tile([P, N // 4], I32, name="ws_plane", align_bytes=64)
         weight = keep.tile([P, S], F32, name="weight", align_bytes=64)
         windows = [keep.tile([P, T2], F32, name=f"window{n}", align_bytes=64) for n in range(2)]
         v_codes = [
             keep.tile([P, HALF], U32, name="v_codes0", align_bytes=64),
             keep.tile([P, HALF], U32, name="v_codes1", align_bytes=64),
         ]
+        spread_scales = keep.tile([P, S], U8, name="spread_scales", align_bytes=64)
         v_scales = keep.tile([P, S], U8, name="v_scales", align_bytes=64)
         w1_codes = [keep.tile([P, P * PACK], U32, name=f"w1_codes{a}", align_bytes=64) for a in range(BANDS)]
         w1_scales = [
@@ -92,10 +95,12 @@ def tile_list_masked_patch_block_kernel(
 
         nc.vector.memset(table_scales[:], 0)
         nc.vector.memset(gain_rows[:], 0.0)
+        nc.vector.memset(ws_plane[:], 0)
         for n in range(2):
             nc.vector.memset(windows[n][:].bitcast(I32), 0)
-        nc.vector.memset(out_scales[:], 0)
         make_identity(nc, identity[:])
+        nc.gpsimd.memset(v_scales[:].bitcast(I32), 0)
+        nc.gpsimd.memset(out_scales[:], 0)
 
         def load_w1(a):
             cols = slice(a * P * PACK, (a + 1) * P * PACK)
@@ -103,12 +108,14 @@ def tile_list_masked_patch_block_kernel(
 
         nc.sync.dma_start(picks[:], offs)
         load_w1(0)
-        nc.sync.dma_start(out=gain_rows[0:BANDS, :], in_=ga.rearrange("(a c) -> a c", a=BANDS))
+        nc.sync.dma_start(out=gain_rows[0 : 4 * BANDS : 4, :], in_=ga.rearrange("(a c) -> a c", a=BANDS))
+        nc.sync.dma_start(out=table_scales[0:P:8, :], in_=tab_scales[0].bitcast(I32))
         for r in range(4):
-            nc.sync.dma_start(out=table_scales[r:P:32, :], in_=tab_scales[0, r:16:4, :].bitcast(I32))
+            nc.sync.dma_start(out=ws_plane[r:P:32, :], in_=ws_scales[0, r:16:4, :].bitcast(I32))
         nc.sync.dma_start(out=table[:], in_=tab_words[0].rearrange("p t i -> p (t i)").bitcast(I32))
+        nc.vector.tensor_copy(spread_scales[:], table_scales[:].bitcast(U8).indirect(picks[:]))
         for r in range(4):
-            nc.sync.dma_start(out=out_scales[r:P:32, BANDS, :], in_=ws_scales[0, r:16:4, :].bitcast(I32))
+            nc.sync.dma_start(out=v_scales[r:P:32, :].bitcast(I32), in_=spread_scales[8 * r : P : 32, :].bitcast(I32))
         load_w1(1)
         load_w1(2)
         load_w1(LAST)
@@ -219,7 +226,7 @@ def tile_list_masked_patch_block_kernel(
             nc.tensor.matmul_mx(
                 out=dst,
                 lhsT=ws_codes[:, n * P : (n + 1) * P].bitcast(FP8X4),
-                lhsT_scale=out_scales[:, BANDS, :].bitcast(U8)[:, n * P : (n + 1) * P],
+                lhsT_scale=ws_plane[:].bitcast(U8)[:, n * P : (n + 1) * P],
                 rhs=codes,
                 rhs_scale=scales,
                 start=start,
@@ -316,16 +323,15 @@ def tile_list_masked_patch_block_kernel(
             accumulate(c, hidden, [[(LAST, y)]])
             return y
 
-        nc.vector.tensor_copy(v_scales[:], table_scales[:].bitcast(U8).indirect(picks[:]))
         quantize_w1(0)
-        windows.append(shared.tile([P, T2], F32, name="window2", offset=FIRST_RAW_AT * KIB, align_bytes=64))
-        nc.gpsimd.memset(windows[2][:].bitcast(I32), 0)
-        windows.append(shared.tile([P, T2], F32, name="window_last", offset=LAST_WINDOW_AT * KIB, align_bytes=64))
-        nc.gpsimd.memset(windows[LAST][:].bitcast(I32), 0)
         turned = bank(LAST_BANK)
         for t in range(PACK):
             nc.tensor.transpose(turned[:, t : HALF : PACK], gain_rows[:, t : P * PACK : PACK], identity[:])
-        bank_gain = turned[:].rearrange("p (a t) -> p a t", t=PACK)
+        windows.append(shared.tile([P, T2], F32, name="window2", offset=GAIN_ROWS_AT * KIB, align_bytes=64))
+        nc.gpsimd.memset(windows[2][:].bitcast(I32), 0)
+        windows.append(shared.tile([P, T2], F32, name="window_last", offset=LAST_WINDOW_AT * KIB, align_bytes=64))
+        nc.gpsimd.memset(windows[LAST][:].bitcast(I32), 0)
+        bank_gain = turned[:].rearrange("p (a u) -> p a u", u=4 * PACK)[:, :, 0:PACK]
         nc.scalar.copy(out=gain[:], in_=bank_gain[:, 0:BANDS, :])
         gather_codes(0)
         gather_codes(1)

@@ -45,7 +45,7 @@ LAST_WINDOW_AT = 52
 TABLE_SCALES_AT = 60
 LAST_RAW_AT = 95
 FIRST_RAW_AT = 87
-SECOND_RAW_AT = 62
+SECOND_RAW_AT = 103
 GAIN_ROWS_AT = 79
 GATES_AT = 70
 
@@ -96,15 +96,16 @@ def tile_list_masked_patch_block_kernel(
         nc.vector.memset(table_scales[:], 0)
         nc.vector.memset(gain_rows[:], 0.0)
         nc.vector.memset(ws_plane[:], 0)
+        nc.vector.memset(v_scales[:].bitcast(I32), 0)
+        nc.vector.memset(out_scales[:], 0)
         for n in range(2):
             nc.vector.memset(windows[n][:].bitcast(I32), 0)
         make_identity(nc, identity[:])
-        nc.gpsimd.memset(v_scales[:].bitcast(I32), 0)
-        nc.gpsimd.memset(out_scales[:], 0)
 
-        def load_w1(a):
+        def load_w1(a, lo=0, hi=PACK):
             cols = slice(a * P * PACK, (a + 1) * P * PACK)
-            nc.sync.dma_start(out=raw[a][:], in_=w1[:, cols].rearrange("(p j) c -> p j c", j=PACK))
+            rows = w1[:, cols].rearrange("(p j) c -> p j c", j=PACK)
+            nc.sync.dma_start(out=raw[a][:, lo:hi, :], in_=rows[:, lo:hi, :])
 
         nc.sync.dma_start(picks[:], offs)
         load_w1(0)
@@ -113,10 +114,11 @@ def tile_list_masked_patch_block_kernel(
         for r in range(4):
             nc.sync.dma_start(out=ws_plane[r:P:32, :], in_=ws_scales[0, r:16:4, :].bitcast(I32))
         nc.sync.dma_start(out=table[:], in_=tab_words[0].rearrange("p t i -> p (t i)").bitcast(I32))
+        load_w1(1, 0, 2)
         nc.vector.tensor_copy(spread_scales[:], table_scales[:].bitcast(U8).indirect(picks[:]))
         for r in range(4):
             nc.sync.dma_start(out=v_scales[r:P:32, :].bitcast(I32), in_=spread_scales[8 * r : P : 32, :].bitcast(I32))
-        load_w1(1)
+        load_w1(1, 2, PACK)
         load_w1(2)
         load_w1(LAST)
         for r in range(4):

@@ -47,7 +47,8 @@ LAST_RAW_AT = 95
 FIRST_RAW_AT = 87
 SECOND_RAW_AT = 103
 GAIN_ROWS_AT = 79
-GATES_AT = 70
+GATES_AT = [70, 32, 76]
+LAST_PAIR_AT = 111
 
 
 def tile_list_masked_patch_block_kernel(
@@ -221,7 +222,8 @@ def tile_list_masked_patch_block_kernel(
             else:
                 scales = shared.tile([P, count], U8, name=f"h_scales{name}", offset=offset, align_bytes=64)
             nc.vector.quantize_mx(out=codes[:].bitcast(FP8X4), scales=scales[:], in_=rounded)
-            return [(codes[:, lo : lo + GROUP], scales[:, lo : lo + GROUP]) for lo in range(0, count, GROUP)]
+            width = min(count, STEP)
+            return [(codes[:, lo : lo + width], scales[:, lo : lo + width]) for lo in range(0, count, width)]
 
         def shortcut_pass(n, c, dst, start):
             codes, scales = patch(c * STEP, STEP)
@@ -236,16 +238,17 @@ def tile_list_masked_patch_block_kernel(
             )
 
         def band_passes(n, a, hidden, dst, opens, closes):
-            for lo in range(0, STEP, GROUP):
-                codes, scales = hidden[a][lo // GROUP]
+            width = STEP // len(hidden[a])
+            for lo in range(0, STEP, width):
+                codes, scales = hidden[a][lo // width]
                 nc.tensor.matmul_mx(
-                    out=dst[:, lo : lo + GROUP],
+                    out=dst[:, lo : lo + width],
                     lhsT=w2_codes[:, a, 2 * n * P : 2 * (n + 1) * P].bitcast(FP4X4),
                     lhsT_scale=out_scales[:, a, :].bitcast(U8)[:, n * P : (n + 1) * P],
                     rhs=codes.bitcast(FP8X4),
                     rhs_scale=scales,
                     start=opens and lo == 0,
-                    stop=closes and lo + GROUP == STEP,
+                    stop=closes and lo + width == STEP,
                 )
 
         def accumulate(c, hidden, groups, turn=0):
@@ -268,7 +271,7 @@ def tile_list_masked_patch_block_kernel(
             return ys
 
         def gate(c):
-            return (GATES_AT + 3 * (c - 1)) * KIB
+            return GATES_AT[c - 1] * KIB
 
         def quantize_late(c, rounded):
             hidden = []
@@ -277,7 +280,7 @@ def tile_list_masked_patch_block_kernel(
                 offset = gate(c) + 2 * KIB + (2 * u - 1) * KIB // 4
                 half = rounded[:, u * width : (u + 1) * width]
                 groups = quantize_hidden(f"late{c}_{u}", half, 2 * STEP, offset)
-                hidden.extend([groups[0:2], groups[2:4]])
+                hidden.extend([groups[0:1], groups[1:2]])
             return hidden
 
         def act_tile(c, a, place):
@@ -362,7 +365,7 @@ def tile_list_masked_patch_block_kernel(
         halves = [rounded_last[:, lo * PACK : (lo + GROUP) * PACK] for lo in range(0, STEP, GROUP)]
         apply_gain(nc.vector, bank_gain[:, LAST, :], first_acts[LAST][:, 0:GROUP, :], halves[0])
         groups = quantize_hidden("middle", rounded_middle[:], 2 * STEP)
-        hidden.extend([groups[0:2], groups[2:4]])
+        hidden.extend([groups[0:1], groups[1:2]])
         apply_gain(nc.vector, bank_gain[:, LAST, :], first_acts[LAST][:, GROUP:STEP, :], halves[1])
         hidden.append([quantize_hidden(f"last{u}", halves[u], GROUP)[0] for u in range(2)])
         rounded_ahead = shared.tile(
@@ -373,9 +376,11 @@ def tile_list_masked_patch_block_kernel(
 
         pair = act_pair(1, 1, SECOND_ACTS_AT[1])
         ys = second_product(0, hidden, 3)
-        scatter_early(0, ys, 2)
         rounded = shared.tile([P, 3 * unit], BF16, name="rounded1", offset=ROUNDED_AT * KIB, align_bytes=64)
-        apply_gain_to_pair(1, pair[:], rounded[:, 0 : 2 * unit])
+        apply_gain(nc.vector, bank_gain[:, 1, :], pair[:, 0, 0:GROUP, :], rounded[:, 0 : unit // 2])
+        scatter_early(0, ys, 2)
+        apply_gain(nc.gpsimd, gain[:, 1, :], pair[:, 0, GROUP:STEP, :], rounded[:, unit // 2 : unit])
+        apply_gain(nc.gpsimd, gain[:, 2, :], pair[:, 1], rounded[:, unit : 2 * unit])
         planes = last_planes(1)
         sums = keep.tile([P, STEP], F32, name="sums_early0", align_bytes=64)
         nc.scalar.copy(out=sums[:], in_=ys[2])
@@ -388,7 +393,7 @@ def tile_list_masked_patch_block_kernel(
         weighted = weigh(0, LAST, y_last, gate(1))
         groups = quantize_hidden("second_pair", rounded[:, 0 : 2 * unit], 2 * STEP, gate(1) + 7 * KIB // 4)
         last = quantize_hidden("second_last", rounded[:, 2 * unit : 3 * unit], STEP, gate(1) + 9 * KIB // 4)
-        hidden = [ahead, groups[0:2], groups[2:4], last]
+        hidden = [ahead, groups[0:1], groups[1:2], last]
         scatter_copy(0, LAST, weighted)
 
         ys = second_product(1, hidden, 3)
@@ -399,10 +404,12 @@ def tile_list_masked_patch_block_kernel(
         activate(2, 2, act)
         apply_gain(nc.gpsimd, gain[:, 2, :], act[:], rounded[:, 2 * unit : 3 * unit])
         planes = last_planes(2)
-        last_pair = act_pair(3, 0, LATER_ACTS_AT + 12)
+        last_pair = shared.tile([P, 2, STEP, PACK], F32, name="act_pair3", offset=LAST_PAIR_AT * KIB, align_bytes=64)
+        activate(0, 3, last_pair[:, 0])
         interleave(planes, rounded[:, 3 * unit : 4 * unit])
+        activate(1, 3, last_pair[:, 1])
         y_last = last_stripe(1, hidden)
-        weighted = weigh(1, LAST, y_last, gate(2))
+        weighted = weigh(1, LAST, y_last, gate(2) - KIB // 2)
         hidden = quantize_late(2, rounded)
         scatter_copy(1, LAST, weighted)
 

@@ -29,12 +29,19 @@ CHUNKS = S // STEP
 LANES = 16
 KIB = 1024
 
-ROUNDED_BY_VECTOR = [0, 128, 64, 80]
+ROUNDED_BY_VECTOR = [(0, 0), (0, 128), (0, 64), (48, 128)]
 UNITS_ON_SCALAR = [0, 1, 1, 2]
 AHEAD = 2
 SHORTCUT_AT = 2
-TURN_BANKS = [0, 1, 3, 4, 5, 6, 7]
-LAST_BANK = 2
+X_BANKS = [
+    [(0, 1), (4, 5), (6, 0), (1, 2)],
+    [(2, 3), (3, 4), (5, 1), (6, 3)],
+    [(4, 2), (0, 4), (2, 0), (6, 4)],
+    [(2, 0), (6, 4), (2, 0), (6, 4)],
+]
+Y_BANKS = [(2, 0), (3, 5), (0, 6), (3, 2, 5)]
+THIRD_STEPS = [[3, None, 0, 1, 2], [0, None, 3, 1, 2], [2, None, 3, 0, 1]]
+LAST_BANK = 7
 
 ROUNDED_AT = 0
 FIRST_ACTS_AT = [8, 12, 8, 46]
@@ -47,7 +54,7 @@ LAST_RAW_AT = 95
 FIRST_RAW_AT = 87
 SECOND_RAW_AT = 103
 GAIN_ROWS_AT = 79
-GATES_AT = [70, 32, 76]
+GATES_AT = [70, 32, 119]
 LAST_PAIR_AT = 111
 
 
@@ -67,11 +74,16 @@ def tile_list_masked_patch_block_kernel(
         table_scales = shared.tile(
             [P, T // 4], I32, name="table_scales", offset=TABLE_SCALES_AT * KIB, align_bytes=64
         )
-        raw = [keep.tile([P, PACK, P * PACK], F32, name=f"raw{a}", align_bytes=64) for a in range(2, LAST)]
-        for a in range(2):
-            place = [FIRST_RAW_AT, SECOND_RAW_AT][a]
-            raw.insert(a, shared.tile([P, PACK, P * PACK], F32, name=f"raw{a}", offset=place * KIB, align_bytes=64))
-        raw.append(shared.tile([P, PACK, P * PACK], F32, name="raw3", offset=LAST_RAW_AT * KIB, align_bytes=64))
+        def raw_piece(name, place, first, count):
+            tile = shared.tile([P, PACK, count * PACK], F32, name=name, offset=place * KIB, align_bytes=64)
+            return tile, first, count
+
+        raw = [
+            [raw_piece("raw0", FIRST_RAW_AT, 0, P)],
+            [raw_piece(f"raw1_{u}", SECOND_RAW_AT + 4 * u, u * P // 2, P // 2) for u in range(2)],
+            [raw_piece("raw2", FIRST_ACTS_AT[1], 0, P)],
+            [raw_piece("raw3_0", LAST_RAW_AT + 4, 0, P // 2), raw_piece("raw3_1", LAST_RAW_AT, P // 2, P // 2)],
+        ]
         gain_rows = shared.tile([P, P * PACK], F32, name="gain_rows", offset=GAIN_ROWS_AT * KIB, align_bytes=64)
         identity = keep.tile([P, P], F32, name="identity", align_bytes=64)
         gain = shared.tile([P, BANDS, PACK], F32, name="gain", offset=(TABLE_SCALES_AT + 1) * KIB)
@@ -103,10 +115,10 @@ def tile_list_masked_patch_block_kernel(
             nc.vector.memset(windows[n][:].bitcast(I32), 0)
         make_identity(nc, identity[:])
 
-        def load_w1(a, lo=0, hi=PACK):
-            cols = slice(a * P * PACK, (a + 1) * P * PACK)
-            rows = w1[:, cols].rearrange("(p j) c -> p j c", j=PACK)
-            nc.sync.dma_start(out=raw[a][:, lo:hi, :], in_=rows[:, lo:hi, :])
+        def load_w1(a, u=0):
+            tile, first, count = raw[a][u]
+            cols = slice((a * P + first) * PACK, (a * P + first + count) * PACK)
+            nc.sync.dma_start(out=tile[:], in_=w1[:, cols].rearrange("(p j) c -> p j c", j=PACK))
 
         nc.sync.dma_start(picks[:], offs)
         load_w1(0)
@@ -115,13 +127,14 @@ def tile_list_masked_patch_block_kernel(
         for r in range(4):
             nc.sync.dma_start(out=ws_plane[r:P:32, :], in_=ws_scales[0, r:16:4, :].bitcast(I32))
         nc.sync.dma_start(out=table[:], in_=tab_words[0].rearrange("p t i -> p (t i)").bitcast(I32))
-        load_w1(1, 0, 2)
+        load_w1(1, 0)
         nc.vector.tensor_copy(spread_scales[:], table_scales[:].bitcast(U8).indirect(picks[:]))
         for r in range(4):
             nc.sync.dma_start(out=v_scales[r:P:32, :].bitcast(I32), in_=spread_scales[8 * r : P : 32, :].bitcast(I32))
-        load_w1(1, 2, PACK)
+        load_w1(1, 1)
         load_w1(2)
-        load_w1(LAST)
+        load_w1(LAST, 0)
+        load_w1(LAST, 1)
         for r in range(4):
             nc.sync.dma_start(
                 out=out_scales[r:P:32, 0:BANDS, :],
@@ -149,12 +162,13 @@ def tile_list_masked_patch_block_kernel(
             else:
                 rounded = ring.tile([P, P * PACK * PACK], BF16, name="w1_rounded", bufs=2, align_bytes=64)
             dst = rounded[:].rearrange("p (t m j) -> p m j t", t=PACK, j=PACK)
-            src = raw[a][:].rearrange("p j (m t) -> p m j t", t=PACK)
-            split = ROUNDED_BY_VECTOR[a]
-            if split > 0:
-                nc.vector.tensor_copy(out=dst[:, 0:split], in_=src[:, 0:split])
-            if split < P:
-                nc.scalar.copy(out=dst[:, split:P], in_=src[:, split:P])
+            lo, hi = ROUNDED_BY_VECTOR[a]
+            for tile, first, count in raw[a]:
+                src = tile[:].rearrange("p j (m t) -> p m j t", t=PACK)
+                cuts = sorted({first, first + count, min(max(lo, first), first + count), min(max(hi, first), first + count)})
+                for start, stop in zip(cuts, cuts[1:]):
+                    copy = nc.vector.tensor_copy if lo <= start < hi else nc.scalar.copy
+                    copy(out=dst[:, start:stop], in_=src[:, start - first : stop - first])
             nc.vector.quantize_mx(out=w1_codes[a][:].bitcast(FP8X4), scales=w1_scales[a][:], in_=rounded[:])
 
         def first_product(a, t, first, count, dst):
@@ -176,15 +190,9 @@ def tile_list_masked_patch_block_kernel(
             tenants.append(k)
             return psum.tile([P, HALF], F32, name=f"bank{len(tenants)}", offset=k * 2 * KIB)
 
-        turns = []
-
-        def next_bank():
-            turns.append(TURN_BANKS[len(turns) % len(TURN_BANKS)])
-            return bank(turns[-1])
-
         def activate(a, c, act):
             for lo in range(0, STEP, GROUP):
-                x = next_bank()
+                x = bank(X_BANKS[c][a][lo // GROUP])
                 for t in range(PACK):
                     first_product(a, t, c * STEP + lo, GROUP, x[:, t * GROUP : (t + 1) * GROUP])
                 nc.scalar.activation(
@@ -201,7 +209,7 @@ def tile_list_masked_patch_block_kernel(
 
         def hidden_on_scalar(a, c, planes):
             for pair in range(2):
-                x = next_bank()
+                x = bank(X_BANKS[c][a][pair])
                 for u in range(2):
                     first_product(a, 2 * pair + u, c * STEP, STEP, x[:, u * STEP : (u + 1) * STEP])
                 act = ring.tile([P, 2 * STEP], F32, name="act_planes", bufs=2, align_bytes=64)
@@ -251,9 +259,10 @@ def tile_list_masked_patch_block_kernel(
                     stop=closes and lo + width == STEP,
                 )
 
-        def accumulate(c, hidden, groups, turn=0):
+        def accumulate(c, hidden, groups, turn=0, steps=None):
             bands = [(turn + i) % BANDS for i in range(BANDS)]
-            steps = [bands[0], None] + bands[1:] if c == 0 else [None] + bands
+            if steps is None:
+                steps = [bands[0], None] + bands[1:] if c == 0 else [None] + bands
             for a in steps:
                 for stripes in groups:
                     for i, (n, dst) in enumerate(stripes):
@@ -264,10 +273,10 @@ def tile_list_masked_patch_block_kernel(
                             band_passes(n, a, hidden, dst, opens, a == steps[-1] and i == len(stripes) - 1)
 
         def second_product(c, hidden, turn):
-            banks = [next_bank() for k in range(2)]
+            banks = [bank(k) for k in Y_BANKS[c]]
             ys = [banks[n // 2][:, n % 2 * STEP : (n % 2 + 1) * STEP] for n in range(LAST)]
             accumulate(c, hidden, [[(0, ys[0]), (1, ys[1])]])
-            accumulate(c, hidden, [[(2, ys[2])]], turn)
+            accumulate(c, hidden, [[(2, ys[2])]], 0, THIRD_STEPS[c])
             return ys
 
         def gate(c):
@@ -278,6 +287,8 @@ def tile_list_masked_patch_block_kernel(
             for u in range(2):
                 width = 2 * STEP * PACK
                 offset = gate(c) + 2 * KIB + (2 * u - 1) * KIB // 4
+                if c - u == 2:
+                    offset = gate(c) - KIB
                 half = rounded[:, u * width : (u + 1) * width]
                 groups = quantize_hidden(f"late{c}_{u}", half, 2 * STEP, offset)
                 hidden.extend([groups[0:1], groups[1:2]])
@@ -344,7 +355,7 @@ def tile_list_masked_patch_block_kernel(
             quantize_w1(a)
 
         rounded_first = shared.tile(
-            [P, unit], BF16, name="h_rounded_first", offset=SECOND_RAW_AT * KIB, align_bytes=64
+            [P, unit], BF16, name="h_rounded_first", offset=(SECOND_RAW_AT + 4) * KIB, align_bytes=64
         )
         rounded_middle = shared.tile(
             [P, 2 * unit], BF16, name="h_rounded_middle", offset=LAST_RAW_AT * KIB, align_bytes=64
@@ -413,27 +424,27 @@ def tile_list_masked_patch_block_kernel(
         hidden = quantize_late(2, rounded)
         scatter_copy(1, LAST, weighted)
 
+        third_planes = keep.tile([P, PACK, STEP], BF16, name="third_planes", align_bytes=64)
+        hidden_on_scalar(2, 3, third_planes)
+        planes = last_planes(3)
         ys = second_product(2, hidden, 2)
         scatter_early(2, ys, 2)
         rounded = shared.tile([P, BANDS * unit], BF16, name="rounded3", offset=ROUNDED_AT * KIB, align_bytes=64)
         apply_gain_to_pair(0, last_pair[:], rounded[:, 0 : 2 * unit])
-        third_planes = keep.tile([P, PACK, STEP], BF16, name="third_planes", align_bytes=64)
-        hidden_on_scalar(2, 3, third_planes)
-        planes = last_planes(3)
         interleave(third_planes, rounded[:, 2 * unit : 3 * unit])
         interleave(planes, rounded[:, 3 * unit : 4 * unit])
 
         c = CHUNKS - 1
         held = STRIPES - 2
-        joint = bank(LAST_BANK)
+        joint = bank(X_BANKS[3][LAST][1])
         accumulate(c - 1, hidden, [[(LAST, joint[:, 0:STEP])]])
         hidden = quantize_late(c, rounded)
-        sums = shared.tile([P, STEP], F32, name="sums_held", offset=gate(c), align_bytes=64)
+        sums = shared.tile([P, STEP], F32, name="sums_held", offset=gate(c) - KIB // 2, align_bytes=64)
         nc.scalar.copy(out=sums[:], in_=ys[held])
         scatter_weighted(held, (c - 1) * STEP, STEP, sums)
         for n in range(STRIPES):
             if n < LAST:
-                y = next_bank()
+                y = bank(Y_BANKS[c][n])
                 accumulate(c, hidden, [[(n, y[:, 0:STEP])]], 2 if n > 0 else 0)
                 sums = keep.tile([P, STEP], F32, name=f"sums{n}", align_bytes=64)
                 nc.scalar.copy(out=sums[:], in_=y[:, 0:STEP])

@@ -30,9 +30,7 @@ LANES = 16
 KIB = 1024
 
 ROUNDED_BY_VECTOR = [(0, 0), (0, 128), (0, 64), (48, 128)]
-UNITS_ON_SCALAR = [0, 1, 1, 2]
-AHEAD = 2
-SHORTCUT_AT = 2
+
 X_BANKS = [
     [(0, 1), (4, 5), (6, 0), (1, 2)],
     [(2, 3), (3, 4), (5, 1), (6, 3)],
@@ -46,16 +44,16 @@ LAST_BANK = 7
 ROUNDED_AT = 0
 FIRST_ACTS_AT = [8, 12, 8, 46]
 SECOND_ACTS_AT = [32, 12]
-LAST_W1_AT = 66
-LATER_ACTS_AT = 20
+THIRD_ACTS_AT = 20
+LAST_PAIR_AT = 111
+GATES_AT = [70, 32, 119]
 LAST_WINDOW_AT = 52
 TABLE_SCALES_AT = 60
-LAST_RAW_AT = 95
-FIRST_RAW_AT = 87
-SECOND_RAW_AT = 103
+LAST_W1_AT = 66
 GAIN_ROWS_AT = 79
-GATES_AT = [70, 32, 119]
-LAST_PAIR_AT = 111
+FIRST_RAW_AT = 87
+LAST_RAW_AT = 95
+SECOND_RAW_AT = 103
 
 
 def tile_list_masked_patch_block_kernel(
@@ -64,7 +62,7 @@ def tile_list_masked_patch_block_kernel(
     nc = tc.nc
     with ExitStack() as ctx:
         keep = ctx.enter_context(tc.tile_pool(name="keep", bufs=1))
-        ring = ctx.enter_context(tc.tile_pool(name="ring", bufs=3))
+        ring = ctx.enter_context(tc.tile_pool(name="ring", bufs=2))
         shared = ctx.enter_context(tc.tile_pool(name="shared", bufs=1))
         psum = ctx.enter_context(tc.psum_pool(name="psum", bufs=1))
 
@@ -74,6 +72,7 @@ def tile_list_masked_patch_block_kernel(
         table_scales = shared.tile(
             [P, T // 4], I32, name="table_scales", offset=TABLE_SCALES_AT * KIB, align_bytes=64
         )
+
         def raw_piece(name, place, first, count):
             tile = shared.tile([P, PACK, count * PACK], F32, name=name, offset=place * KIB, align_bytes=64)
             return tile, first, count
@@ -93,10 +92,7 @@ def tile_list_masked_patch_block_kernel(
         ws_plane = keep.tile([P, N // 4], I32, name="ws_plane", align_bytes=64)
         weight = keep.tile([P, S], F32, name="weight", align_bytes=64)
         windows = [keep.tile([P, T2], F32, name=f"window{n}", align_bytes=64) for n in range(2)]
-        v_codes = [
-            keep.tile([P, HALF], U32, name="v_codes0", align_bytes=64),
-            keep.tile([P, HALF], U32, name="v_codes1", align_bytes=64),
-        ]
+        v_codes = [keep.tile([P, HALF], U32, name=f"v_codes{i}", align_bytes=64) for i in range(S // HALF)]
         spread_scales = keep.tile([P, S], U8, name="spread_scales", align_bytes=64)
         v_scales = keep.tile([P, S], U8, name="v_scales", align_bytes=64)
         w1_codes = [keep.tile([P, P * PACK], U32, name=f"w1_codes{a}", align_bytes=64) for a in range(BANDS)]
@@ -160,12 +156,12 @@ def tile_list_masked_patch_block_kernel(
                     [P, P * PACK * PACK], BF16, name=f"w1_rounded{a}", offset=place * KIB, align_bytes=64
                 )
             else:
-                rounded = ring.tile([P, P * PACK * PACK], BF16, name="w1_rounded", bufs=2, align_bytes=64)
+                rounded = ring.tile([P, P * PACK * PACK], BF16, name="w1_rounded", align_bytes=64)
             dst = rounded[:].rearrange("p (t m j) -> p m j t", t=PACK, j=PACK)
             lo, hi = ROUNDED_BY_VECTOR[a]
             for tile, first, count in raw[a]:
                 src = tile[:].rearrange("p j (m t) -> p m j t", t=PACK)
-                cuts = sorted({first, first + count, min(max(lo, first), first + count), min(max(hi, first), first + count)})
+                cuts = sorted({min(max(cut, first), first + count) for cut in (0, lo, hi, P)})
                 for start, stop in zip(cuts, cuts[1:]):
                     copy = nc.vector.tensor_copy if lo <= start < hi else nc.scalar.copy
                     copy(out=dst[:, start:stop], in_=src[:, start - first : stop - first])
@@ -212,16 +208,18 @@ def tile_list_masked_patch_block_kernel(
                 x = bank(X_BANKS[c][a][pair])
                 for u in range(2):
                     first_product(a, 2 * pair + u, c * STEP, STEP, x[:, u * STEP : (u + 1) * STEP])
-                act = ring.tile([P, 2 * STEP], F32, name="act_planes", bufs=2, align_bytes=64)
+                act = ring.tile([P, 2 * STEP], F32, name="act_planes", align_bytes=64)
                 nc.scalar.activation(act[:], x[:], ACT.Gelu_apprx_sigmoid)
                 for u in range(2):
                     t = 2 * pair + u
                     nc.scalar.activation(
-                        planes[:, t, :], act[:, u * STEP : (u + 1) * STEP], ACT.Copy, scale=gain[:, a, t : t + 1]
+                        planes[:, pair, :, u], act[:, u * STEP : (u + 1) * STEP], ACT.Copy, scale=gain[:, a, t : t + 1]
                     )
 
         def interleave(planes, rounded):
-            nc.scalar.copy(out=rounded.rearrange("p (j t) -> p j t", t=PACK), in_=planes[:].rearrange("p t j -> p j t"))
+            words = planes[:].rearrange("p u j t -> p u (j t)").bitcast(U32)
+            dst = rounded.bitcast(U32).rearrange("p (j u) -> p j u", u=2)
+            nc.scalar.copy(out=dst, in_=words.rearrange("p u j -> p j u"))
 
         def quantize_hidden(name, rounded, count, offset=None):
             codes = keep.tile([P, count], U32, name=f"h_codes{name}", align_bytes=64)
@@ -259,38 +257,43 @@ def tile_list_masked_patch_block_kernel(
                     stop=closes and lo + width == STEP,
                 )
 
-        def accumulate(c, hidden, groups, turn=0, steps=None):
-            bands = [(turn + i) % BANDS for i in range(BANDS)]
+        def accumulate(c, hidden, stripes, steps=None):
             if steps is None:
-                steps = [bands[0], None] + bands[1:] if c == 0 else [None] + bands
+                steps = [0, None, 1, 2, 3] if c == 0 else [None, 0, 1, 2, 3]
             for a in steps:
-                for stripes in groups:
-                    for i, (n, dst) in enumerate(stripes):
-                        opens = a == steps[0] and i == 0
-                        if a is None:
-                            shortcut_pass(n, c, dst, opens)
-                        else:
-                            band_passes(n, a, hidden, dst, opens, a == steps[-1] and i == len(stripes) - 1)
+                for i, (n, dst) in enumerate(stripes):
+                    opens = a == steps[0] and i == 0
+                    if a is None:
+                        shortcut_pass(n, c, dst, opens)
+                    else:
+                        band_passes(n, a, hidden, dst, opens, a == steps[-1] and i == len(stripes) - 1)
 
-        def second_product(c, hidden, turn):
+        def second_product(c, hidden):
             banks = [bank(k) for k in Y_BANKS[c]]
             ys = [banks[n // 2][:, n % 2 * STEP : (n % 2 + 1) * STEP] for n in range(LAST)]
-            accumulate(c, hidden, [[(0, ys[0]), (1, ys[1])]])
-            accumulate(c, hidden, [[(2, ys[2])]], 0, THIRD_STEPS[c])
+            accumulate(c, hidden, [(0, ys[0]), (1, ys[1])])
+            accumulate(c, hidden, [(2, ys[2])], THIRD_STEPS[c])
             return ys
+
+        unit = STEP * PACK
 
         def gate(c):
             return GATES_AT[c - 1] * KIB
 
-        def quantize_late(c, rounded):
+        def on_planes(c):
+            return gate(c) + 2 * KIB - KIB // 4
+
+        def on_weighted(c):
+            return gate(c) + 2 * KIB + KIB // 4
+
+        def on_last_act(c):
+            return gate(c) - KIB
+
+        def quantize_late(c, rounded, offsets):
             hidden = []
             for u in range(2):
-                width = 2 * STEP * PACK
-                offset = gate(c) + 2 * KIB + (2 * u - 1) * KIB // 4
-                if c - u == 2:
-                    offset = gate(c) - KIB
-                half = rounded[:, u * width : (u + 1) * width]
-                groups = quantize_hidden(f"late{c}_{u}", half, 2 * STEP, offset)
+                half = rounded[:, 2 * u * unit : 2 * (u + 1) * unit]
+                groups = quantize_hidden(f"late{c}_{u}", half, 2 * STEP, offsets[u])
                 hidden.extend([groups[0:1], groups[1:2]])
             return hidden
 
@@ -302,7 +305,7 @@ def tile_list_masked_patch_block_kernel(
 
         def weigh(c, n, y, offset=None):
             if offset is None:
-                weighted = ring.tile([P, STEP], F32, name="weighted", bufs=2, align_bytes=64)
+                weighted = ring.tile([P, STEP], F32, name="weighted", align_bytes=64)
             else:
                 weighted = shared.tile([P, STEP], F32, name=f"weighted{c}_{n}", offset=offset, align_bytes=64)
             nc.vector.tensor_tensor(weighted[:], y, weight[:, c * STEP : (c + 1) * STEP], MULT)
@@ -316,8 +319,6 @@ def tile_list_masked_patch_block_kernel(
                 windows[n][:].indirect(places(first, count)), sums[:], weight[:, first : first + count], MULT
             )
 
-        unit = STEP * PACK
-
         def act_pair(c, a, place):
             pair = shared.tile([P, 2, STEP, PACK], F32, name=f"act_pair{c}", offset=place * KIB, align_bytes=64)
             for u in range(2):
@@ -325,7 +326,7 @@ def tile_list_masked_patch_block_kernel(
             return pair
 
         def last_planes(c):
-            planes = shared.tile([P, PACK, STEP], BF16, name=f"planes{c}", offset=gate(c), align_bytes=64)
+            planes = shared.tile([P, 2, STEP, 2], BF16, name=f"planes{c}", offset=gate(c), align_bytes=64)
             hidden_on_scalar(LAST, c, planes)
             return planes
 
@@ -336,7 +337,7 @@ def tile_list_masked_patch_block_kernel(
 
         def last_stripe(c, hidden):
             y = bank(LAST_BANK)[:, 0:STEP]
-            accumulate(c, hidden, [[(LAST, y)]])
+            accumulate(c, hidden, [(LAST, y)])
             return y
 
         quantize_w1(0)
@@ -386,7 +387,7 @@ def tile_list_masked_patch_block_kernel(
         ahead = quantize_hidden("ahead", rounded_ahead[:], STEP, FIRST_ACTS_AT[LAST] * KIB)
 
         pair = act_pair(1, 1, SECOND_ACTS_AT[1])
-        ys = second_product(0, hidden, 3)
+        ys = second_product(0, hidden)
         rounded = shared.tile([P, 3 * unit], BF16, name="rounded1", offset=ROUNDED_AT * KIB, align_bytes=64)
         apply_gain(nc.vector, bank_gain[:, 1, :], pair[:, 0, 0:GROUP, :], rounded[:, 0 : unit // 2])
         scatter_early(0, ys, 2)
@@ -396,22 +397,22 @@ def tile_list_masked_patch_block_kernel(
         sums = keep.tile([P, STEP], F32, name="sums_early0", align_bytes=64)
         nc.scalar.copy(out=sums[:], in_=ys[2])
         scatter_weighted(2, 0 * STEP, STEP, sums)
-        pair = shared.tile([P, 2, STEP, PACK], F32, name="act_pair2", offset=LATER_ACTS_AT * KIB, align_bytes=64)
+        pair = shared.tile([P, 2, STEP, PACK], F32, name="act_pair2", offset=THIRD_ACTS_AT * KIB, align_bytes=64)
         activate(0, 2, pair[:, 0])
         interleave(planes, rounded[:, 2 * unit : 3 * unit])
         activate(1, 2, pair[:, 1])
         y_last = last_stripe(0, hidden)
         weighted = weigh(0, LAST, y_last, gate(1))
-        groups = quantize_hidden("second_pair", rounded[:, 0 : 2 * unit], 2 * STEP, gate(1) + 7 * KIB // 4)
-        last = quantize_hidden("second_last", rounded[:, 2 * unit : 3 * unit], STEP, gate(1) + 9 * KIB // 4)
+        groups = quantize_hidden("second_pair", rounded[:, 0 : 2 * unit], 2 * STEP, on_planes(1))
+        last = quantize_hidden("second_last", rounded[:, 2 * unit : 3 * unit], STEP, on_weighted(1))
         hidden = [ahead, groups[0:1], groups[1:2], last]
         scatter_copy(0, LAST, weighted)
 
-        ys = second_product(1, hidden, 3)
+        ys = second_product(1, hidden)
         scatter_early(1, ys, LAST)
         rounded = shared.tile([P, BANDS * unit], BF16, name="rounded2", offset=ROUNDED_AT * KIB, align_bytes=64)
         apply_gain_to_pair(0, pair[:], rounded[:, 0 : 2 * unit])
-        act = act_tile(2, 2, LATER_ACTS_AT + 8)
+        act = act_tile(2, 2, THIRD_ACTS_AT + 8)
         activate(2, 2, act)
         apply_gain(nc.gpsimd, gain[:, 2, :], act[:], rounded[:, 2 * unit : 3 * unit])
         planes = last_planes(2)
@@ -421,13 +422,13 @@ def tile_list_masked_patch_block_kernel(
         activate(1, 3, last_pair[:, 1])
         y_last = last_stripe(1, hidden)
         weighted = weigh(1, LAST, y_last, gate(2) - KIB // 2)
-        hidden = quantize_late(2, rounded)
+        hidden = quantize_late(2, rounded, [on_last_act(2), on_weighted(2)])
         scatter_copy(1, LAST, weighted)
 
-        third_planes = keep.tile([P, PACK, STEP], BF16, name="third_planes", align_bytes=64)
+        third_planes = keep.tile([P, 2, STEP, 2], BF16, name="third_planes", align_bytes=64)
         hidden_on_scalar(2, 3, third_planes)
         planes = last_planes(3)
-        ys = second_product(2, hidden, 2)
+        ys = second_product(2, hidden)
         scatter_early(2, ys, 2)
         rounded = shared.tile([P, BANDS * unit], BF16, name="rounded3", offset=ROUNDED_AT * KIB, align_bytes=64)
         apply_gain_to_pair(0, last_pair[:], rounded[:, 0 : 2 * unit])
@@ -436,21 +437,22 @@ def tile_list_masked_patch_block_kernel(
 
         c = CHUNKS - 1
         held = STRIPES - 2
+        later_steps = [None, 2, 3, 0, 1]
         joint = bank(X_BANKS[3][LAST][1])
-        accumulate(c - 1, hidden, [[(LAST, joint[:, 0:STEP])]])
-        hidden = quantize_late(c, rounded)
+        accumulate(c - 1, hidden, [(LAST, joint[:, 0:STEP])])
+        hidden = quantize_late(c, rounded, [on_planes(c), on_last_act(c)])
         sums = shared.tile([P, STEP], F32, name="sums_held", offset=gate(c) - KIB // 2, align_bytes=64)
         nc.scalar.copy(out=sums[:], in_=ys[held])
         scatter_weighted(held, (c - 1) * STEP, STEP, sums)
         for n in range(STRIPES):
             if n < LAST:
                 y = bank(Y_BANKS[c][n])
-                accumulate(c, hidden, [[(n, y[:, 0:STEP])]], 2 if n > 0 else 0)
+                accumulate(c, hidden, [(n, y[:, 0:STEP])], later_steps if n > 0 else None)
                 sums = keep.tile([P, STEP], F32, name=f"sums{n}", align_bytes=64)
                 nc.scalar.copy(out=sums[:], in_=y[:, 0:STEP])
                 scatter_weighted(n, c * STEP, STEP, sums)
             else:
-                accumulate(c, hidden, [[(n, joint[:, STEP:HALF])]], 2)
+                accumulate(c, hidden, [(n, joint[:, STEP:HALF])], later_steps)
                 sums = keep.tile([P, HALF], F32, name=f"sums{n}", align_bytes=64)
                 nc.scalar.copy(out=sums[:], in_=joint[:])
                 scatter_weighted(n, (c - 1) * STEP, HALF, sums)

from contextlib import ExitStack

import concourse.mybir as mybir
from concourse.masks import make_identity

K, H, N, T, S, T2 = 512, 2048, 512, 4096, 1024, 2048
FLOPS = 2 * S * (K * H + H * N + K * N)

F32 = mybir.dt.float32
BF16 = mybir.dt.bfloat16
I32 = mybir.dt.int32
U32 = mybir.dt.uint32
U16 = mybir.dt.uint16
U8 = mybir.dt.uint8
FP8X4 = mybir.dt.float8_e4m3fn_x4
FP4X4 = mybir.dt.float4_e2m1fn_x4
ACT = mybir.ActivationFunctionType
MULT = mybir.AluOpType.mult

P = 128
PACK = 4
BANDS = H // (P * PACK)
STRIPES = N // P
LAST = BANDS - 1
GROUP = 128
HALF = 512
STEP = 256
CHUNKS = S // STEP
LANES = 16
KIB = 1024

ROUNDED_BY_VECTOR = [(0, 0), (0, 128), (0, 64), (48, 128)]

X_BANKS = [
    [(0, 1), (4, 5), (6, 0), (1, 2)],
    [(2, 3), (3, 4), (5, 1), (6, 3)],
    [(4, 2), (0, 4), (2, 0), (6, 4)],
    [(2, 0), (6, 4), (2, 0), (6, 4)],
]
Y_BANKS = [(2, 0), (3, 5), (0, 6), (3, 2, 5)]
THIRD_STEPS = [[3, None, 0, 1, 2], [0, None, 3, 1, 2], [2, None, 3, 0, 1]]
LAST_BANK = 7

ROUNDED_AT = 0
FIRST_ACTS_AT = [8, 12, 8, 46]
SECOND_ACTS_AT = [32, 12]
THIRD_ACTS_AT = 20
LAST_PAIR_AT = 111
GATES_AT = [70, 32, 119]
LAST_WINDOW_AT = 52
TABLE_SCALES_AT = 60
LAST_W1_AT = 66
GAIN_ROWS_AT = 79
FIRST_RAW_AT = 87
LAST_RAW_AT = 95
SECOND_RAW_AT = 103


def tile_list_masked_patch_block_kernel(
    tc, tab_words, tab_scales, offs, w1, ga, w2_words, w2_scales, ws_words, ws_scales, wgo, offs2, out
):
    nc = tc.nc
    with ExitStack() as ctx:
        keep = ctx.enter_context(tc.tile_pool(name="keep", bufs=1))
        ring = ctx.enter_context(tc.tile_pool(name="ring", bufs=2))
        shared = ctx.enter_context(tc.tile_pool(name="shared", bufs=1))
        psum = ctx.enter_context(tc.psum_pool(name="psum", bufs=1))

        picks = keep.tile([P, S // LANES], U16, name="picks")
        slots = keep.tile([P, S // LANES], U16, name="slots")
        table = keep.tile([P, T], I32, name="table", align_bytes=64)
        table_scales = shared.tile(
            [P, T // 4], I32, name="table_scales", offset=TABLE_SCALES_AT * KIB, align_bytes=64
        )

        def raw_piece(name, place, first, count):
            tile = shared.tile([P, PACK, count * PACK], F32, name=name, offset=place * KIB, align_bytes=64)
            return tile, first, count

        raw = [
            [raw_piece("raw0", FIRST_RAW_AT, 0, P)],
            [raw_piece(f"raw1_{u}", SECOND_RAW_AT + 4 * u, u * P // 2, P // 2) for u in range(2)],
            [raw_piece("raw2", FIRST_ACTS_AT[1], 0, P)],
            [raw_piece("raw3_0", LAST_RAW_AT + 4, 0, P // 2), raw_piece("raw3_1", LAST_RAW_AT, P // 2, P // 2)],
        ]
        gain_rows = shared.tile([P, P * PACK], F32, name="gain_rows", offset=GAIN_ROWS_AT * KIB, align_bytes=64)
        identity = keep.tile([P, P], F32, name="identity", align_bytes=64)
        gain = shared.tile([P, BANDS, PACK], F32, name="gain", offset=(TABLE_SCALES_AT + 1) * KIB)
        w2_codes = keep.tile([P, BANDS, 2 * N], U8, name="w2_codes", align_bytes=64)
        ws_codes = keep.tile([P, N], I32, name="ws_codes", align_bytes=64)
        out_scales = keep.tile([P, BANDS, N // 4], I32, name="out_scales", align_bytes=64)
        ws_plane = keep.tile([P, N // 4], I32, name="ws_plane", align_bytes=64)
        weight = keep.tile([P, S], F32, name="weight", align_bytes=64)
        windows = [keep.tile([P, T2], F32, name=f"window{n}", align_bytes=64) for n in range(2)]
        v_codes = [keep.tile([P, HALF], U32, name=f"v_codes{i}", align_bytes=64) for i in range(S // HALF)]
        spread_scales = keep.tile([P, S], U8, name="spread_scales", align_bytes=64)
        v_scales = keep.tile([P, S], U8, name="v_scales", align_bytes=64)
        w1_codes = [keep.tile([P, P * PACK], U32, name=f"w1_codes{a}", align_bytes=64) for a in range(BANDS)]
        w1_scales = [
            shared.tile([P, P * PACK], U8, name="w1_scales0", offset=TABLE_SCALES_AT * KIB, align_bytes=64)
        ]
        for a in range(1, BANDS):
            w1_scales.append(keep.tile([P, P * PACK], U8, name=f"w1_scales{a}", align_bytes=64))

        nc.vector.memset(table_scales[:], 0)
        nc.vector.memset(gain_rows[:], 0.0)
        nc.vector.memset(ws_plane[:], 0)
        nc.vector.memset(v_scales[:].bitcast(I32), 0)
        nc.vector.memset(out_scales[:], 0)
        for n in range(2):
            nc.vector.memset(windows[n][:].bitcast(I32), 0)
        make_identity(nc, identity[:])

        def load_w1(a, u=0):
            tile, first, count = raw[a][u]
            cols = slice((a * P + first) * PACK, (a * P + first + count) * PACK)
            nc.sync.dma_start(out=tile[:], in_=w1[:, cols].rearrange("(p j) c -> p j c", j=PACK))

        nc.sync.dma_start(picks[:], offs)
        load_w1(0)
        nc.sync.dma_start(out=gain_rows[0 : 4 * BANDS : 4, :], in_=ga.rearrange("(a c) -> a c", a=BANDS))
        nc.sync.dma_start(out=table_scales[0:P:8, :], in_=tab_scales[0].bitcast(I32))
        for r in range(4):
            nc.sync.dma_start(out=ws_plane[r:P:32, :], in_=ws_scales[0, r:16:4, :].bitcast(I32))
        nc.sync.dma_start(out=table[:], in_=tab_words[0].rearrange("p t i -> p (t i)").bitcast(I32))
        load_w1(1, 0)
        nc.vector.tensor_copy(spread_scales[:], table_scales[:].bitcast(U8).indirect(picks[:]))
        for r in range(4):
            nc.sync.dma_start(out=v_scales[r:P:32, :].bitcast(I32), in_=spread_scales[8 * r : P : 32, :].bitcast(I32))
        load_w1(1, 1)
        load_w1(2)
        load_w1(LAST, 0)
        load_w1(LAST, 1)
        for r in range(4):
            nc.sync.dma_start(
                out=out_scales[r:P:32, 0:BANDS, :],
                in_=w2_scales[:, r:16:4, :].rearrange("a q c -> q a c").bitcast(I32),
            )
        nc.sync.dma_start(out=w2_codes[:].bitcast(I32), in_=w2_words.rearrange("a p c -> p a c").bitcast(I32))
        nc.sync.dma_start(out=ws_codes[:], in_=ws_words[0].rearrange("p c i -> p (c i)").bitcast(I32))
        nc.sync.dma_start(out=weight[:], in_=wgo)
        nc.sync.dma_start(slots[:], offs2)

        def gather_codes(i):
            cols = slice(i * HALF // LANES, (i + 1) * HALF // LANES)
            nc.vector.tensor_copy(v_codes[i][:], table[:].bitcast(U32).indirect(picks[:, cols]))

        def patch(first, count):
            i, lo = divmod(first, HALF)
            return v_codes[i][:, lo : lo + count].bitcast(FP8X4), v_scales[:, first : first + count]

        def quantize_w1(a):
            if a == 0 or a == LAST:
                place = LAST_WINDOW_AT if a == 0 else LAST_W1_AT
                rounded = shared.tile(
                    [P, P * PACK * PACK], BF16, name=f"w1_rounded{a}", offset=place * KIB, align_bytes=64
                )
            else:
                rounded = ring.tile([P, P * PACK * PACK], BF16, name="w1_rounded", align_bytes=64)
            dst = rounded[:].rearrange("p (t m j) -> p m j t", t=PACK, j=PACK)
            lo, hi = ROUNDED_BY_VECTOR[a]
            for tile, first, count in raw[a]:
                src = tile[:].rearrange("p j (m t) -> p m j t", t=PACK)
                cuts = sorted({min(max(cut, first), first + count) for cut in (0, lo, hi, P)})
                for start, stop in zip(cuts, cuts[1:]):
                    copy = nc.vector.tensor_copy if lo <= start < hi else nc.scalar.copy
                    copy(out=dst[:, start:stop], in_=src[:, start - first : stop - first])
            nc.vector.quantize_mx(out=w1_codes[a][:].bitcast(FP8X4), scales=w1_scales[a][:], in_=rounded[:])

        def first_product(a, t, first, count, dst):
            codes, scales = patch(first, count)
            cols = slice(t * P, (t + 1) * P)
            nc.tensor.matmul_mx(
                out=dst,
                lhsT=w1_codes[a][:, cols].bitcast(FP8X4),
                lhsT_scale=w1_scales[a][:, cols],
                rhs=codes,
                rhs_scale=scales,
                start=True,
                stop=True,
            )

        tenants = []

        def bank(k):
            tenants.append(k)
            return psum.tile([P, HALF], F32, name=f"bank{len(tenants)}", offset=k * 2 * KIB)

        def activate(a, c, act):
            for lo in range(0, STEP, GROUP):
                x = bank(X_BANKS[c][a][lo // GROUP])
                for t in range(PACK):
                    first_product(a, t, c * STEP + lo, GROUP, x[:, t * GROUP : (t + 1) * GROUP])
                nc.scalar.activation(
                    act[:, lo : lo + GROUP, :], x[:].rearrange("p (t j) -> p j t", t=PACK), ACT.Gelu_apprx_sigmoid
                )

        def apply_gain(engine, gains, act, rounded):
            gains = gains.unsqueeze(1).to_broadcast(list(act.shape))
            engine.tensor_tensor(rounded.rearrange("p (j t) -> p j t", t=PACK), act, gains, MULT)

        def apply_gain_to_pair(a, pair, rounded):
            gains = gain[:, a : a + 2, :].unsqueeze(2).to_broadcast([P, 2, STEP, PACK])
            nc.gpsimd.tensor_tensor(rounded.rearrange("p (a j t) -> p a j t", a=2, t=PACK), pair, gains, MULT)

        def hidden_on_scalar(a, c, planes):
            for pair in range(2):
                x = bank(X_BANKS[c][a][pair])
                for u in range(2):
                    first_product(a, 2 * pair + u, c * STEP, STEP, x[:, u * STEP : (u + 1) * STEP])
                act = ring.tile([P, 2 * STEP], F32, name="act_planes", align_bytes=64)
                nc.scalar.activation(act[:], x[:], ACT.Gelu_apprx_sigmoid)
                for u in range(2):
                    t = 2 * pair + u
                    nc.scalar.activation(
                        planes[:, pair, :, u], act[:, u * STEP : (u + 1) * STEP], ACT.Copy, scale=gain[:, a, t : t + 1]
                    )

        def interleave(planes, rounded):
            words = planes[:].rearrange("p u j t -> p u (j t)").bitcast(U32)
            dst = rounded.bitcast(U32).rearrange("p (j u) -> p j u", u=2)
            nc.scalar.copy(out=dst, in_=words.rearrange("p u j -> p j u"))

        def quantize_hidden(name, rounded, count, offset=None):
            codes = keep.tile([P, count], U32, name=f"h_codes{name}", align_bytes=64)
            if offset is None:
                scales = keep.tile([P, count], U8, name=f"h_scales{name}", align_bytes=64)
            else:
                scales = shared.tile([P, count], U8, name=f"h_scales{name}", offset=offset, align_bytes=64)
            nc.vector.quantize_mx(out=codes[:].bitcast(FP8X4), scales=scales[:], in_=rounded)
            width = min(count, STEP)
            return [(codes[:, lo : lo + width], scales[:, lo : lo + width]) for lo in range(0, count, width)]

        def shortcut_pass(n, c, dst, start):
            codes, scales = patch(c * STEP, STEP)
            nc.tensor.matmul_mx(
                out=dst,
                lhsT=ws_codes[:, n * P : (n + 1) * P].bitcast(FP8X4),
                lhsT_scale=ws_plane[:].bitcast(U8)[:, n * P : (n + 1) * P],
                rhs=codes,
                rhs_scale=scales,
                start=start,
                stop=False,
            )

        def band_passes(n, a, hidden, dst, opens, closes):
            width = STEP // len(hidden[a])
            for lo in range(0, STEP, width):
                codes, scales = hidden[a][lo // width]
                nc.tensor.matmul_mx(
                    out=dst[:, lo : lo + width],
                    lhsT=w2_codes[:, a, 2 * n * P : 2 * (n + 1) * P].bitcast(FP4X4),
                    lhsT_scale=out_scales[:, a, :].bitcast(U8)[:, n * P : (n + 1) * P],
                    rhs=codes.bitcast(FP8X4),
                    rhs_scale=scales,
                    start=opens and lo == 0,
                    stop=closes and lo + width == STEP,
                )

        def accumulate(c, hidden, stripes, steps=None):
            if steps is None:
                steps = [0, None, 1, 2, 3] if c == 0 else [None, 0, 1, 2, 3]
            for a in steps:
                for i, (n, dst) in enumerate(stripes):
                    opens = a == steps[0] and i == 0
                    if a is None:
                        shortcut_pass(n, c, dst, opens)
                    else:
                        band_passes(n, a, hidden, dst, opens, a == steps[-1] and i == len(stripes) - 1)

        def second_product(c, hidden):
            banks = [bank(k) for k in Y_BANKS[c]]
            ys = [banks[n // 2][:, n % 2 * STEP : (n % 2 + 1) * STEP] for n in range(LAST)]
            accumulate(c, hidden, [(0, ys[0]), (1, ys[1])])
            accumulate(c, hidden, [(2, ys[2])], THIRD_STEPS[c])
            return ys

        unit = STEP * PACK

        def gate(c):
            return GATES_AT[c - 1] * KIB

        def on_planes(c):
            return gate(c) + 2 * KIB - KIB // 4

        def on_weighted(c):
            return gate(c) + 2 * KIB + KIB // 4

        def on_last_act(c):
            return gate(c) - KIB

        def quantize_late(c, rounded, offsets):
            hidden = []
            for u in range(2):
                half = rounded[:, 2 * u * unit : 2 * (u + 1) * unit]
                groups = quantize_hidden(f"late{c}_{u}", half, 2 * STEP, offsets[u])
                hidden.extend([groups[0:1], groups[1:2]])
            return hidden

        def act_tile(c, a, place):
            return shared.tile([P, STEP, PACK], F32, name=f"act{c}_{a}", offset=place * KIB, align_bytes=64)

        def places(first, count):
            return slots[:, first // LANES : (first + count) // LANES]

        def weigh(c, n, y, offset=None):
            if offset is None:
                weighted = ring.tile([P, STEP], F32, name="weighted", align_bytes=64)
            else:
                weighted = shared.tile([P, STEP], F32, name=f"weighted{c}_{n}", offset=offset, align_bytes=64)
            nc.vector.tensor_tensor(weighted[:], y, weight[:, c * STEP : (c + 1) * STEP], MULT)
            return weighted

        def scatter_copy(c, n, weighted):
            nc.vector.tensor_copy(windows[n][:].indirect(places(c * STEP, STEP)), weighted[:])

        def scatter_weighted(n, first, count, sums):
            nc.vector.tensor_tensor(
                windows[n][:].indirect(places(first, count)), sums[:], weight[:, first : first + count], MULT
            )

        def act_pair(c, a, place):
            pair = shared.tile([P, 2, STEP, PACK], F32, name=f"act_pair{c}", offset=place * KIB, align_bytes=64)
            for u in range(2):
                activate(a + u, c, pair[:, u])
            return pair

        def last_planes(c):
            planes = shared.tile([P, 2, STEP, 2], BF16, name=f"planes{c}", offset=gate(c), align_bytes=64)
            hidden_on_scalar(LAST, c, planes)
            return planes

        def scatter_early(c, ys, count):
            weighed = [weigh(c, n, ys[n], gate(c + 1) + 2 * KIB if n == count - 2 else None) for n in range(count)]
            for n in range(count):
                scatter_copy(c, n, weighed[n])

        def last_stripe(c, hidden):
            y = bank(LAST_BANK)[:, 0:STEP]
            accumulate(c, hidden, [(LAST, y)])
            return y

        quantize_w1(0)
        turned = bank(LAST_BANK)
        for t in range(PACK):
            nc.tensor.transpose(turned[:, t : HALF : PACK], gain_rows[:, t : P * PACK : PACK], identity[:])
        windows.append(shared.tile([P, T2], F32, name="window2", offset=GAIN_ROWS_AT * KIB, align_bytes=64))
        nc.gpsimd.memset(windows[2][:].bitcast(I32), 0)
        windows.append(shared.tile([P, T2], F32, name="window_last", offset=LAST_WINDOW_AT * KIB, align_bytes=64))
        nc.gpsimd.memset(windows[LAST][:].bitcast(I32), 0)
        bank_gain = turned[:].rearrange("p (a u) -> p a u", u=4 * PACK)[:, :, 0:PACK]
        nc.scalar.copy(out=gain[:], in_=bank_gain[:, 0:BANDS, :])
        gather_codes(0)
        gather_codes(1)
        for a in range(1, BANDS):
            quantize_w1(a)

        rounded_first = shared.tile(
            [P, unit], BF16, name="h_rounded_first", offset=(SECOND_RAW_AT + 4) * KIB, align_bytes=64
        )
        rounded_middle = shared.tile(
            [P, 2 * unit], BF16, name="h_rounded_middle", offset=LAST_RAW_AT * KIB, align_bytes=64
        )
        rounded_last = shared.tile([P, unit], BF16, name="h_rounded_last", offset=ROUNDED_AT * KIB, align_bytes=64)
        first_acts = []
        for a in range(BANDS):
            first_acts.append(act_tile(0, a, FIRST_ACTS_AT[a]))
            activate(a, 0, first_acts[a])
            if a == 0:
                apply_gain(nc.vector, bank_gain[:, a, :], first_acts[a][:], rounded_first[:])
                hidden = [quantize_hidden(0, rounded_first[:], STEP)]
                act_ahead = act_tile(1, 0, SECOND_ACTS_AT[0])
                activate(0, 1, act_ahead)
            elif a < LAST:
                dst = rounded_middle[:, (a - 1) * unit : a * unit]
                apply_gain(nc.vector, bank_gain[:, a, :], first_acts[a][:], dst)
        halves = [rounded_last[:, lo * PACK : (lo + GROUP) * PACK] for lo in range(0, STEP, GROUP)]
        apply_gain(nc.vector, bank_gain[:, LAST, :], first_acts[LAST][:, 0:GROUP, :], halves[0])
        groups = quantize_hidden("middle", rounded_middle[:], 2 * STEP)
        hidden.extend([groups[0:1], groups[1:2]])
        apply_gain(nc.vector, bank_gain[:, LAST, :], first_acts[LAST][:, GROUP:STEP, :], halves[1])
        hidden.append([quantize_hidden(f"last{u}", halves[u], GROUP)[0] for u in range(2)])
        rounded_ahead = shared.tile(
            [P, unit], BF16, name="h_rounded_ahead", offset=(LAST_W1_AT + 2) * KIB, align_bytes=64
        )
        apply_gain(nc.gpsimd, gain[:, 0, :], act_ahead[:], rounded_ahead[:])
        ahead = quantize_hidden("ahead", rounded_ahead[:], STEP, FIRST_ACTS_AT[LAST] * KIB)

        pair = act_pair(1, 1, SECOND_ACTS_AT[1])
        ys = second_product(0, hidden)
        rounded = shared.tile([P, 3 * unit], BF16, name="rounded1", offset=ROUNDED_AT * KIB, align_bytes=64)
        apply_gain(nc.vector, bank_gain[:, 1, :], pair[:, 0, 0:GROUP, :], rounded[:, 0 : unit // 2])
        scatter_early(0, ys, 2)
        apply_gain(nc.gpsimd, gain[:, 1, :], pair[:, 0, GROUP:STEP, :], rounded[:, unit // 2 : unit])
        apply_gain(nc.gpsimd, gain[:, 2, :], pair[:, 1], rounded[:, unit : 2 * unit])
        planes = last_planes(1)
        sums = keep.tile([P, STEP], F32, name="sums_early0", align_bytes=64)
        nc.scalar.copy(out=sums[:], in_=ys[2])
        scatter_weighted(2, 0 * STEP, STEP, sums)
        pair = shared.tile([P, 2, STEP, PACK], F32, name="act_pair2", offset=THIRD_ACTS_AT * KIB, align_bytes=64)
        activate(0, 2, pair[:, 0])
        interleave(planes, rounded[:, 2 * unit : 3 * unit])
        activate(1, 2, pair[:, 1])
        y_last = last_stripe(0, hidden)
        weighted = weigh(0, LAST, y_last, gate(1))
        groups = quantize_hidden("second_pair", rounded[:, 0 : 2 * unit], 2 * STEP, on_planes(1))
        last = quantize_hidden("second_last", rounded[:, 2 * unit : 3 * unit], STEP, on_weighted(1))
        hidden = [ahead, groups[0:1], groups[1:2], last]
        scatter_copy(0, LAST, weighted)

        ys = second_product(1, hidden)
        scatter_early(1, ys, LAST)
        rounded = shared.tile([P, BANDS * unit], BF16, name="rounded2", offset=ROUNDED_AT * KIB, align_bytes=64)
        apply_gain_to_pair(0, pair[:], rounded[:, 0 : 2 * unit])
        act = act_tile(2, 2, THIRD_ACTS_AT + 8)
        activate(2, 2, act)
        apply_gain(nc.gpsimd, gain[:, 2, :], act[:], rounded[:, 2 * unit : 3 * unit])
        planes = last_planes(2)
        last_pair = shared.tile([P, 2, STEP, PACK], F32, name="act_pair3", offset=LAST_PAIR_AT * KIB, align_bytes=64)
        activate(0, 3, last_pair[:, 0])
        interleave(planes, rounded[:, 3 * unit : 4 * unit])
        activate(1, 3, last_pair[:, 1])
        y_last = last_stripe(1, hidden)
        weighted = weigh(1, LAST, y_last, gate(2) - KIB // 2)
        hidden = quantize_late(2, rounded, [on_last_act(2), on_weighted(2)])
        scatter_copy(1, LAST, weighted)

        third_planes = keep.tile([P, 2, STEP, 2], BF16, name="third_planes", align_bytes=64)
        hidden_on_scalar(2, 3, third_planes)
        planes = last_planes(3)
        ys = second_product(2, hidden)
        scatter_early(2, ys, 2)
        rounded = shared.tile([P, BANDS * unit], BF16, name="rounded3", offset=ROUNDED_AT * KIB, align_bytes=64)
        apply_gain_to_pair(0, last_pair[:], rounded[:, 0 : 2 * unit])
        interleave(third_planes, rounded[:, 2 * unit : 3 * unit])
        interleave(planes, rounded[:, 3 * unit : 4 * unit])

        c = CHUNKS - 1
        held = STRIPES - 2
        later_steps = [None, 2, 3, 0, 1]
        joint = bank(X_BANKS[3][LAST][1])
        accumulate(c - 1, hidden, [(LAST, joint[:, 0:STEP])])
        hidden = quantize_late(c, rounded, [on_planes(c), on_last_act(c)])
        sums = shared.tile([P, STEP], F32, name="sums_held", offset=gate(c) - KIB // 2, align_bytes=64)
        nc.scalar.copy(out=sums[:], in_=ys[held])
        scatter_weighted(held, (c - 1) * STEP, STEP, sums)
        for n in range(STRIPES):
            if n < LAST:
                y = bank(Y_BANKS[c][n])
                accumulate(c, hidden, [(n, y[:, 0:STEP])], later_steps if n > 0 else None)
                sums = keep.tile([P, STEP], F32, name=f"sums{n}", align_bytes=64)
                nc.scalar.copy(out=sums[:], in_=y[:, 0:STEP])
                scatter_weighted(n, c * STEP, STEP, sums)
            else:
                accumulate(c, hidden, [(n, joint[:, STEP:HALF])], later_steps)
                sums = keep.tile([P, HALF], F32, name=f"sums{n}", align_bytes=64)
                nc.scalar.copy(out=sums[:], in_=joint[:])
                scatter_weighted(n, (c - 1) * STEP, HALF, sums)
            nc.sync.dma_start(out=out[n * P : (n + 1) * P, :], in_=windows[n][:])
